import numpy as np
import ml_dtypes


def mxq(x, axis, fmt="e4m3"):
    dtype, down = {"e4m3": (ml_dtypes.float8_e4m3fn, 7), "e5m2": (ml_dtypes.float8_e5m2, 14)}[fmt]
    v = np.moveaxis(np.asarray(x, np.float32).astype(ml_dtypes.bfloat16).astype(np.float64), axis, -1)
    blocks = v.reshape(v.shape[:-1] + (-1, 32))
    amax = np.abs(blocks).max(-1, keepdims=True)
    byte = np.maximum(np.where(amax > 0, np.frexp(amax)[1] - 1 + 127, 0) - down, 1)
    scale = np.exp2(byte - 127.0)
    codes = (blocks / scale).astype(np.float32).astype(dtype).astype(np.float64)
    return np.moveaxis((codes * scale).reshape(v.shape), -1, axis)


WIDE = False


def mx_kscale(k):
    if not WIDE:
        return np.ones(k)
    levels = np.array([10, -10, 5, -5, 0])
    if k % 512:
        return np.exp2(np.random.permutation(np.resize(levels, k // 32))).repeat(32)
    a = np.empty((k // 512, 16))
    for p in range(k // 512):
        a[p, :8] = np.random.permutation(np.resize(levels, 8))
        for g in range(8):
            far = levels[np.abs(levels - a[p, g]) >= 10]
            a[p, g + 8] = far[np.random.randint(len(far))]
    return np.exp2(a.ravel()).repeat(32)


def f64(x):
    return np.asarray(x).astype(np.float64)


def striped(idx):
    return np.tile(idx.reshape(-1, 16).T, (8, 1)).astype(np.uint16)


def unstriped(offs):
    return offs[:16].T.reshape(-1).astype(np.int64)


E2M1 = np.array([0.0, 0.5, 1.0, 1.5, 2.0, 3.0, 4.0, 6.0, -0.0, -0.5, -1.0, -1.5, -2.0, -3.0, -4.0, -6.0])


def pack_weight(w, fmt):
    k, n = w.shape
    w = f64(np.asarray(w, np.float32).astype(ml_dtypes.bfloat16)).reshape(k // 32, 32, n)
    amax = np.abs(w).max(1)
    if fmt == "e4m3":
        byte = np.frexp(amax)[1] - 1 + 127 - 7
    else:
        mant, ex = np.frexp(amax / 6.0)
        byte = np.where(mant > 0.5, ex, ex - 1) + 127
    byte = np.clip(np.where(amax > 0, byte, 1), 1, 254)
    scaled = (w * np.exp2(127.0 - byte)[:, None, :]).reshape(k, n).astype(np.float32)
    by_word = np.ascontiguousarray(scaled.reshape(k // 512, 128, 4, n).transpose(0, 1, 3, 2))
    if fmt == "e4m3":
        words = by_word.astype(ml_dtypes.float8_e4m3fn).view(np.uint8)
    else:
        c = by_word.astype(ml_dtypes.float4_e2m1fn).view(np.uint8) & 0xF
        words = (c[..., 0::2] | (c[..., 1::2] << 4)).reshape(k // 512, 128, 2 * n)
    return np.ascontiguousarray(words), np.ascontiguousarray(byte.astype(np.uint8).reshape(k // 512, 16, n))


def unpack_weight(words, scales, fmt):
    g, _, n = scales.shape
    words = np.ascontiguousarray(words).reshape(g, 128, n, -1)
    if fmt == "e4m3":
        vals = words.view(ml_dtypes.float8_e4m3fn).astype(np.float64)
    else:
        nib = np.empty((g, 128, n, 4), np.uint8)
        nib[..., 0::2] = words & 0xF
        nib[..., 1::2] = words >> 4
        vals = E2M1[nib]
    vals = vals * np.repeat(np.exp2(scales.astype(np.float64) - 127.0), 8, axis=1)[..., None]
    return vals.transpose(0, 1, 3, 2).reshape(g * 512, n)


def d_relu2(v):
    return 2.0 * np.maximum(v, 0.0)


K, T, E, C, H, N = 512, 640, 10, 128, 512, 1536


def by_expert(wq, xq):
    return np.concatenate([wq[e].T @ xq[:, e * C:(e + 1) * C] for e in range(E)], axis=1)


def setup_inputs():
    n = np.random.standard_normal
    v = mx_kscale(N)
    u = mx_kscale(H)
    first = np.random.permutation(np.repeat(np.arange(E), T // E))
    second = (first + 1 + np.random.permutation(np.repeat(np.arange(E - 1), -(-T // (E - 1)))[:T])) % E
    while np.bincount(second, minlength=E).max() != T // E:
        load = np.bincount(second, minlength=E); hi, lo = int(load.argmax()), int(load.argmin())
        t = np.flatnonzero((second == hi) & (first != lo))[0]; second[t] = lo
    slot_token = np.empty(E * C, np.int64); pos = np.empty((2, T), np.int64); fill = np.zeros(E, np.int64)
    place = np.stack([np.random.permutation(C) for _ in range(E)])
    for r, deal in enumerate((first, second)):
        for t in np.random.permutation(T):
            e = deal[t]; j = e * C + place[e, fill[e]]; fill[e] += 1; slot_token[j] = t; pos[r, t] = j
    g = np.random.uniform(0.2, 0.8, T)
    dy = pack_weight(n((N, T)) * v[:, None], "e4m3")
    w2t = [pack_weight(m, "e2m1") for m in n((E, N, H)) / np.sqrt(N) / v[None, :, None] * u]
    w1t = pack_weight(n((H, K)) / np.sqrt(H) / u[:, None], "e2m1")
    return {
        "dy_words": dy[0],
        "dy_scales": dy[1],
        "w2t_words": np.stack([m[0] for m in w2t]),
        "w2t_scales": np.stack([m[1] for m in w2t]),
        "w1t_words": w1t[0],
        "w1t_scales": w1t[1],
        "a": (n((H, T))).astype(np.float32),
        "gate": np.stack([np.tile(g, (128, 1)), np.tile(1.0 - g, (128, 1))]).astype(np.float32),
        "offs": striped(slot_token),
        "pos1": striped(pos[0]),
        "pos2": striped(pos[1]),
    }


def reference(dy_words, dy_scales, w2t_words, w2t_scales, w1t_words, w1t_scales, a, gate, offs, pos1, pos2):
    w2t = np.stack([unpack_weight(w2t_words[e], w2t_scales[e], "e2m1") for e in range(E)])
    w1t = unpack_weight(w1t_words, w1t_scales, "e2m1")
    idx = unstriped(offs)
    gq = unpack_weight(dy_words, dy_scales, "e4m3")[:, idx]
    y = by_expert(w2t, gq)
    dh = sum(f64(gate[r, :1]) * y[:, unstriped(p)] for r, p in enumerate((pos1, pos2)))
    return w1t.T @ mxq(dh * d_relu2(f64(a)), 0, "e4m3")

@@ -1,0 +1,248 @@
+from contextlib import ExitStack
+
+import concourse.mybir as mybir
+from concourse.masks import make_identity
+
+K, T, E, C, H, N = 512, 640, 10, 128, 512, 1536
+S = E * C
+P = 128
+PASSES = N // 512
+CHUNKS = H // P
+
+FLOPS = 2 * N * H * S + 2 * H * K * T
+
+F32 = mybir.dt.float32
+BF16 = mybir.dt.bfloat16
+I32 = mybir.dt.int32
+U32 = mybir.dt.uint32
+U16 = mybir.dt.uint16
+U8 = mybir.dt.uint8
+FP8X4 = mybir.dt.float8_e4m3fn_x4
+FP4X4 = mybir.dt.float4_e2m1fn_x4
+MULT = mybir.AluOpType.mult
+MAX = mybir.AluOpType.max
+COPY = mybir.ActivationFunctionType.Copy
+
+EXPERT_GROUPS_FIRST = [(0, 3), (3, 6), (6, 9), (9, 10)]
+EXPERT_GROUPS_SECOND = [(0, 4), (4, 8), (8, 10)]
+BYTE_PIECES = [(0, 448), (448, 896), (896, 1280)]
+TOKEN_GROUPS = [(0, 256), (256, 512), (512, 640)]
+SHIFT_ROWS = 112
+
+
+def tile_moe_sub_relu2_kernel(
+    tc, dy_words, dy_scales, w2t_words, w2t_scales, w1t_words, w1t_scales, a, gate, offs, pos1, pos2, out
+):
+    nc = tc.nc
+    with ExitStack() as ctx:
+        keep = ctx.enter_context(tc.tile_pool(name="keep", bufs=1))
+        psum = ctx.enter_context(tc.psum_pool(name="psum", bufs=1))
+
+        offs_t = keep.tile([P, S // 16], U16, name="offs_t")
+        pos_t = [keep.tile([P, T // 16], U16, name="pos%d_t" % r) for r in range(2)]
+        dyw = [keep.tile([P, T], I32, name="dyw%d" % s, align_bytes=64) for s in range(PASSES)]
+        dys = keep.tile([P, T], U8, name="dys", align_bytes=64)
+        gw = [keep.tile([P, S], I32, name="gw%d" % s, align_bytes=64) for s in range(PASSES)]
+        gs = [keep.tile([P, S], U8, name="gs%d" % s, align_bytes=64) for s in range(PASSES)]
+        w2 = [keep.tile([P, E * PASSES, 512], U8, name="w2h%d" % h, align_bytes=64) for h in range(2)]
+        w2s = keep.tile([P, E * PASSES, H], U8, name="w2s", align_bytes=64)
+        w1 = keep.tile([P, 2 * K], U8, name="w1", align_bytes=64)
+        w1s = keep.tile([P, K], U8, name="w1s", align_bytes=64)
+        gate_t = [keep.tile([P, T], F32, name="gate%d" % r) for r in range(2)]
+        a_t = keep.tile([P, 4, T], F32, name="a_t")
+        ident = keep.tile([P, P], F32, name="ident")
+        y = [keep.tile([P, S], F32, name="y%d" % c) for c in range(CHUNKS)]
+        picked = [[keep.tile([P, T], F32, name="picked%d_%d" % (r, c)) for c in range(CHUNKS)] for r in range(2)]
+        dh_t = keep.tile([P, T // P, 4, P], F32, name="dh_t")
+        da = keep.tile([P, T, 4], BF16, name="da", align_bytes=64)
+        da_codes = keep.tile([P, T], U32, name="da_codes", align_bytes=64)
+        da_scales = keep.tile([P, T], U8, name="da_scales", align_bytes=64)
+        result = keep.tile([P, CHUNKS, T], F32, name="result")
+
+        y_banks = [psum.tile([P, 512], F32, name="y_bank%d" % b) for b in range(2)]
+        sum_banks = [psum.tile([P, 512], F32, name="sum_bank%d" % b) for b in range(2)]
+        back_banks = [psum.tile([P, 512], F32, name="back_bank%d" % b) for b in range(2)]
+        out_banks = [psum.tile([P, 512], F32, name="out_bank%d" % b) for b in range(2)] + y_banks
+
+        nc.vector.memset(dys[:].bitcast(I32), 0)
+        nc.vector.memset(w2s[:].rearrange("p a b -> p (a b)").bitcast(I32), 0)
+        for s in (1, 2):
+            nc.vector.memset(gs[s][96:128, :].bitcast(I32), 0)
+        nc.vector.memset(w1s[:].bitcast(I32), 0)
+        make_identity(nc, ident[:])
+
+        dyw_src = dy_words.rearrange("s p t d -> s p (t d)")
+        w2_src = w2t_words.rearrange("e s p b -> p (e s) b")
+        w2s_src = w2t_scales.rearrange("e s (q r) n -> r q (e s) n", r=4)
+
+        def load_dys(engine, q):
+            engine.dma_start(out=dys[32 * q : 32 * q + 12, :].bitcast(I32), in_=dy_scales[:, 4 * q : 4 * q + 4, :].bitcast(I32))
+
+        def load_w2(h, e0, e1):
+            nc.sync.dma_start(
+                out=w2[h][:, PASSES * e0 : PASSES * e1, :].bitcast(I32),
+                in_=w2_src[:, PASSES * e0 : PASSES * e1, 512 * h : 512 * (h + 1)].bitcast(I32),
+            )
+
+        nc.sync.dma_start(offs_t[:], offs)
+        nc.sync.dma_start(out=dyw[0][:], in_=dyw_src[0].bitcast(I32))
+        load_dys(nc.scalar, 0)
+        load_dys(nc.scalar, 1)
+        load_dys(nc.sync, 2)
+        load_dys(nc.sync, 3)
+        nc.sync.dma_start(out=dyw[1][:], in_=dyw_src[1].bitcast(I32))
+        nc.sync.dma_start(out=dyw[2][:], in_=dyw_src[2].bitcast(I32))
+        for r in range(4):
+            nc.sync.dma_start(out=w2s[r:P:32, :, :].bitcast(I32), in_=w2s_src[r].bitcast(I32))
+        for e0, e1 in EXPERT_GROUPS_FIRST:
+            load_w2(0, e0, e1)
+        nc.sync.dma_start(pos_t[0][:], pos1)
+        nc.sync.dma_start(pos_t[1][:], pos2)
+        for r in range(2):
+            nc.sync.dma_start(out=gate_t[r][:], in_=gate[r])
+        for e0, e1 in EXPERT_GROUPS_SECOND:
+            load_w2(1, e0, e1)
+        nc.sync.dma_start(out=a_t[:], in_=a.rearrange("(p t) n -> p t n", t=4))
+        nc.sync.dma_start(out=w1[:].bitcast(I32), in_=w1t_words[0].bitcast(I32))
+        w1s_src = w1t_scales[0].rearrange("(q r) n -> r q n", r=4)
+        for r in range(4):
+            nc.sync.dma_start(out=w1s[r:P:32, :].bitcast(I32), in_=w1s_src[r].bitcast(I32))
+
+        def gather_words(s, e0, e1):
+            nc.vector.tensor_copy(
+                gw[s][:, C * e0 : C * e1].bitcast(U32),
+                dyw[s][:].bitcast(U32).indirect(offs_t[:, C * e0 // 16 : C * e1 // 16]),
+            )
+
+        def gather_bytes():
+            for j0, j1 in BYTE_PIECES:
+                nc.vector.tensor_copy(gs[0][:, j0:j1], dys[:].indirect(offs_t[:, j0 // 16 : j1 // 16]))
+            for s in (1, 2):
+                nc.scalar.dma_start(out=gs[s][0:SHIFT_ROWS, :].bitcast(I32), in_=gs[0][4 * s : 4 * s + SHIFT_ROWS, :].bitcast(I32))
+
+        def experts(h, e0, e1):
+            for cc in range(2):
+                c = 2 * h + cc
+                bank = y_banks[cc]
+                for e in range(e0, e1):
+                    for s in range(PASSES):
+                        nc.tensor.matmul_mx(
+                            out=bank[:, C * (e - e0) : C * (e - e0 + 1)],
+                            lhsT=w2[h][:, PASSES * e + s, 256 * cc : 256 * (cc + 1)].bitcast(FP4X4),
+                            lhsT_scale=w2s[:, PASSES * e + s, P * c : P * (c + 1)],
+                            rhs=gw[s][:, C * e : C * (e + 1)].bitcast(FP8X4),
+                            rhs_scale=gs[s][:, C * e : C * (e + 1)],
+                            start=(s == 0),
+                            stop=(s == PASSES - 1),
+                        )
+                nc.scalar.copy(out=y[c][:, C * e0 : C * e1], in_=bank[:, 0 : C * (e1 - e0)])
+
+        for g, (e0, e1) in enumerate(EXPERT_GROUPS_FIRST):
+            for s in range(PASSES):
+                gather_words(s, e0, e1)
+                if g == 0 and s == 0:
+                    gather_bytes()
+            experts(0, e0, e1)
+        for e0, e1 in EXPERT_GROUPS_SECOND:
+            experts(1, e0, e1)
+
+        def pick(c, t0, t1):
+            for r in range(2):
+                nc.vector.tensor_tensor(
+                    picked[r][c][:, t0:t1], y[c][:].indirect(pos_t[r][:, t0 // 16 : t1 // 16]), gate_t[r][:, t0:t1], MULT
+                )
+
+        def turn_and_add(h, g):
+            t0, t1 = TOKEN_GROUPS[g]
+            tiles = (t1 - t0) // P
+            bank = sum_banks[(len(TOKEN_GROUPS) * h + g) % 2]
+            for cc in range(2):
+                for jj in range(tiles):
+                    for r in range(2):
+                        nc.tensor.matmul(
+                            out=bank[:, 256 * jj + P * cc : 256 * jj + P * (cc + 1)],
+                            lhsT=picked[r][2 * h + cc][:, t0 + P * jj : t0 + P * (jj + 1)],
+                            rhs=ident[:],
+                            is_transpose=True,
+                            start=(r == 0),
+                            stop=(r == 1),
+                        )
+            nc.scalar.activation(
+                out=dh_t[:, t0 // P : t1 // P, :, 64 * h : 64 * (h + 1)],
+                in_=bank[:, 0 : 256 * tiles].rearrange("p (j m t) -> p j t m", j=tiles, t=4),
+                func=COPY,
+                scale=2.0,
+            )
+
+        def turn_back(j):
+            bank = back_banks[j % 2]
+            for t in range(4):
+                nc.tensor.transpose(bank[:, P * t : P * (t + 1)], dh_t[:, j, t, :], ident[:])
+
+        def make_da(j):
+            nc.vector.scalar_tensor_tensor(
+                out=da[:, P * j : P * (j + 1), :],
+                in0=a_t[:, :, P * j : P * (j + 1)].rearrange("p t n -> p n t"),
+                scalar=0.0,
+                in1=back_banks[j % 2][:].rearrange("p (t n) -> p n t", t=4),
+                op0=MAX,
+                op1=MULT,
+            )
+
+        def finish(g):
+            t0, t1 = TOKEN_GROUPS[g]
+            n = t1 - t0
+            nc.vector.quantize_mx(
+                out=da_codes[:, t0:t1].bitcast(FP8X4),
+                scales=da_scales[:, t0:t1],
+                in_=da[:, t0:t1, :].rearrange("p n t -> p (n t)"),
+            )
+            out_view = out.rearrange("(c p) n -> p c n", p=P)
+            for half in range(2):
+                bank = out_banks[(2 * g + half) % 4]
+                for cc in range(2):
+                    c = 2 * half + cc
+                    nc.tensor.matmul_mx(
+                        out=bank[:, n * cc : n * (cc + 1)],
+                        lhsT=w1[:, 256 * c : 256 * (c + 1)].bitcast(FP4X4),
+                        lhsT_scale=w1s[:, P * c : P * (c + 1)],
+                        rhs=da_codes[:, t0:t1].bitcast(FP8X4),
+                        rhs_scale=da_scales[:, t0:t1],
+                        start=True,
+                        stop=True,
+                    )
+                dst = result[:, 2 * half : 2 * half + 2, t0:t1]
+                src = bank[:, 0 : 2 * n].rearrange("p (c n) -> p c n", c=2)
+                if g == len(TOKEN_GROUPS) - 1 and half == 1:
+                    nc.vector.tensor_copy(out=dst, in_=src)
+                else:
+                    nc.scalar.copy(out=dst, in_=src)
+                nc.sync.dma_start(out=out_view[:, 2 * half : 2 * half + 2, t0:t1], in_=dst)
+
+        pick(0, 0, T)
+        pick(1, 0, T)
+        for g in range(len(TOKEN_GROUPS)):
+            turn_and_add(0, g)
+
+        def second_half(g):
+            t0, t1 = TOKEN_GROUPS[g]
+            pick(2, t0, t1)
+            pick(3, t0, t1)
+            turn_and_add(1, g)
+
+        second_half(0)
+        turn_back(0)
+        turn_back(1)
+        second_half(1)
+        make_da(0)
+        make_da(1)
+        finish(0)
+        turn_back(2)
+        turn_back(3)
+        second_half(2)
+        make_da(2)
+        turn_back(4)
+        make_da(3)
+        finish(1)
+        make_da(4)
+        finish(2)

@@ -40,16 +40,17 @@ def tile_moe_sub_relu2_kernel(
 
         offs_t = keep.tile([P, S // 16], U16, name="offs_t")
         pos_t = [keep.tile([P, T // 16], U16, name="pos%d_t" % r) for r in range(2)]
-        dyw = [keep.tile([P, T], I32, name="dyw%d" % s, align_bytes=64) for s in range(PASSES)]
+        dyw = keep.tile([P, PASSES, T], I32, name="dyw", align_bytes=64)
         dys = keep.tile([P, T], U8, name="dys", align_bytes=64)
         gw = [keep.tile([P, S], I32, name="gw%d" % s, align_bytes=64) for s in range(PASSES)]
         gs = [keep.tile([P, S], U8, name="gs%d" % s, align_bytes=64) for s in range(PASSES)]
         w2 = [keep.tile([P, E * PASSES, 512], U8, name="w2h%d" % h, align_bytes=64) for h in range(2)]
-        w2s = keep.tile([P, E * PASSES, H], U8, name="w2s", align_bytes=64)
+        w2s = [keep.tile([P, E * PASSES, 256], U8, name="w2s%d" % h, align_bytes=64) for h in range(2)]
         w1 = keep.tile([P, 2 * K], U8, name="w1", align_bytes=64)
         w1s = keep.tile([P, K], U8, name="w1s", align_bytes=64)
         gate_t = [keep.tile([P, T], F32, name="gate%d" % r) for r in range(2)]
         a_t = keep.tile([P, 4, T], F32, name="a_t")
+        ident_made = keep.tile([P, P], F32, name="ident_made")
         ident = keep.tile([P, P], F32, name="ident")
         y = [keep.tile([P, S], F32, name="y%d" % c) for c in range(CHUNKS)]
         picked = [[keep.tile([P, T], F32, name="picked%d_%d" % (r, c)) for c in range(CHUNKS)] for r in range(2)]
@@ -62,16 +63,18 @@ def tile_moe_sub_relu2_kernel(
         y_banks = [psum.tile([P, 512], F32, name="y_bank%d" % b) for b in range(2)]
         sum_banks = [psum.tile([P, 512], F32, name="sum_bank%d" % b) for b in range(2)]
         back_banks = [psum.tile([P, 512], F32, name="back_bank%d" % b) for b in range(2)]
-        out_banks = [psum.tile([P, 512], F32, name="out_bank%d" % b) for b in range(2)] + y_banks
+        spare_banks = [psum.tile([P, 512], F32, name="spare_bank%d" % b) for b in range(2)]
+        out_banks = spare_banks + y_banks
 
-        nc.vector.memset(dys[:].bitcast(I32), 0)
-        nc.vector.memset(w2s[:].rearrange("p a b -> p (a b)").bitcast(I32), 0)
+        w2s_words = [t[:].rearrange("p a b -> p (a b)").bitcast(I32) for t in w2s]
+        nc.gpsimd.memset(dys[:].bitcast(I32), 0)
+        nc.vector.memset(w2s_words[0], 0)
         for s in (1, 2):
             nc.vector.memset(gs[s][96:128, :].bitcast(I32), 0)
+        nc.vector.memset(w2s_words[1], 0)
         nc.vector.memset(w1s[:].bitcast(I32), 0)
-        make_identity(nc, ident[:])
 
-        dyw_src = dy_words.rearrange("s p t d -> s p (t d)")
+        dyw_src = dy_words.rearrange("s p t d -> p s (t d)")
         w2_src = w2t_words.rearrange("e s p b -> p (e s) b")
         w2s_src = w2t_scales.rearrange("e s (q r) n -> r q (e s) n", r=4)
 
@@ -84,34 +87,41 @@ def tile_moe_sub_relu2_kernel(
                 in_=w2_src[:, PASSES * e0 : PASSES * e1, 512 * h : 512 * (h + 1)].bitcast(I32),
             )
 
+        def load_w2s(h):
+            for r in range(4):
+                nc.sync.dma_start(out=w2s[h][r:P:32, :, :].bitcast(I32), in_=w2s_src[r][:, :, 256 * h : 256 * (h + 1)].bitcast(I32))
+
+        a_src = a.rearrange("(p t) n -> p t n", t=4)
+        w1s_src = w1t_scales[0].rearrange("(q r) n -> r q n", r=4)
+
         nc.sync.dma_start(offs_t[:], offs)
-        nc.sync.dma_start(out=dyw[0][:], in_=dyw_src[0].bitcast(I32))
         load_dys(nc.scalar, 0)
         load_dys(nc.scalar, 1)
         load_dys(nc.sync, 2)
         load_dys(nc.sync, 3)
-        nc.sync.dma_start(out=dyw[1][:], in_=dyw_src[1].bitcast(I32))
-        nc.sync.dma_start(out=dyw[2][:], in_=dyw_src[2].bitcast(I32))
-        for r in range(4):
-            nc.sync.dma_start(out=w2s[r:P:32, :, :].bitcast(I32), in_=w2s_src[r].bitcast(I32))
+        nc.sync.dma_start(out=dyw[:], in_=dyw_src.bitcast(I32))
+        load_w2s(0)
+        make_identity(nc, ident_made[:])
+        nc.scalar.copy(out=ident[:], in_=ident_made[:])
         for e0, e1 in EXPERT_GROUPS_FIRST:
             load_w2(0, e0, e1)
         nc.sync.dma_start(pos_t[0][:], pos1)
+        nc.sync.dma_start(out=gate_t[0][:], in_=gate[0])
+        load_w2s(1)
         nc.sync.dma_start(pos_t[1][:], pos2)
-        for r in range(2):
-            nc.sync.dma_start(out=gate_t[r][:], in_=gate[r])
+        nc.sync.dma_start(out=gate_t[1][:], in_=gate[1])
         for e0, e1 in EXPERT_GROUPS_SECOND:
             load_w2(1, e0, e1)
-        nc.sync.dma_start(out=a_t[:], in_=a.rearrange("(p t) n -> p t n", t=4))
+        nc.sync.dma_start(out=a_t[:, :, 0:256], in_=a_src[:, :, 0:256])
         nc.sync.dma_start(out=w1[:].bitcast(I32), in_=w1t_words[0].bitcast(I32))
-        w1s_src = w1t_scales[0].rearrange("(q r) n -> r q n", r=4)
         for r in range(4):
             nc.sync.dma_start(out=w1s[r:P:32, :].bitcast(I32), in_=w1s_src[r].bitcast(I32))
+        nc.sync.dma_start(out=a_t[:, :, 256:T], in_=a_src[:, :, 256:T])
 
         def gather_words(s, e0, e1):
             nc.vector.tensor_copy(
                 gw[s][:, C * e0 : C * e1].bitcast(U32),
-                dyw[s][:].bitcast(U32).indirect(offs_t[:, C * e0 // 16 : C * e1 // 16]),
+                dyw[:, s, :].bitcast(U32).indirect(offs_t[:, C * e0 // 16 : C * e1 // 16]),
             )
 
         def gather_bytes():
@@ -120,16 +130,16 @@ def tile_moe_sub_relu2_kernel(
             for s in (1, 2):
                 nc.scalar.dma_start(out=gs[s][0:SHIFT_ROWS, :].bitcast(I32), in_=gs[0][4 * s : 4 * s + SHIFT_ROWS, :].bitcast(I32))
 
-        def experts(h, e0, e1):
+        def experts(h, e0, e1, banks):
             for cc in range(2):
                 c = 2 * h + cc
-                bank = y_banks[cc]
+                bank = banks[cc]
                 for e in range(e0, e1):
                     for s in range(PASSES):
                         nc.tensor.matmul_mx(
                             out=bank[:, C * (e - e0) : C * (e - e0 + 1)],
                             lhsT=w2[h][:, PASSES * e + s, 256 * cc : 256 * (cc + 1)].bitcast(FP4X4),
-                            lhsT_scale=w2s[:, PASSES * e + s, P * c : P * (c + 1)],
+                            lhsT_scale=w2s[h][:, PASSES * e + s, P * cc : P * (cc + 1)],
                             rhs=gw[s][:, C * e : C * (e + 1)].bitcast(FP8X4),
                             rhs_scale=gs[s][:, C * e : C * (e + 1)],
                             start=(s == 0),
@@ -137,14 +147,13 @@ def tile_moe_sub_relu2_kernel(
                         )
                 nc.scalar.copy(out=y[c][:, C * e0 : C * e1], in_=bank[:, 0 : C * (e1 - e0)])
 
+        gather_bytes()
         for g, (e0, e1) in enumerate(EXPERT_GROUPS_FIRST):
             for s in range(PASSES):
                 gather_words(s, e0, e1)
-                if g == 0 and s == 0:
-                    gather_bytes()
-            experts(0, e0, e1)
+            experts(0, e0, e1, y_banks if g % 2 else spare_banks)
         for e0, e1 in EXPERT_GROUPS_SECOND:
-            experts(1, e0, e1)
+            experts(1, e0, e1, y_banks)
 
         def pick(c, t0, t1):
             for r in range(2):
@@ -155,7 +164,7 @@ def tile_moe_sub_relu2_kernel(
         def turn_and_add(h, g):
             t0, t1 = TOKEN_GROUPS[g]
             tiles = (t1 - t0) // P
-            bank = sum_banks[(len(TOKEN_GROUPS) * h + g) % 2]
+            bank = (y_banks, sum_banks)[h][g % 2]
             for cc in range(2):
                 for jj in range(tiles):
                     for r in range(2):

@@ -20,14 +20,10 @@ U8 = mybir.dt.uint8
 FP8X4 = mybir.dt.float8_e4m3fn_x4
 FP4X4 = mybir.dt.float4_e2m1fn_x4
 MULT = mybir.AluOpType.mult
-MAX = mybir.AluOpType.max
-COPY = mybir.ActivationFunctionType.Copy
+RELU = mybir.ActivationFunctionType.Relu
 
-EXPERT_GROUPS_FIRST = [(0, 3), (3, 6), (6, 9), (9, 10)]
-EXPERT_GROUPS_SECOND = [(0, 4), (4, 8), (8, 10)]
-BYTE_PIECES = [(0, 448), (448, 896), (896, 1280)]
+EXPERT_GROUPS = [(0, 3), (3, 6), (6, 9), (9, 10)]
 TOKEN_GROUPS = [(0, 256), (256, 512), (512, 640)]
-SHIFT_ROWS = 112
 
 
 def tile_moe_sub_relu2_kernel(
@@ -40,16 +36,17 @@ def tile_moe_sub_relu2_kernel(
 
         offs_t = keep.tile([P, S // 16], U16, name="offs_t")
         pos_t = [keep.tile([P, T // 16], U16, name="pos%d_t" % r) for r in range(2)]
-        dyw = keep.tile([P, PASSES, T], I32, name="dyw", align_bytes=64)
-        dys = keep.tile([P, T], U8, name="dys", align_bytes=64)
+        dyw = [keep.tile([P, T], I32, name="dyw%d" % s, align_bytes=64) for s in range(PASSES)]
+        dys = keep.tile([P, PASSES, T], U8, name="dys", align_bytes=64)
         gw = [keep.tile([P, S], I32, name="gw%d" % s, align_bytes=64) for s in range(PASSES)]
         gs = [keep.tile([P, S], U8, name="gs%d" % s, align_bytes=64) for s in range(PASSES)]
-        w2 = [keep.tile([P, E * PASSES, 512], U8, name="w2h%d" % h, align_bytes=64) for h in range(2)]
-        w2s = [keep.tile([P, E * PASSES, 256], U8, name="w2s%d" % h, align_bytes=64) for h in range(2)]
+        w2 = keep.tile([P, E * PASSES, 2 * H], U8, name="w2", align_bytes=64)
+        w2s = keep.tile([P, E * PASSES, H], U8, name="w2s", align_bytes=64)
         w1 = keep.tile([P, 2 * K], U8, name="w1", align_bytes=64)
         w1s = keep.tile([P, K], U8, name="w1s", align_bytes=64)
         gate_t = [keep.tile([P, T], F32, name="gate%d" % r) for r in range(2)]
         a_t = keep.tile([P, 4, T], F32, name="a_t")
+        slope = keep.tile([P, T, 4], F32, name="slope")
         ident_made = keep.tile([P, P], F32, name="ident_made")
         ident = keep.tile([P, P], F32, name="ident")
         y = [keep.tile([P, S], F32, name="y%d" % c) for c in range(CHUNKS)]
@@ -60,128 +57,108 @@ def tile_moe_sub_relu2_kernel(
         da_scales = keep.tile([P, T], U8, name="da_scales", align_bytes=64)
         result = keep.tile([P, CHUNKS, T], F32, name="result")
 
-        y_banks = [psum.tile([P, 512], F32, name="y_bank%d" % b) for b in range(2)]
+        mx_banks = [psum.tile([P, 512], F32, name="mx_bank%d" % b) for b in range(4)]
         sum_banks = [psum.tile([P, 512], F32, name="sum_bank%d" % b) for b in range(2)]
         back_banks = [psum.tile([P, 512], F32, name="back_bank%d" % b) for b in range(2)]
-        spare_banks = [psum.tile([P, 512], F32, name="spare_bank%d" % b) for b in range(2)]
-        out_banks = spare_banks + y_banks
 
-        w2s_words = [t[:].rearrange("p a b -> p (a b)").bitcast(I32) for t in w2s]
-        nc.gpsimd.memset(dys[:].bitcast(I32), 0)
-        nc.vector.memset(w2s_words[0], 0)
-        for s in (1, 2):
-            nc.vector.memset(gs[s][96:128, :].bitcast(I32), 0)
-        nc.vector.memset(w2s_words[1], 0)
+        nc.vector.memset(dys[:].rearrange("p a b -> p (a b)").bitcast(I32), 0)
+        nc.vector.memset(w2s[:].rearrange("p a b -> p (a b)").bitcast(I32), 0)
         nc.vector.memset(w1s[:].bitcast(I32), 0)
+        make_identity(nc, ident_made[:])
+        nc.scalar.copy(out=ident[:], in_=ident_made[:])
 
-        dyw_src = dy_words.rearrange("s p t d -> p s (t d)")
+        dyw_src = dy_words.rearrange("s p t d -> s p (t d)")
+        dys_src = dy_scales.rearrange("s (q r) t -> r q s t", r=4)
         w2_src = w2t_words.rearrange("e s p b -> p (e s) b")
         w2s_src = w2t_scales.rearrange("e s (q r) n -> r q (e s) n", r=4)
-
-        def load_dys(engine, q):
-            engine.dma_start(out=dys[32 * q : 32 * q + 12, :].bitcast(I32), in_=dy_scales[:, 4 * q : 4 * q + 4, :].bitcast(I32))
-
-        def load_w2(h, e0, e1):
-            nc.sync.dma_start(
-                out=w2[h][:, PASSES * e0 : PASSES * e1, :].bitcast(I32),
-                in_=w2_src[:, PASSES * e0 : PASSES * e1, 512 * h : 512 * (h + 1)].bitcast(I32),
-            )
-
-        def load_w2s(h):
-            for r in range(4):
-                nc.sync.dma_start(out=w2s[h][r:P:32, :, :].bitcast(I32), in_=w2s_src[r][:, :, 256 * h : 256 * (h + 1)].bitcast(I32))
-
         a_src = a.rearrange("(p t) n -> p t n", t=4)
         w1s_src = w1t_scales[0].rearrange("(q r) n -> r q n", r=4)
 
+        def load_w2(g):
+            e0, e1 = EXPERT_GROUPS[g]
+            nc.sync.dma_start(
+                out=w2[:, PASSES * e0 : PASSES * e1, :].bitcast(I32),
+                in_=w2_src[:, PASSES * e0 : PASSES * e1, :].bitcast(I32),
+            )
+
         nc.sync.dma_start(offs_t[:], offs)
-        load_dys(nc.scalar, 0)
-        load_dys(nc.scalar, 1)
-        load_dys(nc.sync, 2)
-        load_dys(nc.sync, 3)
-        nc.sync.dma_start(out=dyw[:], in_=dyw_src.bitcast(I32))
-        load_w2s(0)
-        make_identity(nc, ident_made[:])
-        nc.scalar.copy(out=ident[:], in_=ident_made[:])
-        for e0, e1 in EXPERT_GROUPS_FIRST:
-            load_w2(0, e0, e1)
+        for s in range(PASSES):
+            nc.sync.dma_start(out=dyw[s][:], in_=dyw_src[s].bitcast(I32))
+        for r in range(4):
+            nc.scalar.dma_start(out=dys[r:P:32, :, :].bitcast(I32), in_=dys_src[r].bitcast(I32))
+        for r in range(4):
+            nc.sync.dma_start(out=w2s[r:P:32, :, :].bitcast(I32), in_=w2s_src[r].bitcast(I32))
+        load_w2(0)
+        load_w2(1)
+        load_w2(2)
         nc.sync.dma_start(pos_t[0][:], pos1)
         nc.sync.dma_start(out=gate_t[0][:], in_=gate[0])
-        load_w2s(1)
+        load_w2(3)
         nc.sync.dma_start(pos_t[1][:], pos2)
         nc.sync.dma_start(out=gate_t[1][:], in_=gate[1])
-        for e0, e1 in EXPERT_GROUPS_SECOND:
-            load_w2(1, e0, e1)
         nc.sync.dma_start(out=a_t[:, :, 0:256], in_=a_src[:, :, 0:256])
         nc.sync.dma_start(out=w1[:].bitcast(I32), in_=w1t_words[0].bitcast(I32))
         for r in range(4):
             nc.sync.dma_start(out=w1s[r:P:32, :].bitcast(I32), in_=w1s_src[r].bitcast(I32))
         nc.sync.dma_start(out=a_t[:, :, 256:T], in_=a_src[:, :, 256:T])
 
-        def gather_words(s, e0, e1):
-            nc.vector.tensor_copy(
-                gw[s][:, C * e0 : C * e1].bitcast(U32),
-                dyw[:, s, :].bitcast(U32).indirect(offs_t[:, C * e0 // 16 : C * e1 // 16]),
-            )
-
-        def gather_bytes():
-            for j0, j1 in BYTE_PIECES:
-                nc.vector.tensor_copy(gs[0][:, j0:j1], dys[:].indirect(offs_t[:, j0 // 16 : j1 // 16]))
-            for s in (1, 2):
-                nc.scalar.dma_start(out=gs[s][0:SHIFT_ROWS, :].bitcast(I32), in_=gs[0][4 * s : 4 * s + SHIFT_ROWS, :].bitcast(I32))
-
-        def experts(h, e0, e1, banks):
-            for cc in range(2):
-                c = 2 * h + cc
-                bank = banks[cc]
-                for e in range(e0, e1):
-                    for s in range(PASSES):
-                        nc.tensor.matmul_mx(
-                            out=bank[:, C * (e - e0) : C * (e - e0 + 1)],
-                            lhsT=w2[h][:, PASSES * e + s, 256 * cc : 256 * (cc + 1)].bitcast(FP4X4),
-                            lhsT_scale=w2s[h][:, PASSES * e + s, P * cc : P * (cc + 1)],
-                            rhs=gw[s][:, C * e : C * (e + 1)].bitcast(FP8X4),
-                            rhs_scale=gs[s][:, C * e : C * (e + 1)],
-                            start=(s == 0),
-                            stop=(s == PASSES - 1),
-                        )
-                nc.scalar.copy(out=y[c][:, C * e0 : C * e1], in_=bank[:, 0 : C * (e1 - e0)])
-
-        gather_bytes()
-        for g, (e0, e1) in enumerate(EXPERT_GROUPS_FIRST):
+        def gather_slots(e0, e1):
+            picks = offs_t[:, C * e0 // 16 : C * e1 // 16]
             for s in range(PASSES):
-                gather_words(s, e0, e1)
-            experts(0, e0, e1, y_banks if g % 2 else spare_banks)
-        for e0, e1 in EXPERT_GROUPS_SECOND:
-            experts(1, e0, e1, y_banks)
+                nc.vector.tensor_copy(gw[s][:, C * e0 : C * e1].bitcast(U32), dyw[s][:].bitcast(U32).indirect(picks))
+            for s in range(PASSES):
+                nc.vector.tensor_copy(gs[s][:, C * e0 : C * e1], dys[:, s, :].indirect(picks))
 
-        def pick(c, t0, t1):
-            for r in range(2):
-                nc.vector.tensor_tensor(
-                    picked[r][c][:, t0:t1], y[c][:].indirect(pos_t[r][:, t0 // 16 : t1 // 16]), gate_t[r][:, t0:t1], MULT
-                )
+        def experts(c, e0, e1, bank):
+            for e in range(e0, e1):
+                for s in range(PASSES):
+                    nc.tensor.matmul_mx(
+                        out=bank[:, C * (e - e0) : C * (e - e0 + 1)],
+                        lhsT=w2[:, PASSES * e + s, 2 * P * c : 2 * P * (c + 1)].bitcast(FP4X4),
+                        lhsT_scale=w2s[:, PASSES * e + s, P * c : P * (c + 1)],
+                        rhs=gw[s][:, C * e : C * (e + 1)].bitcast(FP8X4),
+                        rhs_scale=gs[s][:, C * e : C * (e + 1)],
+                        start=(s == 0),
+                        stop=(s == PASSES - 1),
+                    )
+            nc.scalar.copy(out=y[c][:, C * e0 : C * e1], in_=bank[:, 0 : C * (e1 - e0)])
 
-        def turn_and_add(h, g):
-            t0, t1 = TOKEN_GROUPS[g]
-            tiles = (t1 - t0) // P
-            bank = (y_banks, sum_banks)[h][g % 2]
-            for cc in range(2):
-                for jj in range(tiles):
-                    for r in range(2):
-                        nc.tensor.matmul(
-                            out=bank[:, 256 * jj + P * cc : 256 * jj + P * (cc + 1)],
-                            lhsT=picked[r][2 * h + cc][:, t0 + P * jj : t0 + P * (jj + 1)],
-                            rhs=ident[:],
-                            is_transpose=True,
-                            start=(r == 0),
-                            stop=(r == 1),
-                        )
+        for g, (e0, e1) in enumerate(EXPERT_GROUPS):
+            gather_slots(e0, e1)
+            for c in range(CHUNKS if g < 2 else 2):
+                experts(c, e0, e1, mx_banks[c])
+        for c in (2, 3):
+            experts(c, EXPERT_GROUPS[2][0], E, mx_banks[c - 2])
+
+        def make_slope(j):
             nc.scalar.activation(
-                out=dh_t[:, t0 // P : t1 // P, :, 64 * h : 64 * (h + 1)],
-                in_=bank[:, 0 : 256 * tiles].rearrange("p (j m t) -> p j t m", j=tiles, t=4),
-                func=COPY,
+                out=slope[:, P * j : P * (j + 1), :],
+                in_=a_t[:, :, P * j : P * (j + 1)].rearrange("p t n -> p n t"),
+                func=RELU,
                 scale=2.0,
             )
+
+        def pick(g):
+            t0, t1 = TOKEN_GROUPS[g]
+            for c in range(CHUNKS):
+                for r in range(2):
+                    nc.vector.tensor_tensor(
+                        picked[r][c][:, t0:t1], y[c][:].indirect(pos_t[r][:, t0 // 16 : t1 // 16]), gate_t[r][:, t0:t1], MULT
+                    )
+
+        def turn_and_add(j):
+            bank = sum_banks[j % 2]
+            for c in range(CHUNKS):
+                for r in range(2):
+                    nc.tensor.matmul(
+                        out=bank[:, P * c : P * (c + 1)],
+                        lhsT=picked[r][c][:, P * j : P * (j + 1)],
+                        rhs=ident[:],
+                        is_transpose=True,
+                        start=(r == 0),
+                        stop=(r == 1),
+                    )
+            nc.scalar.copy(out=dh_t[:, j, :, :], in_=bank[:].rearrange("p (m t) -> p t m", t=4))
 
         def turn_back(j):
             bank = back_banks[j % 2]
@@ -189,13 +166,11 @@ def tile_moe_sub_relu2_kernel(
                 nc.tensor.transpose(bank[:, P * t : P * (t + 1)], dh_t[:, j, t, :], ident[:])
 
         def make_da(j):
-            nc.vector.scalar_tensor_tensor(
-                out=da[:, P * j : P * (j + 1), :],
-                in0=a_t[:, :, P * j : P * (j + 1)].rearrange("p t n -> p n t"),
-                scalar=0.0,
-                in1=back_banks[j % 2][:].rearrange("p (t n) -> p n t", t=4),
-                op0=MAX,
-                op1=MULT,
+            nc.vector.tensor_tensor(
+                da[:, P * j : P * (j + 1), :],
+                back_banks[j % 2][:].rearrange("p (t n) -> p n t", t=4),
+                slope[:, P * j : P * (j + 1), :],
+                MULT,
             )
 
         def finish(g):
@@ -208,7 +183,7 @@ def tile_moe_sub_relu2_kernel(
             )
             out_view = out.rearrange("(c p) n -> p c n", p=P)
             for half in range(2):
-                bank = out_banks[(2 * g + half) % 4]
+                bank = mx_banks[(2 * g + half + 2) % 4]
                 for cc in range(2):
                     c = 2 * half + cc
                     nc.tensor.matmul_mx(
@@ -228,27 +203,26 @@ def tile_moe_sub_relu2_kernel(
                     nc.scalar.copy(out=dst, in_=src)
                 nc.sync.dma_start(out=out_view[:, 2 * half : 2 * half + 2, t0:t1], in_=dst)
 
-        pick(0, 0, T)
-        pick(1, 0, T)
-        for g in range(len(TOKEN_GROUPS)):
-            turn_and_add(0, g)
-
-        def second_half(g):
-            t0, t1 = TOKEN_GROUPS[g]
-            pick(2, t0, t1)
-            pick(3, t0, t1)
-            turn_and_add(1, g)
-
-        second_half(0)
+        pick(0)
+        turn_and_add(0)
+        turn_and_add(1)
         turn_back(0)
         turn_back(1)
-        second_half(1)
+        make_slope(0)
+        make_slope(1)
+        pick(1)
+        turn_and_add(2)
+        turn_and_add(3)
         make_da(0)
         make_da(1)
         finish(0)
         turn_back(2)
         turn_back(3)
-        second_half(2)
+        make_slope(2)
+        make_slope(3)
+        make_slope(4)
+        pick(2)
+        turn_and_add(4)
         make_da(2)
         turn_back(4)
         make_da(3)

@@ -8,6 +8,7 @@ S = E * C
 P = 128
 PASSES = N // 512
 CHUNKS = H // P
+BLOCKS = T // P
 
 FLOPS = 2 * N * H * S + 2 * H * K * T
 
@@ -20,10 +21,17 @@ U8 = mybir.dt.uint8
 FP8X4 = mybir.dt.float8_e4m3fn_x4
 FP4X4 = mybir.dt.float4_e2m1fn_x4
 MULT = mybir.AluOpType.mult
+ADD = mybir.AluOpType.add
 RELU = mybir.ActivationFunctionType.Relu
+COPY = mybir.ActivationFunctionType.Copy
 
-EXPERT_GROUPS = [(0, 3), (3, 6), (6, 9), (9, 10)]
-TOKEN_GROUPS = [(0, 256), (256, 512), (512, 640)]
+BYTE_WINDOW = 1792
+SHIFT_ROWS = 112
+GATHER_GROUPS = [(0, 3), (3, 6), (6, 9), (9, 10)]
+FIRST_LOADS = [(0, 2, 0, 4), (2, 5, 0, 2), (5, 8, 0, 2), (8, 10, 0, 2)]
+SECOND_LOADS = [(2, 6, 2, 4), (6, 10, 2, 4)]
+SCALE_RUNS = [(0, 10)]
+OUT_GROUPS = [(0, 256), (256, 512), (512, 640)]
 
 
 def tile_moe_sub_relu2_kernel(
@@ -36,99 +44,112 @@ def tile_moe_sub_relu2_kernel(
 
         offs_t = keep.tile([P, S // 16], U16, name="offs_t")
         pos_t = [keep.tile([P, T // 16], U16, name="pos%d_t" % r) for r in range(2)]
-        dyw = [keep.tile([P, T], I32, name="dyw%d" % s, align_bytes=64) for s in range(PASSES)]
-        dys = keep.tile([P, PASSES, T], U8, name="dys", align_bytes=64)
+        dyw = keep.tile([P, PASSES, T], I32, name="dyw", align_bytes=64)
+        dys = keep.tile([P, BYTE_WINDOW], U8, name="dys", align_bytes=64)
         gw = [keep.tile([P, S], I32, name="gw%d" % s, align_bytes=64) for s in range(PASSES)]
         gs = [keep.tile([P, S], U8, name="gs%d" % s, align_bytes=64) for s in range(PASSES)]
-        w2 = keep.tile([P, E * PASSES, 2 * H], U8, name="w2", align_bytes=64)
-        w2s = keep.tile([P, E * PASSES, H], U8, name="w2s", align_bytes=64)
+        w2s = [keep.tile([P, (e1 - e0) * PASSES, H], U8, name="w2s%d" % e0, align_bytes=64) for e0, e1 in SCALE_RUNS]
         w1 = keep.tile([P, 2 * K], U8, name="w1", align_bytes=64)
         w1s = keep.tile([P, K], U8, name="w1s", align_bytes=64)
-        gate_t = [keep.tile([P, T], F32, name="gate%d" % r) for r in range(2)]
+        gate_rows = keep.tile([P, P], F32, name="gate_rows")
+        gate_cols = keep.tile([P, 2 * BLOCKS], F32, name="gate_cols")
         a_t = keep.tile([P, 4, T], F32, name="a_t")
         slope = keep.tile([P, T, 4], F32, name="slope")
         ident_made = keep.tile([P, P], F32, name="ident_made")
         ident = keep.tile([P, P], F32, name="ident")
         y = [keep.tile([P, S], F32, name="y%d" % c) for c in range(CHUNKS)]
-        picked = [[keep.tile([P, T], F32, name="picked%d_%d" % (r, c)) for c in range(CHUNKS)] for r in range(2)]
-        dh_t = keep.tile([P, T // P, 4, P], F32, name="dh_t")
+        picked = {}
+        second = {}
+        dh_t = [keep.tile([P, 4, P], F32, name="dh_t%d" % j) for j in range(BLOCKS)]
         da = keep.tile([P, T, 4], BF16, name="da", align_bytes=64)
         da_codes = keep.tile([P, T], U32, name="da_codes", align_bytes=64)
         da_scales = keep.tile([P, T], U8, name="da_scales", align_bytes=64)
         result = keep.tile([P, CHUNKS, T], F32, name="result")
 
-        mx_banks = [psum.tile([P, 512], F32, name="mx_bank%d" % b) for b in range(4)]
-        sum_banks = [psum.tile([P, 512], F32, name="sum_bank%d" % b) for b in range(2)]
-        back_banks = [psum.tile([P, 512], F32, name="back_bank%d" % b) for b in range(2)]
+        banks = [psum.tile([P, 512], F32, name="bank%d" % b) for b in range(8)]
 
-        nc.vector.memset(dys[:].rearrange("p a b -> p (a b)").bitcast(I32), 0)
-        nc.vector.memset(w2s[:].rearrange("p a b -> p (a b)").bitcast(I32), 0)
-        nc.vector.memset(w1s[:].bitcast(I32), 0)
+        nc.gpsimd.memset(dys[:, 0:T].bitcast(I32), 0)
+        nc.gpsimd.memset(dys[:, T:BYTE_WINDOW].bitcast(I32), 0)
         make_identity(nc, ident_made[:])
         nc.scalar.copy(out=ident[:], in_=ident_made[:])
+        for run in w2s:
+            nc.vector.memset(run[:].rearrange("p a b -> p (a b)").bitcast(I32), 0)
+        for s in range(1, PASSES):
+            nc.vector.memset(gs[s][:].bitcast(I32), 0)
+        nc.vector.memset(gate_rows[:], 0.0)
+        nc.vector.memset(w1s[:].bitcast(I32), 0)
 
-        dyw_src = dy_words.rearrange("s p t d -> s p (t d)")
-        dys_src = dy_scales.rearrange("s (q r) t -> r q s t", r=4)
+        dys_src = dy_scales.rearrange("s (q r) t -> q s r t", r=4)
         w2_src = w2t_words.rearrange("e s p b -> p (e s) b")
         w2s_src = w2t_scales.rearrange("e s (q r) n -> r q (e s) n", r=4)
         a_src = a.rearrange("(p t) n -> p t n", t=4)
         w1s_src = w1t_scales[0].rearrange("(q r) n -> r q n", r=4)
+        w2 = {}
+        w2_scale = {}
 
-        def load_w2(g):
-            e0, e1 = EXPERT_GROUPS[g]
+        def load_w2(e0, e1, c0, c1):
+            piece = keep.tile([P, (e1 - e0) * PASSES, 2 * P * (c1 - c0)], U8, name="w2_%d_%d" % (e0, c0), align_bytes=64)
             nc.sync.dma_start(
-                out=w2[:, PASSES * e0 : PASSES * e1, :].bitcast(I32),
-                in_=w2_src[:, PASSES * e0 : PASSES * e1, :].bitcast(I32),
+                out=piece[:].bitcast(I32),
+                in_=w2_src[:, PASSES * e0 : PASSES * e1, 2 * P * c0 : 2 * P * c1].bitcast(I32),
             )
+            for e in range(e0, e1):
+                for c in range(c0, c1):
+                    for s in range(PASSES):
+                        w2[e, c, s] = piece[:, PASSES * (e - e0) + s, 2 * P * (c - c0) : 2 * P * (c - c0 + 1)]
+
+        def load_w2_scales(h):
+            e0, e1 = SCALE_RUNS[h]
+            for r in range(4):
+                nc.sync.dma_start(
+                    out=w2s[h][r:P:32, :, :].bitcast(I32),
+                    in_=w2s_src[r][:, PASSES * e0 : PASSES * e1, :].bitcast(I32),
+                )
+            for e in range(e0, e1):
+                for s in range(PASSES):
+                    w2_scale[e, s] = w2s[h][:, PASSES * (e - e0) + s, :]
 
         nc.sync.dma_start(offs_t[:], offs)
-        for s in range(PASSES):
-            nc.sync.dma_start(out=dyw[s][:], in_=dyw_src[s].bitcast(I32))
-        for r in range(4):
-            nc.scalar.dma_start(out=dys[r:P:32, :, :].bitcast(I32), in_=dys_src[r].bitcast(I32))
-        for r in range(4):
-            nc.sync.dma_start(out=w2s[r:P:32, :, :].bitcast(I32), in_=w2s_src[r].bitcast(I32))
-        load_w2(0)
-        load_w2(1)
-        load_w2(2)
+        for q in range(4):
+            queue = nc.sync if q == 0 else nc.scalar
+            queue.dma_start(out=dys[32 * q : 32 * q + 4 * PASSES, 0:T].bitcast(I32), in_=dys_src[q].bitcast(I32))
+        nc.sync.dma_start(out=dyw[:], in_=dy_words.rearrange("s p t d -> p s (t d)").bitcast(I32))
+        load_w2_scales(0)
+        for piece in FIRST_LOADS:
+            load_w2(*piece)
         nc.sync.dma_start(pos_t[0][:], pos1)
-        nc.sync.dma_start(out=gate_t[0][:], in_=gate[0])
-        load_w2(3)
         nc.sync.dma_start(pos_t[1][:], pos2)
-        nc.sync.dma_start(out=gate_t[1][:], in_=gate[1])
+        nc.sync.dma_start(out=gate_rows[0 : 2 * BLOCKS, :], in_=gate[:, 0, :].rearrange("r (j u) -> r j u", u=P))
+        for piece in SECOND_LOADS:
+            load_w2(*piece)
         nc.sync.dma_start(out=a_t[:, :, 0:256], in_=a_src[:, :, 0:256])
         nc.sync.dma_start(out=w1[:].bitcast(I32), in_=w1t_words[0].bitcast(I32))
         for r in range(4):
             nc.sync.dma_start(out=w1s[r:P:32, :].bitcast(I32), in_=w1s_src[r].bitcast(I32))
         nc.sync.dma_start(out=a_t[:, :, 256:T], in_=a_src[:, :, 256:T])
 
-        def gather_slots(e0, e1):
+        nc.vector.tensor_copy(gs[0][:], dys[:].indirect(offs_t[:]))
+        for s in range(1, PASSES):
+            nc.scalar.dma_start(out=gs[s][0:SHIFT_ROWS, :].bitcast(I32), in_=gs[0][4 * s : 4 * s + SHIFT_ROWS, :].bitcast(I32))
+
+        def gather_words(e0, e1):
             picks = offs_t[:, C * e0 // 16 : C * e1 // 16]
             for s in range(PASSES):
-                nc.vector.tensor_copy(gw[s][:, C * e0 : C * e1].bitcast(U32), dyw[s][:].bitcast(U32).indirect(picks))
-            for s in range(PASSES):
-                nc.vector.tensor_copy(gs[s][:, C * e0 : C * e1], dys[:, s, :].indirect(picks))
+                nc.vector.tensor_copy(gw[s][:, C * e0 : C * e1].bitcast(U32), dyw[:, s, :].bitcast(U32).indirect(picks))
 
         def experts(c, e0, e1, bank):
             for e in range(e0, e1):
                 for s in range(PASSES):
                     nc.tensor.matmul_mx(
                         out=bank[:, C * (e - e0) : C * (e - e0 + 1)],
-                        lhsT=w2[:, PASSES * e + s, 2 * P * c : 2 * P * (c + 1)].bitcast(FP4X4),
-                        lhsT_scale=w2s[:, PASSES * e + s, P * c : P * (c + 1)],
+                        lhsT=w2[e, c, s].bitcast(FP4X4),
+                        lhsT_scale=w2_scale[e, s][:, P * c : P * (c + 1)],
                         rhs=gw[s][:, C * e : C * (e + 1)].bitcast(FP8X4),
                         rhs_scale=gs[s][:, C * e : C * (e + 1)],
                         start=(s == 0),
                         stop=(s == PASSES - 1),
                     )
             nc.scalar.copy(out=y[c][:, C * e0 : C * e1], in_=bank[:, 0 : C * (e1 - e0)])
-
-        for g, (e0, e1) in enumerate(EXPERT_GROUPS):
-            gather_slots(e0, e1)
-            for c in range(CHUNKS if g < 2 else 2):
-                experts(c, e0, e1, mx_banks[c])
-        for c in (2, 3):
-            experts(c, EXPERT_GROUPS[2][0], E, mx_banks[c - 2])
 
         def make_slope(j):
             nc.scalar.activation(
@@ -138,43 +159,56 @@ def tile_moe_sub_relu2_kernel(
                 scale=2.0,
             )
 
-        def pick(g):
-            t0, t1 = TOKEN_GROUPS[g]
-            for c in range(CHUNKS):
-                for r in range(2):
-                    nc.vector.tensor_tensor(
-                        picked[r][c][:, t0:t1], y[c][:].indirect(pos_t[r][:, t0 // 16 : t1 // 16]), gate_t[r][:, t0:t1], MULT
-                    )
+        def pick(c, j0, j1, tags=(None, None)):
+            for r in (1, 0):
+                name = "picked%d_%d_%d" % (r, c, j0)
+                room = keep.tile([P, P * (j1 - j0)], F32, name=name, tag=tags[r] or name)
+                nc.vector.tensor_copy(room[:], y[c][:].indirect(pos_t[r][:, P * j0 // 16 : P * j1 // 16]))
+                for j in range(j0, j1):
+                    picked[r, c, j] = room[:, P * (j - j0) : P * (j - j0 + 1)]
 
-        def turn_and_add(j):
-            bank = sum_banks[j % 2]
-            for c in range(CHUNKS):
-                for r in range(2):
-                    nc.tensor.matmul(
-                        out=bank[:, P * c : P * (c + 1)],
-                        lhsT=picked[r][c][:, P * j : P * (j + 1)],
-                        rhs=ident[:],
-                        is_transpose=True,
-                        start=(r == 0),
-                        stop=(r == 1),
-                    )
-            nc.scalar.copy(out=dh_t[:, j, :, :], in_=bank[:].rearrange("p (m t) -> p t m", t=4))
+        def turn(c, j, bank):
+            for r in (1, 0):
+                at = P * (2 * r + c % 2)
+                nc.tensor.transpose(bank[:, at : at + P], picked[r, c, j], ident[:])
 
-        def turn_back(j):
-            bank = back_banks[j % 2]
+        def scale_second(half, j, bank):
+            nc.scalar.activation(
+                out=second[half, j],
+                in_=bank[:, 2 * P : 4 * P].rearrange("p (m t) -> p t m", t=4),
+                func=COPY,
+                scale=gate_cols[:, BLOCKS + j : BLOCKS + j + 1],
+            )
+
+        def combine(half, j, bank):
+            nc.vector.scalar_tensor_tensor(
+                out=dh_t[j][:, :, 64 * half : 64 * (half + 1)],
+                in0=bank[:, 0 : 2 * P].rearrange("p (m t) -> p t m", t=4),
+                scalar=gate_cols[:, j : j + 1],
+                in1=second[half, j],
+                op0=MULT,
+                op1=ADD,
+            )
+
+        def second_room(half, j0, j1, tag):
+            room = keep.tile([P, j1 - j0, 4, 64], F32, name="second%d_%d" % (half, j0), tag=tag)
+            for j in range(j0, j1):
+                second[half, j] = room[:, j - j0, :, :]
+
+        def turn_back(j, bank):
             for t in range(4):
-                nc.tensor.transpose(bank[:, P * t : P * (t + 1)], dh_t[:, j, t, :], ident[:])
+                nc.tensor.transpose(bank[:, P * t : P * (t + 1)], dh_t[j][:, t, :], ident[:])
 
-        def make_da(j):
+        def make_da(j, bank):
             nc.vector.tensor_tensor(
                 da[:, P * j : P * (j + 1), :],
-                back_banks[j % 2][:].rearrange("p (t n) -> p n t", t=4),
+                bank[:].rearrange("p (t n) -> p n t", t=4),
                 slope[:, P * j : P * (j + 1), :],
                 MULT,
             )
 
-        def finish(g):
-            t0, t1 = TOKEN_GROUPS[g]
+        def finish(g, pair):
+            t0, t1 = OUT_GROUPS[g]
             n = t1 - t0
             nc.vector.quantize_mx(
                 out=da_codes[:, t0:t1].bitcast(FP8X4),
@@ -183,7 +217,7 @@ def tile_moe_sub_relu2_kernel(
             )
             out_view = out.rearrange("(c p) n -> p c n", p=P)
             for half in range(2):
-                bank = mx_banks[(2 * g + half + 2) % 4]
+                bank = pair[half]
                 for cc in range(2):
                     c = 2 * half + cc
                     nc.tensor.matmul_mx(
@@ -197,35 +231,72 @@ def tile_moe_sub_relu2_kernel(
                     )
                 dst = result[:, 2 * half : 2 * half + 2, t0:t1]
                 src = bank[:, 0 : 2 * n].rearrange("p (c n) -> p c n", c=2)
-                if g == len(TOKEN_GROUPS) - 1 and half == 1:
+                if g == len(OUT_GROUPS) - 1 and half == 1:
                     nc.vector.tensor_copy(out=dst, in_=src)
                 else:
                     nc.scalar.copy(out=dst, in_=src)
                 nc.sync.dma_start(out=out_view[:, 2 * half : 2 * half + 2, t0:t1], in_=dst)
 
-        pick(0)
-        turn_and_add(0)
-        turn_and_add(1)
-        turn_back(0)
-        turn_back(1)
-        make_slope(0)
-        make_slope(1)
-        pick(1)
-        turn_and_add(2)
-        turn_and_add(3)
-        make_da(0)
-        make_da(1)
-        finish(0)
-        turn_back(2)
-        turn_back(3)
-        make_slope(2)
-        make_slope(3)
-        make_slope(4)
-        pick(2)
-        turn_and_add(4)
-        make_da(2)
-        turn_back(4)
-        make_da(3)
-        finish(1)
-        make_da(4)
-        finish(2)
+        nc.tensor.transpose(banks[7][:, 0:P], gate_rows[:], ident[:])
+        nc.scalar.copy(out=gate_cols[:], in_=banks[7][:, 0 : 2 * BLOCKS])
+
+        for g, (e0, e1) in enumerate(GATHER_GROUPS):
+            gather_words(e0, e1)
+            for c in range(2):
+                experts(c, e0, e1, banks[2 * (g % 2) + c])
+            if g == 0:
+                for c in (2, 3):
+                    experts(c, 0, 2, banks[c + 2])
+
+        def turn_half(half, j, bank):
+            turn(2 * half, j, bank)
+            turn(2 * half + 1, j, bank)
+            scale_second(half, j, bank)
+
+        second_room(0, 0, 2, "second0_0")
+        second_room(0, 2, BLOCKS, "second0_2")
+        second_room(1, 0, BLOCKS, "second1")
+        pick(0, 0, 2)
+        pick(1, 0, 2)
+        for c in (2, 3):
+            experts(c, 2, 6, banks[c - 2])
+        pick(0, 2, BLOCKS)
+        pick(1, 2, BLOCKS)
+        for j in range(2):
+            turn_half(0, j, banks[j + 2])
+        for c in (2, 3):
+            experts(c, 6, 10, banks[c - 2])
+        for j in range(2, BLOCKS):
+            turn_half(0, j, banks[j + 2])
+        for j in range(BLOCKS):
+            combine(0, j, banks[j + 2])
+        for j in range(BLOCKS):
+            make_slope(j)
+
+        turned = [banks[7], banks[0], banks[1], banks[2], banks[3]]
+        back = [banks[4], banks[5], banks[6], banks[7], banks[0]]
+        pick(2, 0, 3, (None, "second0_0"))
+        pick(3, 0, 3)
+        for j in range(3):
+            turn(2, j, turned[j])
+        for j in range(3):
+            turn(3, j, turned[j])
+            scale_second(1, j, turned[j])
+        pick(2, 3, BLOCKS, (None, "second0_2"))
+        pick(3, 3, BLOCKS)
+        for j in range(3):
+            combine(1, j, turned[j])
+            turn_back(j, back[j])
+        for j in range(3, BLOCKS):
+            turn_half(1, j, turned[j])
+        make_da(0, back[0])
+        make_da(1, back[1])
+        for j in range(3, BLOCKS):
+            combine(1, j, turned[j])
+            turn_back(j, back[j])
+        finish(0, [banks[1], banks[4]])
+        make_da(2, back[2])
+        make_da(3, back[3])
+        finish(1, [banks[5], banks[2]])
+        make_da(4, back[4])
+        finish(2, [banks[3], banks[6]])

@@ -28,9 +28,9 @@ COPY = mybir.ActivationFunctionType.Copy
 BYTE_WINDOW = 1792
 SHIFT_ROWS = 112
 GATHER_GROUPS = [(0, 3), (3, 6), (6, 9), (9, 10)]
-FIRST_LOADS = [(0, 2, 0, 4), (2, 5, 0, 2), (5, 8, 0, 2), (8, 10, 0, 2)]
-SECOND_LOADS = [(2, 6, 2, 4), (6, 10, 2, 4)]
-SCALE_RUNS = [(0, 10)]
+FIRST_LOADS = [(0, 1, 0, 4), (1, 3, 0, 4), (3, 6, 0, 2), (6, 9, 0, 2), (9, 10, 0, 2)]
+SECOND_LOADS = [(3, 7, 2, 4), (7, 10, 2, 4)]
+SCALE_RUNS = [(0, 3), (3, 10)]
 OUT_GROUPS = [(0, 256), (256, 512), (512, 640)]
 
 
@@ -54,10 +54,10 @@ def tile_moe_sub_relu2_kernel(
         gate_rows = keep.tile([P, P], F32, name="gate_rows")
         gate_cols = keep.tile([P, 2 * BLOCKS], F32, name="gate_cols")
         a_t = keep.tile([P, 4, T], F32, name="a_t")
-        slope = keep.tile([P, T, 4], F32, name="slope")
-        ident_made = keep.tile([P, P], F32, name="ident_made")
+        slope = {}
         ident = keep.tile([P, P], F32, name="ident")
-        y = [keep.tile([P, S], F32, name="y%d" % c) for c in range(CHUNKS)]
+        y_first = keep.tile([P, 2, S], F32, name="y_first")
+        y = [y_first[:, 0, :], y_first[:, 1, :]] + [keep.tile([P, S], F32, name="y%d" % c)[:] for c in (2, 3)]
         picked = {}
         second = {}
         dh_t = [keep.tile([P, 4, P], F32, name="dh_t%d" % j) for j in range(BLOCKS)]
@@ -69,14 +69,13 @@ def tile_moe_sub_relu2_kernel(
         banks = [psum.tile([P, 512], F32, name="bank%d" % b) for b in range(8)]
 
         nc.gpsimd.memset(dys[:, 0:T].bitcast(I32), 0)
+        nc.gpsimd.memset(gate_rows[:], 0.0)
         nc.gpsimd.memset(dys[:, T:BYTE_WINDOW].bitcast(I32), 0)
-        make_identity(nc, ident_made[:])
-        nc.scalar.copy(out=ident[:], in_=ident_made[:])
+        make_identity(nc, ident[:])
         for run in w2s:
             nc.vector.memset(run[:].rearrange("p a b -> p (a b)").bitcast(I32), 0)
         for s in range(1, PASSES):
             nc.vector.memset(gs[s][:].bitcast(I32), 0)
-        nc.vector.memset(gate_rows[:], 0.0)
         nc.vector.memset(w1s[:].bitcast(I32), 0)
 
         dys_src = dy_scales.rearrange("s (q r) t -> q s r t", r=4)
@@ -88,7 +87,7 @@ def tile_moe_sub_relu2_kernel(
         w2_scale = {}
 
         def load_w2(e0, e1, c0, c1):
-            piece = keep.tile([P, (e1 - e0) * PASSES, 2 * P * (c1 - c0)], U8, name="w2_%d_%d" % (e0, c0), align_bytes=64)
+            piece = keep.tile([P, (e1 - e0) * PASSES, 2 * P * (c1 - c0)], U8, name="w2_%d_%d" % (e0, c0), tag="w2_%d_%d" % (e0, c0), align_bytes=64)
             nc.sync.dma_start(
                 out=piece[:].bitcast(I32),
                 in_=w2_src[:, PASSES * e0 : PASSES * e1, 2 * P * c0 : 2 * P * c1].bitcast(I32),
@@ -114,19 +113,22 @@ def tile_moe_sub_relu2_kernel(
             queue = nc.sync if q == 0 else nc.scalar
             queue.dma_start(out=dys[32 * q : 32 * q + 4 * PASSES, 0:T].bitcast(I32), in_=dys_src[q].bitcast(I32))
         nc.sync.dma_start(out=dyw[:], in_=dy_words.rearrange("s p t d -> p s (t d)").bitcast(I32))
+        nc.sync.dma_start(out=gate_rows[0 : 2 * BLOCKS, :], in_=gate[:, 0, :].rearrange("r (j u) -> r j u", u=P))
         load_w2_scales(0)
-        for piece in FIRST_LOADS:
+        load_w2(*FIRST_LOADS[0])
+        load_w2(*FIRST_LOADS[1])
+        load_w2_scales(1)
+        for piece in FIRST_LOADS[2:]:
             load_w2(*piece)
         nc.sync.dma_start(pos_t[0][:], pos1)
         nc.sync.dma_start(pos_t[1][:], pos2)
-        nc.sync.dma_start(out=gate_rows[0 : 2 * BLOCKS, :], in_=gate[:, 0, :].rearrange("r (j u) -> r j u", u=P))
         for piece in SECOND_LOADS:
             load_w2(*piece)
         nc.sync.dma_start(out=a_t[:, :, 0:256], in_=a_src[:, :, 0:256])
+        nc.sync.dma_start(out=a_t[:, :, 256:T], in_=a_src[:, :, 256:T])
         nc.sync.dma_start(out=w1[:].bitcast(I32), in_=w1t_words[0].bitcast(I32))
         for r in range(4):
             nc.sync.dma_start(out=w1s[r:P:32, :].bitcast(I32), in_=w1s_src[r].bitcast(I32))
-        nc.sync.dma_start(out=a_t[:, :, 256:T], in_=a_src[:, :, 256:T])
 
         nc.vector.tensor_copy(gs[0][:], dys[:].indirect(offs_t[:]))
         for s in range(1, PASSES):
@@ -137,11 +139,10 @@ def tile_moe_sub_relu2_kernel(
             for s in range(PASSES):
                 nc.vector.tensor_copy(gw[s][:, C * e0 : C * e1].bitcast(U32), dyw[:, s, :].bitcast(U32).indirect(picks))
 
-        def experts(c, e0, e1, bank):
-            for e in range(e0, e1):
-                for s in range(PASSES):
+        def product(c, e, place):
+            for s in range(PASSES):
                     nc.tensor.matmul_mx(
-                        out=bank[:, C * (e - e0) : C * (e - e0 + 1)],
+                        out=place,
                         lhsT=w2[e, c, s].bitcast(FP4X4),
                         lhsT_scale=w2_scale[e, s][:, P * c : P * (c + 1)],
                         rhs=gw[s][:, C * e : C * (e + 1)].bitcast(FP8X4),
@@ -149,23 +150,37 @@ def tile_moe_sub_relu2_kernel(
                         start=(s == 0),
                         stop=(s == PASSES - 1),
                     )
+
+        def experts(c, e0, e1, bank):
+            for e in range(e0, e1):
+                product(c, e, bank[:, C * (e - e0) : C * (e - e0 + 1)])
             nc.scalar.copy(out=y[c][:, C * e0 : C * e1], in_=bank[:, 0 : C * (e1 - e0)])
+
+        def first_half_of(e, bank):
+            for c in range(2):
+                product(c, e, bank[:, C * c : C * (c + 1)])
+            nc.scalar.copy(out=y_first[:, :, C * e : C * (e + 1)], in_=bank[:, 0 : 2 * C].rearrange("p (c n) -> p c n", c=2))
+
+        def slope_room(tag):
+            room = keep.tile([P, T, 4], F32, name="slope", tag=tag, align_bytes=64)
+            for j in range(BLOCKS):
+                slope[j] = room[:, P * j : P * (j + 1), :]
 
         def make_slope(j):
             nc.scalar.activation(
-                out=slope[:, P * j : P * (j + 1), :],
+                out=slope[j],
                 in_=a_t[:, :, P * j : P * (j + 1)].rearrange("p t n -> p n t"),
                 func=RELU,
                 scale=2.0,
             )
 
-        def pick(c, j0, j1, tags=(None, None)):
+        def pick(c, j0, j1, tag=None):
+            name = "picked%d_%d" % (c, j0)
+            room = keep.tile([P, 2, P * (j1 - j0)], F32, name=name, tag=tag or name)
             for r in (1, 0):
-                name = "picked%d_%d_%d" % (r, c, j0)
-                room = keep.tile([P, P * (j1 - j0)], F32, name=name, tag=tags[r] or name)
-                nc.vector.tensor_copy(room[:], y[c][:].indirect(pos_t[r][:, P * j0 // 16 : P * j1 // 16]))
+                nc.vector.tensor_copy(room[:, r, :], y[c].indirect(pos_t[r][:, P * j0 // 16 : P * j1 // 16]))
                 for j in range(j0, j1):
-                    picked[r, c, j] = room[:, P * (j - j0) : P * (j - j0 + 1)]
+                    picked[r, c, j] = room[:, r, P * (j - j0) : P * (j - j0 + 1)]
 
         def turn(c, j, bank):
             for r in (1, 0):
@@ -203,7 +218,7 @@ def tile_moe_sub_relu2_kernel(
             nc.vector.tensor_tensor(
                 da[:, P * j : P * (j + 1), :],
                 bank[:].rearrange("p (t n) -> p n t", t=4),
-                slope[:, P * j : P * (j + 1), :],
+                slope[j],
                 MULT,
             )
 
@@ -242,11 +257,14 @@ def tile_moe_sub_relu2_kernel(
 
         for g, (e0, e1) in enumerate(GATHER_GROUPS):
             gather_words(e0, e1)
-            for c in range(2):
-                experts(c, e0, e1, banks[2 * (g % 2) + c])
+            if e1 == E:
+                first_half_of(e0, banks[6])
+            else:
+                for c in range(2):
+                    experts(c, e0, e1, banks[2 * (g % 2) + c])
             if g == 0:
                 for c in (2, 3):
-                    experts(c, 0, 2, banks[c + 2])
+                    experts(c, e0, e1, banks[c + 2])
 
         def turn_half(half, j, bank):
             turn(2 * half, j, bank)
@@ -255,40 +273,48 @@ def tile_moe_sub_relu2_kernel(
 
         second_room(0, 0, 2, "second0_0")
         second_room(0, 2, BLOCKS, "second0_2")
-        second_room(1, 0, BLOCKS, "second1")
+        second_room(1, 0, 3, "second1_0")
+        second_room(1, 3, BLOCKS, "second1_3")
         pick(0, 0, 2)
         pick(1, 0, 2)
         for c in (2, 3):
-            experts(c, 2, 6, banks[c - 2])
+            experts(c, 3, 7, banks[c])
         pick(0, 2, BLOCKS)
         pick(1, 2, BLOCKS)
         for j in range(2):
             turn_half(0, j, banks[j + 2])
-        for c in (2, 3):
-            experts(c, 6, 10, banks[c - 2])
+        experts(2, 7, 10, banks[4])
+        experts(3, 7, 9, banks[5])
+        experts(3, 9, 10, banks[6])
         for j in range(2, BLOCKS):
             turn_half(0, j, banks[j + 2])
         for j in range(BLOCKS):
             combine(0, j, banks[j + 2])
-        for j in range(BLOCKS):
-            make_slope(j)
+        slope_room("w2_7_2")
 
         turned = [banks[7], banks[0], banks[1], banks[2], banks[3]]
         back = [banks[4], banks[5], banks[6], banks[7], banks[0]]
-        pick(2, 0, 3, (None, "second0_0"))
+        pick(2, 0, 3, "second0_0")
         pick(3, 0, 3)
         for j in range(3):
             turn(2, j, turned[j])
         for j in range(3):
             turn(3, j, turned[j])
             scale_second(1, j, turned[j])
-        pick(2, 3, BLOCKS, (None, "second0_2"))
-        pick(3, 3, BLOCKS)
+        pick(2, 3, BLOCKS, "second0_2")
+        for j in range(3, BLOCKS):
+            turn(2, j, turned[j])
         for j in range(3):
             combine(1, j, turned[j])
             turn_back(j, back[j])
+        make_slope(0)
+        make_slope(1)
+        pick(3, 3, BLOCKS, "second1_0")
         for j in range(3, BLOCKS):
-            turn_half(1, j, turned[j])
+            turn(3, j, turned[j])
+            scale_second(1, j, turned[j])
+        for j in range(2, BLOCKS):
+            make_slope(j)
         make_da(0, back[0])
         make_da(1, back[1])
         for j in range(3, BLOCKS):

@@ -28,9 +28,9 @@ COPY = mybir.ActivationFunctionType.Copy
 BYTE_WINDOW = 1792
 SHIFT_ROWS = 112
 GATHER_GROUPS = [(0, 3), (3, 6), (6, 9), (9, 10)]
-FIRST_LOADS = [(0, 1, 0, 4), (1, 3, 0, 4), (3, 6, 0, 2), (6, 9, 0, 2), (9, 10, 0, 2)]
-SECOND_LOADS = [(3, 7, 2, 4), (7, 10, 2, 4)]
-SCALE_RUNS = [(0, 3), (3, 10)]
+FIRST_LOADS = [(0, 3, 0, 2), (3, 6, 0, 2), (6, 9, 0, 2), (9, 10, 0, 2)]
+SECOND_LOADS = [(0, 4, 2, 4), (4, 8, 2, 4), (8, 10, 2, 4)]
+SCALE_RUNS = [(0, 10, 0, 2), (0, 10, 2, 4)]
 OUT_GROUPS = [(0, 256), (256, 512), (512, 640)]
 
 
@@ -48,7 +48,10 @@ def tile_moe_sub_relu2_kernel(
         dys = keep.tile([P, BYTE_WINDOW], U8, name="dys", align_bytes=64)
         gw = [keep.tile([P, S], I32, name="gw%d" % s, align_bytes=64) for s in range(PASSES)]
         gs = [keep.tile([P, S], U8, name="gs%d" % s, align_bytes=64) for s in range(PASSES)]
-        w2s = [keep.tile([P, (e1 - e0) * PASSES, H], U8, name="w2s%d" % e0, align_bytes=64) for e0, e1 in SCALE_RUNS]
+        w2s = [
+            keep.tile([P, (e1 - e0) * PASSES, P * (c1 - c0)], U8, name="w2s%d_%d" % (e0, c0), align_bytes=64)
+            for e0, e1, c0, c1 in SCALE_RUNS
+        ]
         w1 = keep.tile([P, 2 * K], U8, name="w1", align_bytes=64)
         w1s = keep.tile([P, K], U8, name="w1s", align_bytes=64)
         gate_rows = keep.tile([P, P], F32, name="gate_rows")
@@ -69,11 +72,12 @@ def tile_moe_sub_relu2_kernel(
         banks = [psum.tile([P, 512], F32, name="bank%d" % b) for b in range(8)]
 
         nc.gpsimd.memset(dys[:, 0:T].bitcast(I32), 0)
-        nc.gpsimd.memset(gate_rows[:], 0.0)
-        nc.gpsimd.memset(dys[:, T:BYTE_WINDOW].bitcast(I32), 0)
         make_identity(nc, ident[:])
-        for run in w2s:
+        nc.vector.memset(w2s[0][:].rearrange("p a b -> p (a b)").bitcast(I32), 0)
+        nc.vector.memset(dys[:, T:BYTE_WINDOW].bitcast(I32), 0)
+        for run in w2s[1:]:
             nc.vector.memset(run[:].rearrange("p a b -> p (a b)").bitcast(I32), 0)
+        nc.vector.memset(gate_rows[:], 0.0)
         for s in range(1, PASSES):
             nc.vector.memset(gs[s][:].bitcast(I32), 0)
         nc.vector.memset(w1s[:].bitcast(I32), 0)
@@ -97,33 +101,35 @@ def tile_moe_sub_relu2_kernel(
                     for s in range(PASSES):
                         w2[e, c, s] = piece[:, PASSES * (e - e0) + s, 2 * P * (c - c0) : 2 * P * (c - c0 + 1)]
 
+        def load_small():
+            nc.sync.dma_start(pos_t[0][:], pos1)
+            nc.sync.dma_start(pos_t[1][:], pos2)
+            nc.sync.dma_start(out=gate_rows[0 : 2 * BLOCKS, :], in_=gate[:, 0, :].rearrange("r (j u) -> r j u", u=P))
+
         def load_w2_scales(h):
-            e0, e1 = SCALE_RUNS[h]
+            e0, e1, c0, c1 = SCALE_RUNS[h]
             for r in range(4):
                 nc.sync.dma_start(
                     out=w2s[h][r:P:32, :, :].bitcast(I32),
-                    in_=w2s_src[r][:, PASSES * e0 : PASSES * e1, :].bitcast(I32),
+                    in_=w2s_src[r][:, PASSES * e0 : PASSES * e1, P * c0 : P * c1].bitcast(I32),
                 )
             for e in range(e0, e1):
-                for s in range(PASSES):
-                    w2_scale[e, s] = w2s[h][:, PASSES * (e - e0) + s, :]
+                for c in range(c0, c1):
+                    for s in range(PASSES):
+                        w2_scale[e, c, s] = w2s[h][:, PASSES * (e - e0) + s, P * (c - c0) : P * (c - c0 + 1)]
 
         nc.sync.dma_start(offs_t[:], offs)
         for q in range(4):
             queue = nc.sync if q == 0 else nc.scalar
             queue.dma_start(out=dys[32 * q : 32 * q + 4 * PASSES, 0:T].bitcast(I32), in_=dys_src[q].bitcast(I32))
         nc.sync.dma_start(out=dyw[:], in_=dy_words.rearrange("s p t d -> p s (t d)").bitcast(I32))
-        nc.sync.dma_start(out=gate_rows[0 : 2 * BLOCKS, :], in_=gate[:, 0, :].rearrange("r (j u) -> r j u", u=P))
         load_w2_scales(0)
-        load_w2(*FIRST_LOADS[0])
-        load_w2(*FIRST_LOADS[1])
+        for piece in FIRST_LOADS:
+            load_w2(*piece)
+        load_small()
         load_w2_scales(1)
-        for piece in FIRST_LOADS[2:]:
-            load_w2(*piece)
-        nc.sync.dma_start(pos_t[0][:], pos1)
-        nc.sync.dma_start(pos_t[1][:], pos2)
-        for piece in SECOND_LOADS:
-            load_w2(*piece)
+        for late in SECOND_LOADS:
+            load_w2(*late)
         nc.sync.dma_start(out=a_t[:, :, 0:256], in_=a_src[:, :, 0:256])
         nc.sync.dma_start(out=a_t[:, :, 256:T], in_=a_src[:, :, 256:T])
         nc.sync.dma_start(out=w1[:].bitcast(I32), in_=w1t_words[0].bitcast(I32))
@@ -144,7 +150,7 @@ def tile_moe_sub_relu2_kernel(
                     nc.tensor.matmul_mx(
                         out=place,
                         lhsT=w2[e, c, s].bitcast(FP4X4),
-                        lhsT_scale=w2_scale[e, s][:, P * c : P * (c + 1)],
+                        lhsT_scale=w2_scale[e, c, s],
                         rhs=gw[s][:, C * e : C * (e + 1)].bitcast(FP8X4),
                         rhs_scale=gs[s][:, C * e : C * (e + 1)],
                         start=(s == 0),
@@ -252,8 +258,9 @@ def tile_moe_sub_relu2_kernel(
                     nc.scalar.copy(out=dst, in_=src)
                 nc.sync.dma_start(out=out_view[:, 2 * half : 2 * half + 2, t0:t1], in_=dst)
 
-        nc.tensor.transpose(banks[7][:, 0:P], gate_rows[:], ident[:])
-        nc.scalar.copy(out=gate_cols[:], in_=banks[7][:, 0 : 2 * BLOCKS])
+        def turn_gate(bank):
+            nc.tensor.transpose(bank[:, 0:P], gate_rows[:], ident[:])
+            nc.scalar.copy(out=gate_cols[:], in_=bank[:, 0 : 2 * BLOCKS])
 
         for g, (e0, e1) in enumerate(GATHER_GROUPS):
             gather_words(e0, e1)
@@ -262,9 +269,7 @@ def tile_moe_sub_relu2_kernel(
             else:
                 for c in range(2):
                     experts(c, e0, e1, banks[2 * (g % 2) + c])
-            if g == 0:
-                for c in (2, 3):
-                    experts(c, e0, e1, banks[c + 2])
+        turn_gate(banks[0])
 
         def turn_half(half, j, bank):
             turn(2 * half, j, bank)
@@ -278,19 +283,21 @@ def tile_moe_sub_relu2_kernel(
         pick(0, 0, 2)
         pick(1, 0, 2)
         for c in (2, 3):
-            experts(c, 3, 7, banks[c])
+            experts(c, 0, 4, banks[c])
         pick(0, 2, BLOCKS)
         pick(1, 2, BLOCKS)
         for j in range(2):
             turn_half(0, j, banks[j + 2])
-        experts(2, 7, 10, banks[4])
-        experts(3, 7, 9, banks[5])
+        for c in (2, 3):
+            experts(c, 4, 8, banks[c - 2])
+        experts(2, 8, 10, banks[4])
+        experts(3, 8, 9, banks[5])
         experts(3, 9, 10, banks[6])
         for j in range(2, BLOCKS):
             turn_half(0, j, banks[j + 2])
         for j in range(BLOCKS):
             combine(0, j, banks[j + 2])
-        slope_room("w2_7_2")
+        slope_room("w2_8_2")
 
         turned = [banks[7], banks[0], banks[1], banks[2], banks[3]]
         back = [banks[4], banks[5], banks[6], banks[7], banks[0]]

@@ -21,9 +21,7 @@ U8 = mybir.dt.uint8
 FP8X4 = mybir.dt.float8_e4m3fn_x4
 FP4X4 = mybir.dt.float4_e2m1fn_x4
 MULT = mybir.AluOpType.mult
-ADD = mybir.AluOpType.add
 RELU = mybir.ActivationFunctionType.Relu
-COPY = mybir.ActivationFunctionType.Copy
 
 BYTE_WINDOW = 1792
 SHIFT_ROWS = 112
@@ -56,14 +54,13 @@ def tile_moe_sub_relu2_kernel(
         w1s = keep.tile([P, K], U8, name="w1s", align_bytes=64)
         gate_rows = keep.tile([P, P], F32, name="gate_rows")
         gate_cols = keep.tile([P, 2 * BLOCKS], F32, name="gate_cols")
+        gate_t = [keep.tile([P, T], F32, name="gate%d" % r) for r in range(2)]
         a_t = keep.tile([P, 4, T], F32, name="a_t")
         slope = {}
         ident = keep.tile([P, P], F32, name="ident")
-        y_first = keep.tile([P, 2, S], F32, name="y_first")
-        y = [y_first[:, 0, :], y_first[:, 1, :]] + [keep.tile([P, S], F32, name="y%d" % c)[:] for c in (2, 3)]
+        y = [keep.tile([P, S], F32, name="y%d" % c)[:] for c in range(CHUNKS)]
         picked = {}
-        second = {}
-        dh_t = [keep.tile([P, 4, P], F32, name="dh_t%d" % j) for j in range(BLOCKS)]
+        dh_t = keep.tile([P, BLOCKS, 4, P], F32, name="dh_t")
         da = keep.tile([P, T, 4], BF16, name="da", align_bytes=64)
         da_codes = keep.tile([P, T], U32, name="da_codes", align_bytes=64)
         da_scales = keep.tile([P, T], U8, name="da_scales", align_bytes=64)
@@ -72,12 +69,12 @@ def tile_moe_sub_relu2_kernel(
         banks = [psum.tile([P, 512], F32, name="bank%d" % b) for b in range(8)]
 
         nc.gpsimd.memset(dys[:, 0:T].bitcast(I32), 0)
+        nc.gpsimd.memset(gate_rows[:], 0.0)
         make_identity(nc, ident[:])
         nc.vector.memset(w2s[0][:].rearrange("p a b -> p (a b)").bitcast(I32), 0)
         nc.vector.memset(dys[:, T:BYTE_WINDOW].bitcast(I32), 0)
         for run in w2s[1:]:
             nc.vector.memset(run[:].rearrange("p a b -> p (a b)").bitcast(I32), 0)
-        nc.vector.memset(gate_rows[:], 0.0)
         for s in range(1, PASSES):
             nc.vector.memset(gs[s][:].bitcast(I32), 0)
         nc.vector.memset(w1s[:].bitcast(I32), 0)
@@ -104,7 +101,6 @@ def tile_moe_sub_relu2_kernel(
         def load_small():
             nc.sync.dma_start(pos_t[0][:], pos1)
             nc.sync.dma_start(pos_t[1][:], pos2)
-            nc.sync.dma_start(out=gate_rows[0 : 2 * BLOCKS, :], in_=gate[:, 0, :].rearrange("r (j u) -> r j u", u=P))
 
         def load_w2_scales(h):
             e0, e1, c0, c1 = SCALE_RUNS[h]
@@ -123,6 +119,7 @@ def tile_moe_sub_relu2_kernel(
             queue = nc.sync if q == 0 else nc.scalar
             queue.dma_start(out=dys[32 * q : 32 * q + 4 * PASSES, 0:T].bitcast(I32), in_=dys_src[q].bitcast(I32))
         nc.sync.dma_start(out=dyw[:], in_=dy_words.rearrange("s p t d -> p s (t d)").bitcast(I32))
+        nc.sync.dma_start(out=gate_rows[0 : 2 * BLOCKS, :], in_=gate[:, 0, :].rearrange("r (j u) -> r j u", u=P))
         load_w2_scales(0)
         for piece in FIRST_LOADS:
             load_w2(*piece)
@@ -130,8 +127,8 @@ def tile_moe_sub_relu2_kernel(
         load_w2_scales(1)
         for late in SECOND_LOADS:
             load_w2(*late)
-        nc.sync.dma_start(out=a_t[:, :, 0:256], in_=a_src[:, :, 0:256])
-        nc.sync.dma_start(out=a_t[:, :, 256:T], in_=a_src[:, :, 256:T])
+        nc.sync.dma_start(out=a_t[:, :, 0:384], in_=a_src[:, :, 0:384])
+        nc.sync.dma_start(out=a_t[:, :, 384:T], in_=a_src[:, :, 384:T])
         nc.sync.dma_start(out=w1[:].bitcast(I32), in_=w1t_words[0].bitcast(I32))
         for r in range(4):
             nc.sync.dma_start(out=w1s[r:P:32, :].bitcast(I32), in_=w1s_src[r].bitcast(I32))
@@ -162,15 +159,22 @@ def tile_moe_sub_relu2_kernel(
                 product(c, e, bank[:, C * (e - e0) : C * (e - e0 + 1)])
             nc.scalar.copy(out=y[c][:, C * e0 : C * e1], in_=bank[:, 0 : C * (e1 - e0)])
 
-        def first_half_of(e, bank):
-            for c in range(2):
-                product(c, e, bank[:, C * c : C * (c + 1)])
-            nc.scalar.copy(out=y_first[:, :, C * e : C * (e + 1)], in_=bank[:, 0 : 2 * C].rearrange("p (c n) -> p c n", c=2))
-
         def slope_room(tag):
             room = keep.tile([P, T, 4], F32, name="slope", tag=tag, align_bytes=64)
             for j in range(BLOCKS):
                 slope[j] = room[:, P * j : P * (j + 1), :]
+
+        def spread_gate(first, wide, rest):
+            nc.tensor.transpose(first[:, 0:P], gate_rows[:], ident[:])
+            nc.scalar.copy(out=gate_cols[:], in_=first[:, 0 : 2 * BLOCKS])
+            for r in range(2):
+                for j in range(BLOCKS):
+                    place = wide[r][:, P * j : P * (j + 1)] if j < 4 else rest[:, P * r : P * (r + 1)]
+                    column = gate_cols[:, BLOCKS * r + j : BLOCKS * r + j + 1]
+                    nc.tensor.transpose(place, column.to_broadcast([P, P]), ident[:])
+                nc.scalar.copy(out=gate_t[r][:, 0 : 4 * P], in_=wide[r][:])
+            for r in range(2):
+                nc.scalar.copy(out=gate_t[r][:, 4 * P : T], in_=rest[:, P * r : P * (r + 1)])
 
         def make_slope(j):
             nc.scalar.activation(
@@ -183,42 +187,32 @@ def tile_moe_sub_relu2_kernel(
         def pick(c, j0, j1, tag=None):
             name = "picked%d_%d" % (c, j0)
             room = keep.tile([P, 2, P * (j1 - j0)], F32, name=name, tag=tag or name)
-            for r in (1, 0):
-                nc.vector.tensor_copy(room[:, r, :], y[c].indirect(pos_t[r][:, P * j0 // 16 : P * j1 // 16]))
+            for r in range(2):
+                nc.vector.tensor_tensor(
+                    room[:, r, :], y[c].indirect(pos_t[r][:, P * j0 // 16 : P * j1 // 16]), gate_t[r][:, P * j0 : P * j1], MULT
+                )
                 for j in range(j0, j1):
                     picked[r, c, j] = room[:, r, P * (j - j0) : P * (j - j0 + 1)]
 
-        def turn(c, j, bank):
-            for r in (1, 0):
-                at = P * (2 * r + c % 2)
-                nc.tensor.transpose(bank[:, at : at + P], picked[r, c, j], ident[:])
-
-        def scale_second(half, j, bank):
-            nc.scalar.activation(
-                out=second[half, j],
-                in_=bank[:, 2 * P : 4 * P].rearrange("p (m t) -> p t m", t=4),
-                func=COPY,
-                scale=gate_cols[:, BLOCKS + j : BLOCKS + j + 1],
-            )
-
-        def combine(half, j, bank):
-            nc.vector.scalar_tensor_tensor(
-                out=dh_t[j][:, :, 64 * half : 64 * (half + 1)],
-                in0=bank[:, 0 : 2 * P].rearrange("p (m t) -> p t m", t=4),
-                scalar=gate_cols[:, j : j + 1],
-                in1=second[half, j],
-                op0=MULT,
-                op1=ADD,
-            )
-
-        def second_room(half, j0, j1, tag):
-            room = keep.tile([P, j1 - j0, 4, 64], F32, name="second%d_%d" % (half, j0), tag=tag)
+        def turn(c, j0, j1, bank):
             for j in range(j0, j1):
-                second[half, j] = room[:, j - j0, :, :]
+                for r in range(2):
+                    nc.tensor.matmul(
+                        out=bank[:, P * (j - j0) : P * (j - j0 + 1)],
+                        lhsT=picked[r, c, j],
+                        rhs=ident[:],
+                        is_transpose=True,
+                        start=(r == 0),
+                        stop=(r == 1),
+                    )
+            nc.scalar.copy(
+                out=dh_t[:, j0:j1, :, 32 * c : 32 * (c + 1)],
+                in_=bank[:, 0 : P * (j1 - j0)].rearrange("p (j m t) -> p j t m", m=32, t=4),
+            )
 
         def turn_back(j, bank):
             for t in range(4):
-                nc.tensor.transpose(bank[:, P * t : P * (t + 1)], dh_t[j][:, t, :], ident[:])
+                nc.tensor.transpose(bank[:, P * t : P * (t + 1)], dh_t[:, j, t, :], ident[:])
 
         def make_da(j, bank):
             nc.vector.tensor_tensor(
@@ -258,78 +252,49 @@ def tile_moe_sub_relu2_kernel(
                     nc.scalar.copy(out=dst, in_=src)
                 nc.sync.dma_start(out=out_view[:, 2 * half : 2 * half + 2, t0:t1], in_=dst)
 
-        def turn_gate(bank):
-            nc.tensor.transpose(bank[:, 0:P], gate_rows[:], ident[:])
-            nc.scalar.copy(out=gate_cols[:], in_=bank[:, 0 : 2 * BLOCKS])
-
+        spread_gate(banks[7], banks[4:6], banks[6])
         for g, (e0, e1) in enumerate(GATHER_GROUPS):
             gather_words(e0, e1)
-            if e1 == E:
-                first_half_of(e0, banks[6])
-            else:
-                for c in range(2):
-                    experts(c, e0, e1, banks[2 * (g % 2) + c])
-        turn_gate(banks[0])
+            for c in range(2):
+                experts(c, e0, e1, banks[2 * (g % 2) + c])
 
-        def turn_half(half, j, bank):
-            turn(2 * half, j, bank)
-            turn(2 * half + 1, j, bank)
-            scale_second(half, j, bank)
-
-        second_room(0, 0, 2, "second0_0")
-        second_room(0, 2, BLOCKS, "second0_2")
-        second_room(1, 0, 3, "second1_0")
-        second_room(1, 3, BLOCKS, "second1_3")
-        pick(0, 0, 2)
-        pick(1, 0, 2)
+        pick(0, 0, BLOCKS)
         for c in (2, 3):
-            experts(c, 0, 4, banks[c])
-        pick(0, 2, BLOCKS)
-        pick(1, 2, BLOCKS)
-        for j in range(2):
-            turn_half(0, j, banks[j + 2])
+            experts(c, 0, 4, banks[c + 2])
+        pick(1, 0, BLOCKS)
         for c in (2, 3):
-            experts(c, 4, 8, banks[c - 2])
-        experts(2, 8, 10, banks[4])
-        experts(3, 8, 9, banks[5])
-        experts(3, 9, 10, banks[6])
-        for j in range(2, BLOCKS):
-            turn_half(0, j, banks[j + 2])
-        for j in range(BLOCKS):
-            combine(0, j, banks[j + 2])
+            experts(c, 4, 8, banks[c + 4])
+        turn(0, 0, 4, banks[6])
+        turn(0, 4, BLOCKS, banks[7])
+        for c in (2, 3):
+            experts(c, 8, 10, banks[c - 2])
+        turn(1, 0, 4, banks[0])
+        turn(1, 4, BLOCKS, banks[1])
         slope_room("w2_8_2")
-
-        turned = [banks[7], banks[0], banks[1], banks[2], banks[3]]
-        back = [banks[4], banks[5], banks[6], banks[7], banks[0]]
-        pick(2, 0, 3, "second0_0")
-        pick(3, 0, 3)
         for j in range(3):
-            turn(2, j, turned[j])
-        for j in range(3):
-            turn(3, j, turned[j])
-            scale_second(1, j, turned[j])
-        pick(2, 3, BLOCKS, "second0_2")
-        for j in range(3, BLOCKS):
-            turn(2, j, turned[j])
-        for j in range(3):
-            combine(1, j, turned[j])
-            turn_back(j, back[j])
-        make_slope(0)
-        make_slope(1)
-        pick(3, 3, BLOCKS, "second1_0")
-        for j in range(3, BLOCKS):
-            turn(3, j, turned[j])
-            scale_second(1, j, turned[j])
-        for j in range(2, BLOCKS):
             make_slope(j)
+
+        pick(2, 0, BLOCKS)
+        turn(2, 0, 4, banks[2])
+        turn(2, 4, BLOCKS, banks[3])
+        pick(3, 0, 2)
+        turn(3, 0, 2, banks[4])
+        back = [banks[5], banks[6], banks[7], banks[0], banks[1]]
+        turn_back(0, back[0])
+        turn_back(1, back[1])
+        for j in range(3, BLOCKS):
+            make_slope(j)
+        pick(3, 2, BLOCKS)
+        turn(3, 2, 3, banks[2])
+        turn(3, 3, BLOCKS, banks[3])
+        turn_back(2, back[2])
+        turn_back(3, back[3])
+        turn_back(4, back[4])
         make_da(0, back[0])
         make_da(1, back[1])
-        for j in range(3, BLOCKS):
-            combine(1, j, turned[j])
-            turn_back(j, back[j])
-        finish(0, [banks[1], banks[4]])
+        finish(0, [banks[4], banks[5]])
         make_da(2, back[2])
         make_da(3, back[3])
-        finish(1, [banks[5], banks[2]])
+        finish(1, [banks[6], banks[2]])
         make_da(4, back[4])
-        finish(2, [banks[3], banks[6]])
+        finish(2, [banks[3], banks[7]])

@@ -25,11 +25,8 @@ RELU = mybir.ActivationFunctionType.Relu
 
 BYTE_WINDOW = 1792
 SHIFT_ROWS = 112
-GATHER_GROUPS = [(0, 3), (3, 6), (6, 9), (9, 10)]
-FIRST_LOADS = [(0, 3, 0, 2), (3, 6, 0, 2), (6, 9, 0, 2), (9, 10, 0, 2)]
-SECOND_LOADS = [(0, 4, 2, 4), (4, 8, 2, 4), (8, 10, 2, 4)]
-SCALE_RUNS = [(0, 10, 0, 2), (0, 10, 2, 4)]
-OUT_GROUPS = [(0, 256), (256, 512), (512, 640)]
+EARLY_SLOTS = 3 * C
+TOKEN_GROUPS = [(0, 2), (2, 4), (4, 5)]
 
 
 def tile_moe_sub_relu2_kernel(
@@ -42,21 +39,20 @@ def tile_moe_sub_relu2_kernel(
 
         offs_t = keep.tile([P, S // 16], U16, name="offs_t")
         pos_t = [keep.tile([P, T // 16], U16, name="pos%d_t" % r) for r in range(2)]
-        dyw = keep.tile([P, PASSES, T], I32, name="dyw", align_bytes=64)
-        dys = keep.tile([P, BYTE_WINDOW], U8, name="dys", align_bytes=64)
-        gw = [keep.tile([P, S], I32, name="gw%d" % s, align_bytes=64) for s in range(PASSES)]
-        gs = [keep.tile([P, S], U8, name="gs%d" % s, align_bytes=64) for s in range(PASSES)]
-        w2s = [
-            keep.tile([P, (e1 - e0) * PASSES, P * (c1 - c0)], U8, name="w2s%d_%d" % (e0, c0), align_bytes=64)
-            for e0, e1, c0, c1 in SCALE_RUNS
-        ]
+        dyw_first = keep.tile([P, T], I32, name="dyw_first", align_bytes=64)
+        dyw_rest = keep.tile([P, PASSES - 1, T], I32, name="dyw_rest", align_bytes=64)
+        dyw = [dyw_first[:]] + [dyw_rest[:, s, :] for s in range(PASSES - 1)]
+        dys = keep.tile([P, BYTE_WINDOW], U8, name="dys", tag="after_bytes", align_bytes=64)
+        gw_early = keep.tile([P, EARLY_SLOTS], I32, name="gw_early", align_bytes=64)
+        gs = {s: keep.tile([P, S], U8, name="gs%d" % s, align_bytes=64) for s in range(1, PASSES)}
+        w2s = [keep.tile([P, E * PASSES, 2 * P], U8, name="w2s%d" % h, align_bytes=64) for h in range(2)]
         w1 = keep.tile([P, 2 * K], U8, name="w1", align_bytes=64)
         w1s = keep.tile([P, K], U8, name="w1s", align_bytes=64)
-        gate_rows = keep.tile([P, P], F32, name="gate_rows")
+        gate_rows = keep.tile([P, P], F32, name="gate_rows", tag="after_gate_rows", align_bytes=64)
         gate_cols = keep.tile([P, 2 * BLOCKS], F32, name="gate_cols")
         gate_t = [keep.tile([P, T], F32, name="gate%d" % r) for r in range(2)]
-        a_t = keep.tile([P, 4, T], F32, name="a_t")
-        slope = {}
+        a_t = [keep.tile([P, 4, P * (j1 - j0)], F32, name="a%d" % j0) for j0, j1 in TOKEN_GROUPS]
+        slope = [keep.tile([P, P * (j1 - j0), 4], F32, name="slope%d" % j0) for j0, j1 in TOKEN_GROUPS]
         ident = keep.tile([P, P], F32, name="ident")
         y = [keep.tile([P, S], F32, name="y%d" % c)[:] for c in range(CHUNKS)]
         picked = {}
@@ -68,27 +64,26 @@ def tile_moe_sub_relu2_kernel(
 
         banks = [psum.tile([P, 512], F32, name="bank%d" % b) for b in range(8)]
 
-        nc.gpsimd.memset(dys[:, 0:T].bitcast(I32), 0)
+        nc.vector.memset(dys[:, 0:T].bitcast(I32), 0)
         nc.gpsimd.memset(gate_rows[:], 0.0)
         make_identity(nc, ident[:])
         nc.vector.memset(w2s[0][:].rearrange("p a b -> p (a b)").bitcast(I32), 0)
         nc.vector.memset(dys[:, T:BYTE_WINDOW].bitcast(I32), 0)
-        for run in w2s[1:]:
-            nc.vector.memset(run[:].rearrange("p a b -> p (a b)").bitcast(I32), 0)
         for s in range(1, PASSES):
             nc.vector.memset(gs[s][:].bitcast(I32), 0)
+        nc.vector.memset(w2s[1][:].rearrange("p a b -> p (a b)").bitcast(I32), 0)
         nc.vector.memset(w1s[:].bitcast(I32), 0)
 
+        dyw_src = dy_words.rearrange("s p t d -> p s (t d)").bitcast(I32)
         dys_src = dy_scales.rearrange("s (q r) t -> q s r t", r=4)
         w2_src = w2t_words.rearrange("e s p b -> p (e s) b")
         w2s_src = w2t_scales.rearrange("e s (q r) n -> r q (e s) n", r=4)
         a_src = a.rearrange("(p t) n -> p t n", t=4)
         w1s_src = w1t_scales[0].rearrange("(q r) n -> r q n", r=4)
         w2 = {}
-        w2_scale = {}
 
         def load_w2(e0, e1, c0, c1):
-            piece = keep.tile([P, (e1 - e0) * PASSES, 2 * P * (c1 - c0)], U8, name="w2_%d_%d" % (e0, c0), tag="w2_%d_%d" % (e0, c0), align_bytes=64)
+            piece = keep.tile([P, (e1 - e0) * PASSES, 2 * P * (c1 - c0)], U8, name="w2_%d_%d" % (e0, c0), align_bytes=64)
             nc.sync.dma_start(
                 out=piece[:].bitcast(I32),
                 in_=w2_src[:, PASSES * e0 : PASSES * e1, 2 * P * c0 : 2 * P * c1].bitcast(I32),
@@ -98,71 +93,43 @@ def tile_moe_sub_relu2_kernel(
                     for s in range(PASSES):
                         w2[e, c, s] = piece[:, PASSES * (e - e0) + s, 2 * P * (c - c0) : 2 * P * (c - c0 + 1)]
 
-        def load_small():
-            nc.sync.dma_start(pos_t[0][:], pos1)
-            nc.sync.dma_start(pos_t[1][:], pos2)
-
         def load_w2_scales(h):
-            e0, e1, c0, c1 = SCALE_RUNS[h]
             for r in range(4):
                 nc.sync.dma_start(
                     out=w2s[h][r:P:32, :, :].bitcast(I32),
-                    in_=w2s_src[r][:, PASSES * e0 : PASSES * e1, P * c0 : P * c1].bitcast(I32),
+                    in_=w2s_src[r][:, :, 2 * P * h : 2 * P * (h + 1)].bitcast(I32),
                 )
-            for e in range(e0, e1):
-                for c in range(c0, c1):
-                    for s in range(PASSES):
-                        w2_scale[e, c, s] = w2s[h][:, PASSES * (e - e0) + s, P * (c - c0) : P * (c - c0 + 1)]
 
+        nc.sync.dma_start(out=dyw[0], in_=dyw_src[:, 0, :])
         nc.sync.dma_start(offs_t[:], offs)
+        nc.scalar.dma_start(out=gate_rows[0 : 2 * BLOCKS, :], in_=gate[:, 0, :].rearrange("r (j u) -> r j u", u=P))
+        nc.sync.dma_start(out=dyw_rest[:], in_=dyw_src[:, 1:PASSES, :])
         for q in range(4):
-            queue = nc.sync if q == 0 else nc.scalar
+            queue = nc.sync if q < 2 else nc.scalar
             queue.dma_start(out=dys[32 * q : 32 * q + 4 * PASSES, 0:T].bitcast(I32), in_=dys_src[q].bitcast(I32))
-        nc.sync.dma_start(out=dyw[:], in_=dy_words.rearrange("s p t d -> p s (t d)").bitcast(I32))
-        nc.sync.dma_start(out=gate_rows[0 : 2 * BLOCKS, :], in_=gate[:, 0, :].rearrange("r (j u) -> r j u", u=P))
         load_w2_scales(0)
-        for piece in FIRST_LOADS:
-            load_w2(*piece)
-        load_small()
+        load_w2(0, 3, 0, 3)
+        load_w2(3, 6, 0, 3)
+        load_w2(6, 9, 0, 2)
+        load_w2(9, 10, 0, 2)
+        nc.sync.dma_start(pos_t[0][:], pos1)
+        nc.sync.dma_start(pos_t[1][:], pos2)
         load_w2_scales(1)
-        for late in SECOND_LOADS:
-            load_w2(*late)
-        nc.sync.dma_start(out=a_t[:, :, 0:384], in_=a_src[:, :, 0:384])
-        nc.sync.dma_start(out=a_t[:, :, 384:T], in_=a_src[:, :, 384:T])
+        load_w2(6, 10, 2, 4)
+        load_w2(0, 4, 3, 4)
+        load_w2(4, 6, 3, 4)
+        for g, (j0, j1) in enumerate(TOKEN_GROUPS):
+            nc.sync.dma_start(out=a_t[g][:], in_=a_src[:, :, P * j0 : P * j1])
         nc.sync.dma_start(out=w1[:].bitcast(I32), in_=w1t_words[0].bitcast(I32))
         for r in range(4):
             nc.sync.dma_start(out=w1s[r:P:32, :].bitcast(I32), in_=w1s_src[r].bitcast(I32))
 
-        nc.vector.tensor_copy(gs[0][:], dys[:].indirect(offs_t[:]))
-        for s in range(1, PASSES):
-            nc.scalar.dma_start(out=gs[s][0:SHIFT_ROWS, :].bitcast(I32), in_=gs[0][4 * s : 4 * s + SHIFT_ROWS, :].bitcast(I32))
+        gw = {}
 
-        def gather_words(e0, e1):
-            picks = offs_t[:, C * e0 // 16 : C * e1 // 16]
-            for s in range(PASSES):
-                nc.vector.tensor_copy(gw[s][:, C * e0 : C * e1].bitcast(U32), dyw[:, s, :].bitcast(U32).indirect(picks))
-
-        def product(c, e, place):
-            for s in range(PASSES):
-                    nc.tensor.matmul_mx(
-                        out=place,
-                        lhsT=w2[e, c, s].bitcast(FP4X4),
-                        lhsT_scale=w2_scale[e, c, s],
-                        rhs=gw[s][:, C * e : C * (e + 1)].bitcast(FP8X4),
-                        rhs_scale=gs[s][:, C * e : C * (e + 1)],
-                        start=(s == 0),
-                        stop=(s == PASSES - 1),
-                    )
-
-        def experts(c, e0, e1, bank):
+        def gather_words(s, e0, e1, room):
+            nc.vector.tensor_copy(room.bitcast(U32), dyw[s].bitcast(U32).indirect(offs_t[:, C * e0 // 16 : C * e1 // 16]))
             for e in range(e0, e1):
-                product(c, e, bank[:, C * (e - e0) : C * (e - e0 + 1)])
-            nc.scalar.copy(out=y[c][:, C * e0 : C * e1], in_=bank[:, 0 : C * (e1 - e0)])
-
-        def slope_room(tag):
-            room = keep.tile([P, T, 4], F32, name="slope", tag=tag, align_bytes=64)
-            for j in range(BLOCKS):
-                slope[j] = room[:, P * j : P * (j + 1), :]
+                gw[s, e] = room[:, C * (e - e0) : C * (e - e0 + 1)]
 
         def spread_gate(first, wide, rest):
             nc.tensor.transpose(first[:, 0:P], gate_rows[:], ident[:])
@@ -176,13 +143,37 @@ def tile_moe_sub_relu2_kernel(
             for r in range(2):
                 nc.scalar.copy(out=gate_t[r][:, 4 * P : T], in_=rest[:, P * r : P * (r + 1)])
 
-        def make_slope(j):
-            nc.scalar.activation(
-                out=slope[j],
-                in_=a_t[:, :, P * j : P * (j + 1)].rearrange("p t n -> p n t"),
-                func=RELU,
-                scale=2.0,
-            )
+        spread_gate(banks[7], banks[4:6], banks[6])
+
+        gather_words(0, 0, 3, gw_early[:])
+        gs[0] = keep.tile([P, S], U8, name="gs0", tag="after_gate_rows", align_bytes=64)
+        nc.vector.tensor_copy(gs[0][:], dys[:].indirect(offs_t[:]))
+        for s in range(1, PASSES):
+            nc.scalar.dma_start(out=gs[s][0:SHIFT_ROWS, :].bitcast(I32), in_=gs[0][4 * s : 4 * s + SHIFT_ROWS, :].bitcast(I32))
+        gw_late = keep.tile([P, PASSES * S - EARLY_SLOTS], I32, name="gw_late", tag="after_bytes", align_bytes=64)
+        filled = 0
+        for e0, e1 in ((0, 3), (3, 6), (6, 9), (9, 10)):
+            for s in range(PASSES):
+                if (s, e0) not in gw:
+                    gather_words(s, e0, e1, gw_late[:, filled : filled + C * (e1 - e0)])
+                    filled = filled + C * (e1 - e0)
+
+        def experts(c, e0, e1, bank):
+            for e in range(e0, e1):
+                for s in range(PASSES):
+                    nc.tensor.matmul_mx(
+                        out=bank[:, C * (e - e0) : C * (e - e0 + 1)],
+                        lhsT=w2[e, c, s].bitcast(FP4X4),
+                        lhsT_scale=w2s[c // 2][:, PASSES * e + s, P * (c % 2) : P * (c % 2 + 1)],
+                        rhs=gw[s, e].bitcast(FP8X4),
+                        rhs_scale=gs[s][:, C * e : C * (e + 1)],
+                        start=(s == 0),
+                        stop=(s == PASSES - 1),
+                    )
+            nc.scalar.copy(out=y[c][:, C * e0 : C * e1], in_=bank[:, 0 : C * (e1 - e0)])
+
+        def make_slope(g):
+            nc.scalar.activation(out=slope[g][:], in_=a_t[g][:].rearrange("p t n -> p n t"), func=RELU, scale=2.0)
 
         def pick(c, j0, j1, tag=None):
             name = "picked%d_%d" % (c, j0)
@@ -194,17 +185,21 @@ def tile_moe_sub_relu2_kernel(
                 for j in range(j0, j1):
                     picked[r, c, j] = room[:, r, P * (j - j0) : P * (j - j0 + 1)]
 
+        def add_turned(c, j, place):
+            for r in range(2):
+                nc.tensor.matmul(out=place, lhsT=picked[r, c, j], rhs=ident[:], is_transpose=True, start=(r == 0), stop=(r == 1))
+
+        def turn_last(bank):
+            for c in (2, 3):
+                add_turned(c, BLOCKS - 1, bank[:, P * (c - 2) : P * (c - 1)])
+            nc.scalar.copy(
+                out=dh_t[:, BLOCKS - 1, :, 64:P],
+                in_=bank[:, 0 : 2 * P].rearrange("p (m t) -> p t m", t=4),
+            )
+
         def turn(c, j0, j1, bank):
             for j in range(j0, j1):
-                for r in range(2):
-                    nc.tensor.matmul(
-                        out=bank[:, P * (j - j0) : P * (j - j0 + 1)],
-                        lhsT=picked[r, c, j],
-                        rhs=ident[:],
-                        is_transpose=True,
-                        start=(r == 0),
-                        stop=(r == 1),
-                    )
+                add_turned(c, j, bank[:, P * (j - j0) : P * (j - j0 + 1)])
             nc.scalar.copy(
                 out=dh_t[:, j0:j1, :, 32 * c : 32 * (c + 1)],
                 in_=bank[:, 0 : P * (j1 - j0)].rearrange("p (j m t) -> p j t m", m=32, t=4),
@@ -218,18 +213,21 @@ def tile_moe_sub_relu2_kernel(
             nc.vector.tensor_tensor(
                 da[:, P * j : P * (j + 1), :],
                 bank[:].rearrange("p (t n) -> p n t", t=4),
-                slope[j],
+                slope[j // 2][:, P * (j % 2) : P * (j % 2 + 1), :],
                 MULT,
             )
 
-        def finish(g, pair):
-            t0, t1 = OUT_GROUPS[g]
-            n = t1 - t0
+        def quantize(g):
+            t0, t1 = P * TOKEN_GROUPS[g][0], P * TOKEN_GROUPS[g][1]
             nc.vector.quantize_mx(
                 out=da_codes[:, t0:t1].bitcast(FP8X4),
                 scales=da_scales[:, t0:t1],
                 in_=da[:, t0:t1, :].rearrange("p n t -> p (n t)"),
             )
+
+        def finish(g, pair):
+            t0, t1 = P * TOKEN_GROUPS[g][0], P * TOKEN_GROUPS[g][1]
+            n = t1 - t0
             out_view = out.rearrange("(c p) n -> p c n", p=P)
             for half in range(2):
                 bank = pair[half]
@@ -246,55 +244,60 @@ def tile_moe_sub_relu2_kernel(
                     )
                 dst = result[:, 2 * half : 2 * half + 2, t0:t1]
                 src = bank[:, 0 : 2 * n].rearrange("p (c n) -> p c n", c=2)
-                if g == len(OUT_GROUPS) - 1 and half == 1:
+                if g > 0 and half == 1:
                     nc.vector.tensor_copy(out=dst, in_=src)
                 else:
                     nc.scalar.copy(out=dst, in_=src)
                 nc.sync.dma_start(out=out_view[:, 2 * half : 2 * half + 2, t0:t1], in_=dst)
 
-        spread_gate(banks[7], banks[4:6], banks[6])
-        for g, (e0, e1) in enumerate(GATHER_GROUPS):
-            gather_words(e0, e1)
-            for c in range(2):
-                experts(c, e0, e1, banks[2 * (g % 2) + c])
+        experts(0, 0, 3, banks[0])
+        experts(1, 0, 3, banks[1])
+        experts(0, 3, 6, banks[2])
+        experts(1, 3, 6, banks[3])
+        experts(0, 6, 9, banks[4])
+        experts(0, 9, 10, banks[5])
+        experts(1, 6, 9, banks[5])
+        experts(1, 9, 10, banks[6])
 
         pick(0, 0, BLOCKS)
-        for c in (2, 3):
-            experts(c, 0, 4, banks[c + 2])
+        experts(2, 0, 4, banks[0])
+        experts(2, 4, 6, banks[1])
+        turn(0, 0, 4, banks[0])
+        turn(0, 4, BLOCKS, banks[1])
         pick(1, 0, BLOCKS)
-        for c in (2, 3):
-            experts(c, 4, 8, banks[c + 4])
-        turn(0, 0, 4, banks[6])
-        turn(0, 4, BLOCKS, banks[7])
-        for c in (2, 3):
-            experts(c, 8, 10, banks[c - 2])
-        turn(1, 0, 4, banks[0])
-        turn(1, 4, BLOCKS, banks[1])
-        slope_room("w2_8_2")
-        for j in range(3):
-            make_slope(j)
-
-        pick(2, 0, BLOCKS)
-        turn(2, 0, 4, banks[2])
-        turn(2, 4, BLOCKS, banks[3])
+        experts(2, 6, 10, banks[2])
+        experts(3, 6, 10, banks[3])
+        experts(3, 0, 4, banks[4])
+        experts(3, 4, 5, banks[5])
+        experts(3, 5, 6, banks[6])
+        turn(1, 4, BLOCKS, banks[4])
+        turn(1, 0, 4, banks[5])
+        pick(2, 0, 4)
+        turn(2, 0, 4, banks[6])
+        make_slope(0)
         pick(3, 0, 2)
-        turn(3, 0, 2, banks[4])
-        back = [banks[5], banks[6], banks[7], banks[0], banks[1]]
+        turn(3, 0, 2, banks[7])
+        back = [banks[0], banks[1], banks[3], banks[4], banks[5]]
         turn_back(0, back[0])
         turn_back(1, back[1])
-        for j in range(3, BLOCKS):
-            make_slope(j)
-        pick(3, 2, BLOCKS)
-        turn(3, 2, 3, banks[2])
-        turn(3, 3, BLOCKS, banks[3])
+        make_slope(1)
+        pick(3, 2, 4)
+        turn(3, 2, 4, banks[7])
+        pick(3, 4, BLOCKS)
+        pick(2, 4, BLOCKS, tag="picked3_0")
+        make_da(0, back[0])
+        turn_last(back[0])
+        make_slope(2)
+        make_da(1, back[1])
+        quantize(0)
         turn_back(2, back[2])
         turn_back(3, back[3])
         turn_back(4, back[4])
-        make_da(0, back[0])
-        make_da(1, back[1])
-        finish(0, [banks[4], banks[5]])
+        finish(0, [back[0], banks[7]])
         make_da(2, back[2])
         make_da(3, back[3])
-        finish(1, [banks[6], banks[2]])
+        quantize(1)
         make_da(4, back[4])
-        finish(2, [banks[3], banks[7]])
+        quantize(2)
+        finish(1, [banks[2], banks[6]])
+        finish(2, [back[1], back[2]])

@@ -48,7 +48,7 @@ def tile_moe_sub_relu2_kernel(
         w2s = [keep.tile([P, E * PASSES, 2 * P], U8, name="w2s%d" % h, align_bytes=64) for h in range(2)]
         w1 = keep.tile([P, 2 * K], U8, name="w1", align_bytes=64)
         w1s = keep.tile([P, K], U8, name="w1s", align_bytes=64)
-        gate_rows = keep.tile([P, P], F32, name="gate_rows", tag="after_gate_rows", align_bytes=64)
+        gate_rows = keep.tile([P, P], F32, name="gate_rows")
         gate_cols = keep.tile([P, 2 * BLOCKS], F32, name="gate_cols")
         gate_t = [keep.tile([P, T], F32, name="gate%d" % r) for r in range(2)]
         a_t = [keep.tile([P, 4, P * (j1 - j0)], F32, name="a%d" % j0) for j0, j1 in TOKEN_GROUPS]
@@ -108,21 +108,7 @@ def tile_moe_sub_relu2_kernel(
             queue = nc.sync if q < 2 else nc.scalar
             queue.dma_start(out=dys[32 * q : 32 * q + 4 * PASSES, 0:T].bitcast(I32), in_=dys_src[q].bitcast(I32))
         load_w2_scales(0)
-        load_w2(0, 3, 0, 3)
-        load_w2(3, 6, 0, 3)
-        load_w2(6, 9, 0, 2)
-        load_w2(9, 10, 0, 2)
-        nc.sync.dma_start(pos_t[0][:], pos1)
-        nc.sync.dma_start(pos_t[1][:], pos2)
-        load_w2_scales(1)
-        load_w2(6, 10, 2, 4)
-        load_w2(0, 4, 3, 4)
-        load_w2(4, 6, 3, 4)
-        for g, (j0, j1) in enumerate(TOKEN_GROUPS):
-            nc.sync.dma_start(out=a_t[g][:], in_=a_src[:, :, P * j0 : P * j1])
-        nc.sync.dma_start(out=w1[:].bitcast(I32), in_=w1t_words[0].bitcast(I32))
-        for r in range(4):
-            nc.sync.dma_start(out=w1s[r:P:32, :].bitcast(I32), in_=w1s_src[r].bitcast(I32))
+        load_w2(0, 3, 0, 4)
 
         gw = {}
 
@@ -146,10 +132,24 @@ def tile_moe_sub_relu2_kernel(
         spread_gate(banks[7], banks[4:6], banks[6])
 
         gather_words(0, 0, 3, gw_early[:])
-        gs[0] = keep.tile([P, S], U8, name="gs0", tag="after_gate_rows", align_bytes=64)
+        gs[0] = keep.tile([P, S], U8, name="gs0", align_bytes=64)
         nc.vector.tensor_copy(gs[0][:], dys[:].indirect(offs_t[:]))
         for s in range(1, PASSES):
-            nc.scalar.dma_start(out=gs[s][0:SHIFT_ROWS, :].bitcast(I32), in_=gs[0][4 * s : 4 * s + SHIFT_ROWS, :].bitcast(I32))
+            nc.sync.dma_start(out=gs[s][0:SHIFT_ROWS, :].bitcast(I32), in_=gs[0][4 * s : 4 * s + SHIFT_ROWS, :].bitcast(I32))
+        load_w2(3, 6, 0, 2)
+        load_w2(6, 9, 0, 2)
+        load_w2(9, 10, 0, 2)
+        nc.sync.dma_start(pos_t[0][:], pos1)
+        nc.sync.dma_start(pos_t[1][:], pos2)
+        load_w2_scales(1)
+        load_w2(3, 6, 2, 4)
+        load_w2(6, 8, 2, 4)
+        load_w2(8, 10, 2, 4)
+        for g, (j0, j1) in enumerate(TOKEN_GROUPS):
+            nc.sync.dma_start(out=a_t[g][:], in_=a_src[:, :, P * j0 : P * j1])
+        nc.sync.dma_start(out=w1[:].bitcast(I32), in_=w1t_words[0].bitcast(I32))
+        for r in range(4):
+            nc.sync.dma_start(out=w1s[r:P:32, :].bitcast(I32), in_=w1s_src[r].bitcast(I32))
         gw_late = keep.tile([P, PASSES * S - EARLY_SLOTS], I32, name="gw_late", tag="after_bytes", align_bytes=64)
         filled = 0
         for e0, e1 in ((0, 3), (3, 6), (6, 9), (9, 10)):
@@ -189,11 +189,11 @@ def tile_moe_sub_relu2_kernel(
             for r in range(2):
                 nc.tensor.matmul(out=place, lhsT=picked[r, c, j], rhs=ident[:], is_transpose=True, start=(r == 0), stop=(r == 1))
 
-        def turn_last(bank):
-            for c in (2, 3):
-                add_turned(c, BLOCKS - 1, bank[:, P * (c - 2) : P * (c - 1)])
+        def turn_last(c0, bank):
+            for c in (c0, c0 + 1):
+                add_turned(c, BLOCKS - 1, bank[:, P * (c - c0) : P * (c - c0 + 1)])
             nc.scalar.copy(
-                out=dh_t[:, BLOCKS - 1, :, 64:P],
+                out=dh_t[:, BLOCKS - 1, :, 32 * c0 : 32 * (c0 + 2)],
                 in_=bank[:, 0 : 2 * P].rearrange("p (m t) -> p t m", t=4),
             )
 
@@ -260,24 +260,25 @@ def tile_moe_sub_relu2_kernel(
         experts(1, 9, 10, banks[6])
 
         pick(0, 0, BLOCKS)
-        experts(2, 0, 4, banks[0])
-        experts(2, 4, 6, banks[1])
-        turn(0, 0, 4, banks[0])
-        turn(0, 4, BLOCKS, banks[1])
         pick(1, 0, BLOCKS)
-        experts(2, 6, 10, banks[2])
-        experts(3, 6, 10, banks[3])
-        experts(3, 0, 4, banks[4])
-        experts(3, 4, 5, banks[5])
-        experts(3, 5, 6, banks[6])
-        turn(1, 4, BLOCKS, banks[4])
-        turn(1, 0, 4, banks[5])
+        experts(2, 0, 3, banks[0])
+        experts(3, 0, 3, banks[1])
+        experts(2, 3, 6, banks[2])
+        experts(3, 3, 6, banks[3])
+        experts(2, 6, 8, banks[4])
+        experts(3, 6, 8, banks[7])
+        experts(2, 8, 10, banks[0])
+        experts(3, 8, 9, banks[5])
+        experts(3, 9, 10, banks[6])
+        turn(0, 0, 4, banks[5])
+        turn(1, 0, 4, banks[0])
+        turn_last(0, banks[6])
         pick(2, 0, 4)
-        turn(2, 0, 4, banks[6])
+        turn(2, 0, 4, banks[1])
         make_slope(0)
         pick(3, 0, 2)
         turn(3, 0, 2, banks[7])
-        back = [banks[0], banks[1], banks[3], banks[4], banks[5]]
+        back = [banks[2], banks[3], banks[4], banks[5], banks[0]]
         turn_back(0, back[0])
         turn_back(1, back[1])
         make_slope(1)
@@ -286,7 +287,7 @@ def tile_moe_sub_relu2_kernel(
         pick(3, 4, BLOCKS)
         pick(2, 4, BLOCKS, tag="picked3_0")
         make_da(0, back[0])
-        turn_last(back[0])
+        turn_last(2, back[0])
         make_slope(2)
         make_da(1, back[1])
         quantize(0)
@@ -299,5 +300,5 @@ def tile_moe_sub_relu2_kernel(
         quantize(1)
         make_da(4, back[4])
         quantize(2)
-        finish(1, [banks[2], banks[6]])
+        finish(1, [banks[1], banks[6]])
         finish(2, [back[1], back[2]])

@@ -25,7 +25,7 @@ RELU = mybir.ActivationFunctionType.Relu
 
 BYTE_WINDOW = 1792
 SHIFT_ROWS = 112
-EARLY_SLOTS = 3 * C
+SCALE_GROUPS = [(0, 8), (8, 16), (16, 24), (24, 30)]
 TOKEN_GROUPS = [(0, 2), (2, 4), (4, 5)]
 
 
@@ -39,13 +39,10 @@ def tile_moe_sub_relu2_kernel(
 
         offs_t = keep.tile([P, S // 16], U16, name="offs_t")
         pos_t = [keep.tile([P, T // 16], U16, name="pos%d_t" % r) for r in range(2)]
-        dyw_first = keep.tile([P, T], I32, name="dyw_first", align_bytes=64)
-        dyw_rest = keep.tile([P, PASSES - 1, T], I32, name="dyw_rest", align_bytes=64)
-        dyw = [dyw_first[:]] + [dyw_rest[:, s, :] for s in range(PASSES - 1)]
+        dyw = keep.tile([P, PASSES, T], I32, name="dyw", align_bytes=64)
         dys = keep.tile([P, BYTE_WINDOW], U8, name="dys", tag="after_bytes", align_bytes=64)
-        gw_early = keep.tile([P, EARLY_SLOTS], I32, name="gw_early", align_bytes=64)
         gs = {s: keep.tile([P, S], U8, name="gs%d" % s, align_bytes=64) for s in range(1, PASSES)}
-        w2s = [keep.tile([P, E * PASSES, 2 * P], U8, name="w2s%d" % h, align_bytes=64) for h in range(2)]
+        w2s = [keep.tile([P, m1 - m0, H], U8, name="w2s%d" % m0, align_bytes=64) for m0, m1 in SCALE_GROUPS]
         w1 = keep.tile([P, 2 * K], U8, name="w1", align_bytes=64)
         w1s = keep.tile([P, K], U8, name="w1s", align_bytes=64)
         gate_rows = keep.tile([P, P], F32, name="gate_rows")
@@ -71,7 +68,8 @@ def tile_moe_sub_relu2_kernel(
         nc.vector.memset(dys[:, T:BYTE_WINDOW].bitcast(I32), 0)
         for s in range(1, PASSES):
             nc.vector.memset(gs[s][:].bitcast(I32), 0)
-        nc.vector.memset(w2s[1][:].rearrange("p a b -> p (a b)").bitcast(I32), 0)
+        for room in w2s[1:]:
+            nc.vector.memset(room[:].rearrange("p a b -> p (a b)").bitcast(I32), 0)
         nc.vector.memset(w1s[:].bitcast(I32), 0)
 
         dyw_src = dy_words.rearrange("s p t d -> p s (t d)").bitcast(I32)
@@ -93,27 +91,24 @@ def tile_moe_sub_relu2_kernel(
                     for s in range(PASSES):
                         w2[e, c, s] = piece[:, PASSES * (e - e0) + s, 2 * P * (c - c0) : 2 * P * (c - c0 + 1)]
 
-        def load_w2_scales(h):
+        def load_w2_scales(g):
+            m0, m1 = SCALE_GROUPS[g]
             for r in range(4):
-                nc.sync.dma_start(
-                    out=w2s[h][r:P:32, :, :].bitcast(I32),
-                    in_=w2s_src[r][:, :, 2 * P * h : 2 * P * (h + 1)].bitcast(I32),
-                )
+                nc.sync.dma_start(out=w2s[g][r:P:32, :, :].bitcast(I32), in_=w2s_src[r][:, m0:m1, :].bitcast(I32))
 
-        nc.sync.dma_start(out=dyw[0], in_=dyw_src[:, 0, :])
+        nc.sync.dma_start(out=dyw[:], in_=dyw_src)
         nc.sync.dma_start(offs_t[:], offs)
         nc.scalar.dma_start(out=gate_rows[0 : 2 * BLOCKS, :], in_=gate[:, 0, :].rearrange("r (j u) -> r j u", u=P))
-        nc.sync.dma_start(out=dyw_rest[:], in_=dyw_src[:, 1:PASSES, :])
         for q in range(4):
             queue = nc.sync if q < 2 else nc.scalar
             queue.dma_start(out=dys[32 * q : 32 * q + 4 * PASSES, 0:T].bitcast(I32), in_=dys_src[q].bitcast(I32))
-        load_w2_scales(0)
-        load_w2(0, 3, 0, 4)
+        for g in range(len(SCALE_GROUPS)):
+            load_w2_scales(g)
 
         gw = {}
 
         def gather_words(s, e0, e1, room):
-            nc.vector.tensor_copy(room.bitcast(U32), dyw[s].bitcast(U32).indirect(offs_t[:, C * e0 // 16 : C * e1 // 16]))
+            nc.vector.tensor_copy(room.bitcast(U32), dyw[:, s, :].bitcast(U32).indirect(offs_t[:, C * e0 // 16 : C * e1 // 16]))
             for e in range(e0, e1):
                 gw[s, e] = room[:, C * (e - e0) : C * (e - e0 + 1)]
 
@@ -131,17 +126,17 @@ def tile_moe_sub_relu2_kernel(
 
         spread_gate(banks[7], banks[4:6], banks[6])
 
-        gather_words(0, 0, 3, gw_early[:])
         gs[0] = keep.tile([P, S], U8, name="gs0", align_bytes=64)
         nc.vector.tensor_copy(gs[0][:], dys[:].indirect(offs_t[:]))
         for s in range(1, PASSES):
             nc.sync.dma_start(out=gs[s][0:SHIFT_ROWS, :].bitcast(I32), in_=gs[0][4 * s : 4 * s + SHIFT_ROWS, :].bitcast(I32))
+        nc.sync.dma_start(pos_t[0][:], pos1)
+        nc.sync.dma_start(pos_t[1][:], pos2)
+        load_w2(0, 3, 0, 2)
         load_w2(3, 6, 0, 2)
         load_w2(6, 9, 0, 2)
         load_w2(9, 10, 0, 2)
-        nc.sync.dma_start(pos_t[0][:], pos1)
-        nc.sync.dma_start(pos_t[1][:], pos2)
-        load_w2_scales(1)
+        load_w2(0, 3, 2, 4)
         load_w2(3, 6, 2, 4)
         load_w2(6, 8, 2, 4)
         load_w2(8, 10, 2, 4)
@@ -150,13 +145,10 @@ def tile_moe_sub_relu2_kernel(
         nc.sync.dma_start(out=w1[:].bitcast(I32), in_=w1t_words[0].bitcast(I32))
         for r in range(4):
             nc.sync.dma_start(out=w1s[r:P:32, :].bitcast(I32), in_=w1s_src[r].bitcast(I32))
-        gw_late = keep.tile([P, PASSES * S - EARLY_SLOTS], I32, name="gw_late", tag="after_bytes", align_bytes=64)
-        filled = 0
+        gw_all = keep.tile([P, PASSES * S], I32, name="gw_all", tag="after_bytes", align_bytes=64)
         for e0, e1 in ((0, 3), (3, 6), (6, 9), (9, 10)):
             for s in range(PASSES):
-                if (s, e0) not in gw:
-                    gather_words(s, e0, e1, gw_late[:, filled : filled + C * (e1 - e0)])
-                    filled = filled + C * (e1 - e0)
+                gather_words(s, e0, e1, gw_all[:, S * s + C * e0 : S * s + C * e1])
 
         def experts(c, e0, e1, bank):
             for e in range(e0, e1):
@@ -164,7 +156,7 @@ def tile_moe_sub_relu2_kernel(
                     nc.tensor.matmul_mx(
                         out=bank[:, C * (e - e0) : C * (e - e0 + 1)],
                         lhsT=w2[e, c, s].bitcast(FP4X4),
-                        lhsT_scale=w2s[c // 2][:, PASSES * e + s, P * (c % 2) : P * (c % 2 + 1)],
+                        lhsT_scale=w2s[(PASSES * e + s) // 8][:, (PASSES * e + s) % 8, P * c : P * (c + 1)],
                         rhs=gw[s, e].bitcast(FP8X4),
                         rhs_scale=gs[s][:, C * e : C * (e + 1)],
                         start=(s == 0),

@@ -150,19 +150,21 @@ def tile_moe_sub_relu2_kernel(
             for s in range(PASSES):
                 gather_words(s, e0, e1, gw_all[:, S * s + C * e0 : S * s + C * e1])
 
-        def experts(c, e0, e1, bank):
+        def experts(c0, e0, e1, pair):
             for e in range(e0, e1):
                 for s in range(PASSES):
-                    nc.tensor.matmul_mx(
-                        out=bank[:, C * (e - e0) : C * (e - e0 + 1)],
-                        lhsT=w2[e, c, s].bitcast(FP4X4),
-                        lhsT_scale=w2s[(PASSES * e + s) // 8][:, (PASSES * e + s) % 8, P * c : P * (c + 1)],
-                        rhs=gw[s, e].bitcast(FP8X4),
-                        rhs_scale=gs[s][:, C * e : C * (e + 1)],
-                        start=(s == 0),
-                        stop=(s == PASSES - 1),
-                    )
-            nc.scalar.copy(out=y[c][:, C * e0 : C * e1], in_=bank[:, 0 : C * (e1 - e0)])
+                    for c in (c0, c0 + 1):
+                        nc.tensor.matmul_mx(
+                            out=pair[c - c0][:, C * (e - e0) : C * (e - e0 + 1)],
+                            lhsT=w2[e, c, s].bitcast(FP4X4),
+                            lhsT_scale=w2s[(PASSES * e + s) // 8][:, (PASSES * e + s) % 8, P * c : P * (c + 1)],
+                            rhs=gw[s, e].bitcast(FP8X4),
+                            rhs_scale=gs[s][:, C * e : C * (e + 1)],
+                            start=(s == 0),
+                            stop=(s == PASSES - 1),
+                        )
+            for c in (c0, c0 + 1):
+                nc.scalar.copy(out=y[c][:, C * e0 : C * e1], in_=pair[c - c0][:, 0 : C * (e1 - e0)])
 
         def make_slope(g):
             nc.scalar.activation(out=slope[g][:], in_=a_t[g][:].rearrange("p t n -> p n t"), func=RELU, scale=2.0)
@@ -177,21 +179,27 @@ def tile_moe_sub_relu2_kernel(
                 for j in range(j0, j1):
                     picked[r, c, j] = room[:, r, P * (j - j0) : P * (j - j0 + 1)]
 
-        def add_turned(c, j, place):
+        def add_turned(pieces, bank):
             for r in range(2):
-                nc.tensor.matmul(out=place, lhsT=picked[r, c, j], rhs=ident[:], is_transpose=True, start=(r == 0), stop=(r == 1))
+                for n, (c, j) in enumerate(pieces):
+                    nc.tensor.matmul(
+                        out=bank[:, P * n : P * (n + 1)],
+                        lhsT=picked[r, c, j],
+                        rhs=ident[:],
+                        is_transpose=True,
+                        start=(r == 0 and n == 0),
+                        stop=(r == 1 and n == len(pieces) - 1),
+                    )
 
         def turn_last(c0, bank):
-            for c in (c0, c0 + 1):
-                add_turned(c, BLOCKS - 1, bank[:, P * (c - c0) : P * (c - c0 + 1)])
+            add_turned([(c0, BLOCKS - 1), (c0 + 1, BLOCKS - 1)], bank)
             nc.scalar.copy(
                 out=dh_t[:, BLOCKS - 1, :, 32 * c0 : 32 * (c0 + 2)],
                 in_=bank[:, 0 : 2 * P].rearrange("p (m t) -> p t m", t=4),
             )
 
         def turn(c, j0, j1, bank):
-            for j in range(j0, j1):
-                add_turned(c, j, bank[:, P * (j - j0) : P * (j - j0 + 1)])
+            add_turned([(c, j) for j in range(j0, j1)], bank)
             nc.scalar.copy(
                 out=dh_t[:, j0:j1, :, 32 * c : 32 * (c + 1)],
                 in_=bank[:, 0 : P * (j1 - j0)].rearrange("p (j m t) -> p j t m", m=32, t=4),
@@ -242,26 +250,18 @@ def tile_moe_sub_relu2_kernel(
                     nc.scalar.copy(out=dst, in_=src)
                 nc.sync.dma_start(out=out_view[:, 2 * half : 2 * half + 2, t0:t1], in_=dst)
 
-        experts(0, 0, 3, banks[0])
-        experts(1, 0, 3, banks[1])
-        experts(0, 3, 6, banks[2])
-        experts(1, 3, 6, banks[3])
-        experts(0, 6, 9, banks[4])
-        experts(0, 9, 10, banks[5])
-        experts(1, 6, 9, banks[5])
-        experts(1, 9, 10, banks[6])
+        experts(0, 0, 3, banks[0:2])
+        experts(0, 3, 6, banks[2:4])
+        experts(0, 6, 9, banks[4:6])
+        experts(0, 9, 10, banks[6:8])
 
         pick(0, 0, BLOCKS)
         pick(1, 0, BLOCKS)
-        experts(2, 0, 3, banks[0])
-        experts(3, 0, 3, banks[1])
-        experts(2, 3, 6, banks[2])
-        experts(3, 3, 6, banks[3])
-        experts(2, 6, 8, banks[4])
-        experts(3, 6, 8, banks[7])
-        experts(2, 8, 10, banks[0])
-        experts(3, 8, 9, banks[5])
-        experts(3, 9, 10, banks[6])
+        experts(2, 0, 3, banks[0:2])
+        experts(2, 3, 6, banks[2:4])
+        experts(2, 6, 8, [banks[4], banks[7]])
+        experts(2, 8, 9, [banks[0], banks[5]])
+        experts(2, 9, 10, [banks[1], banks[6]])
         turn(0, 0, 4, banks[5])
         turn(1, 0, 4, banks[0])
         turn_last(0, banks[6])

@@ -25,7 +25,7 @@ RELU = mybir.ActivationFunctionType.Relu
 
 BYTE_WINDOW = 1792
 SHIFT_ROWS = 112
-SCALE_GROUPS = [(0, 8), (8, 16), (16, 24), (24, 30)]
+SCALE_GROUPS = [(0, 5, 0), (5, 10, 0), (0, 5, 2), (5, 10, 2)]
 TOKEN_GROUPS = [(0, 2), (2, 4), (4, 5)]
 
 
@@ -42,13 +42,13 @@ def tile_moe_sub_relu2_kernel(
         dyw = keep.tile([P, PASSES, T], I32, name="dyw", align_bytes=64)
         dys = keep.tile([P, BYTE_WINDOW], U8, name="dys", tag="after_bytes", align_bytes=64)
         gs = {s: keep.tile([P, S], U8, name="gs%d" % s, align_bytes=64) for s in range(1, PASSES)}
-        w2s = [keep.tile([P, m1 - m0, H], U8, name="w2s%d" % m0, align_bytes=64) for m0, m1 in SCALE_GROUPS]
+        w2s = [keep.tile([P, PASSES * (e1 - e0), 2 * P], U8, name="w2s%d_%d" % (e0, c0), align_bytes=64) for e0, e1, c0 in SCALE_GROUPS]
         w1 = keep.tile([P, 2 * K], U8, name="w1", align_bytes=64)
         w1s = keep.tile([P, K], U8, name="w1s", align_bytes=64)
         gate_rows = keep.tile([P, P], F32, name="gate_rows")
         gate_cols = keep.tile([P, 2 * BLOCKS], F32, name="gate_cols")
         gate_t = [keep.tile([P, T], F32, name="gate%d" % r) for r in range(2)]
-        a_t = [keep.tile([P, 4, P * (j1 - j0)], F32, name="a%d" % j0) for j0, j1 in TOKEN_GROUPS]
+        a_t = keep.tile([P, 4, T], F32, name="a_t")
         slope = [keep.tile([P, P * (j1 - j0), 4], F32, name="slope%d" % j0) for j0, j1 in TOKEN_GROUPS]
         ident = keep.tile([P, P], F32, name="ident")
         y = [keep.tile([P, S], F32, name="y%d" % c)[:] for c in range(CHUNKS)]
@@ -64,21 +64,22 @@ def tile_moe_sub_relu2_kernel(
         nc.vector.memset(dys[:, 0:T].bitcast(I32), 0)
         nc.gpsimd.memset(gate_rows[:], 0.0)
         make_identity(nc, ident[:])
-        nc.vector.memset(w2s[0][:].rearrange("p a b -> p (a b)").bitcast(I32), 0)
+        for room in w2s[0:2]:
+            nc.vector.memset(room[:].rearrange("p a b -> p (a b)").bitcast(I32), 0)
         nc.vector.memset(dys[:, T:BYTE_WINDOW].bitcast(I32), 0)
         for s in range(1, PASSES):
-            nc.vector.memset(gs[s][:].bitcast(I32), 0)
-        for room in w2s[1:]:
-            nc.vector.memset(room[:].rearrange("p a b -> p (a b)").bitcast(I32), 0)
-        nc.vector.memset(w1s[:].bitcast(I32), 0)
+            nc.gpsimd.memset(gs[s][:].bitcast(I32), 0)
+        for room in w2s[2:]:
+            nc.gpsimd.memset(room[:].rearrange("p a b -> p (a b)").bitcast(I32), 0)
+        nc.gpsimd.memset(w1s[:].bitcast(I32), 0)
 
         dyw_src = dy_words.rearrange("s p t d -> p s (t d)").bitcast(I32)
         dys_src = dy_scales.rearrange("s (q r) t -> q s r t", r=4)
         w2_src = w2t_words.rearrange("e s p b -> p (e s) b")
         w2s_src = w2t_scales.rearrange("e s (q r) n -> r q (e s) n", r=4)
-        a_src = a.rearrange("(p t) n -> p t n", t=4)
         w1s_src = w1t_scales[0].rearrange("(q r) n -> r q n", r=4)
         w2 = {}
+        w2_scale = {}
 
         def load_w2(e0, e1, c0, c1):
             piece = keep.tile([P, (e1 - e0) * PASSES, 2 * P * (c1 - c0)], U8, name="w2_%d_%d" % (e0, c0), align_bytes=64)
@@ -92,18 +93,28 @@ def tile_moe_sub_relu2_kernel(
                         w2[e, c, s] = piece[:, PASSES * (e - e0) + s, 2 * P * (c - c0) : 2 * P * (c - c0 + 1)]
 
         def load_w2_scales(g):
-            m0, m1 = SCALE_GROUPS[g]
+            e0, e1, c0 = SCALE_GROUPS[g]
             for r in range(4):
-                nc.sync.dma_start(out=w2s[g][r:P:32, :, :].bitcast(I32), in_=w2s_src[r][:, m0:m1, :].bitcast(I32))
+                nc.sync.dma_start(
+                    out=w2s[g][r:P:32, :, :].bitcast(I32),
+                    in_=w2s_src[r][:, PASSES * e0 : PASSES * e1, P * c0 : P * (c0 + 2)].bitcast(I32),
+                )
+            for e in range(e0, e1):
+                for s in range(PASSES):
+                    for c in (c0, c0 + 1):
+                        w2_scale[e, c, s] = w2s[g][:, PASSES * (e - e0) + s, P * (c - c0) : P * (c - c0 + 1)]
 
         nc.sync.dma_start(out=dyw[:], in_=dyw_src)
         nc.sync.dma_start(offs_t[:], offs)
-        nc.scalar.dma_start(out=gate_rows[0 : 2 * BLOCKS, :], in_=gate[:, 0, :].rearrange("r (j u) -> r j u", u=P))
         for q in range(4):
             queue = nc.sync if q < 2 else nc.scalar
             queue.dma_start(out=dys[32 * q : 32 * q + 4 * PASSES, 0:T].bitcast(I32), in_=dys_src[q].bitcast(I32))
-        for g in range(len(SCALE_GROUPS)):
-            load_w2_scales(g)
+        nc.scalar.dma_start(out=gate_rows[0 : 2 * BLOCKS, :], in_=gate[:, 0, :].rearrange("r (j u) -> r j u", u=P))
+        load_w2_scales(0)
+        load_w2_scales(1)
+        nc.sync.dma_start(pos_t[0][:], pos1)
+        nc.sync.dma_start(pos_t[1][:], pos2)
+        load_w2(0, 3, 0, CHUNKS)
 
         gw = {}
 
@@ -130,44 +141,39 @@ def tile_moe_sub_relu2_kernel(
         nc.vector.tensor_copy(gs[0][:], dys[:].indirect(offs_t[:]))
         for s in range(1, PASSES):
             nc.sync.dma_start(out=gs[s][0:SHIFT_ROWS, :].bitcast(I32), in_=gs[0][4 * s : 4 * s + SHIFT_ROWS, :].bitcast(I32))
-        nc.sync.dma_start(pos_t[0][:], pos1)
-        nc.sync.dma_start(pos_t[1][:], pos2)
-        load_w2(0, 3, 0, 2)
-        load_w2(3, 6, 0, 2)
-        load_w2(6, 9, 0, 2)
-        load_w2(9, 10, 0, 2)
-        load_w2(0, 3, 2, 4)
-        load_w2(3, 6, 2, 4)
+        load_w2(3, 6, 0, CHUNKS)
+        load_w2(6, 8, 0, 2)
+        load_w2(8, 10, 0, 2)
+        load_w2_scales(2)
+        load_w2_scales(3)
         load_w2(6, 8, 2, 4)
         load_w2(8, 10, 2, 4)
-        for g, (j0, j1) in enumerate(TOKEN_GROUPS):
-            nc.sync.dma_start(out=a_t[g][:], in_=a_src[:, :, P * j0 : P * j1])
+        nc.sync.dma_start(out=a_t[:], in_=a.rearrange("(p t) n -> p t n", t=4))
         nc.sync.dma_start(out=w1[:].bitcast(I32), in_=w1t_words[0].bitcast(I32))
         for r in range(4):
             nc.sync.dma_start(out=w1s[r:P:32, :].bitcast(I32), in_=w1s_src[r].bitcast(I32))
         gw_all = keep.tile([P, PASSES * S], I32, name="gw_all", tag="after_bytes", align_bytes=64)
-        for e0, e1 in ((0, 3), (3, 6), (6, 9), (9, 10)):
+        for e0, e1 in ((0, 3), (3, 6), (6, 8), (8, 10)):
             for s in range(PASSES):
                 gather_words(s, e0, e1, gw_all[:, S * s + C * e0 : S * s + C * e1])
 
-        def experts(c0, e0, e1, pair):
+        def experts(c, e0, e1, bank):
             for e in range(e0, e1):
                 for s in range(PASSES):
-                    for c in (c0, c0 + 1):
-                        nc.tensor.matmul_mx(
-                            out=pair[c - c0][:, C * (e - e0) : C * (e - e0 + 1)],
-                            lhsT=w2[e, c, s].bitcast(FP4X4),
-                            lhsT_scale=w2s[(PASSES * e + s) // 8][:, (PASSES * e + s) % 8, P * c : P * (c + 1)],
-                            rhs=gw[s, e].bitcast(FP8X4),
-                            rhs_scale=gs[s][:, C * e : C * (e + 1)],
-                            start=(s == 0),
-                            stop=(s == PASSES - 1),
-                        )
-            for c in (c0, c0 + 1):
-                nc.scalar.copy(out=y[c][:, C * e0 : C * e1], in_=pair[c - c0][:, 0 : C * (e1 - e0)])
+                    nc.tensor.matmul_mx(
+                        out=bank[:, C * (e - e0) : C * (e - e0 + 1)],
+                        lhsT=w2[e, c, s].bitcast(FP4X4),
+                        lhsT_scale=w2_scale[e, c, s],
+                        rhs=gw[s, e].bitcast(FP8X4),
+                        rhs_scale=gs[s][:, C * e : C * (e + 1)],
+                        start=(s == 0),
+                        stop=(s == PASSES - 1),
+                    )
+            nc.scalar.copy(out=y[c][:, C * e0 : C * e1], in_=bank[:, 0 : C * (e1 - e0)])
 
         def make_slope(g):
-            nc.scalar.activation(out=slope[g][:], in_=a_t[g][:].rearrange("p t n -> p n t"), func=RELU, scale=2.0)
+            j0, j1 = TOKEN_GROUPS[g]
+            nc.scalar.activation(out=slope[g][:], in_=a_t[:, :, P * j0 : P * j1].rearrange("p t n -> p n t"), func=RELU, scale=2.0)
 
         def pick(c, j0, j1, tag=None):
             name = "picked%d_%d" % (c, j0)
@@ -250,32 +256,39 @@ def tile_moe_sub_relu2_kernel(
                     nc.scalar.copy(out=dst, in_=src)
                 nc.sync.dma_start(out=out_view[:, 2 * half : 2 * half + 2, t0:t1], in_=dst)
 
-        experts(0, 0, 3, banks[0:2])
-        experts(0, 3, 6, banks[2:4])
-        experts(0, 6, 9, banks[4:6])
-        experts(0, 9, 10, banks[6:8])
+        experts(0, 0, 3, banks[0])
+        experts(1, 0, 3, banks[1])
+        experts(0, 3, 6, banks[2])
+        experts(1, 3, 6, banks[3])
+        experts(0, 6, 8, banks[4])
+        experts(0, 8, 10, banks[5])
+        experts(1, 6, 8, banks[5])
+        experts(1, 8, 10, banks[6])
 
         pick(0, 0, BLOCKS)
         pick(1, 0, BLOCKS)
-        experts(2, 0, 3, banks[0:2])
-        experts(2, 3, 6, banks[2:4])
-        experts(2, 6, 8, [banks[4], banks[7]])
-        experts(2, 8, 9, [banks[0], banks[5]])
-        experts(2, 9, 10, [banks[1], banks[6]])
-        turn(0, 0, 4, banks[5])
-        turn(1, 0, 4, banks[0])
-        turn_last(0, banks[6])
+        experts(2, 0, 3, banks[0])
+        experts(2, 3, 6, banks[1])
+        experts(2, 6, 8, banks[3])
+        experts(2, 8, 10, banks[7])
+        experts(3, 0, 3, banks[2])
+        experts(3, 3, 6, banks[4])
+        experts(3, 6, 8, banks[5])
+        experts(3, 8, 10, banks[6])
+        turn(0, 0, 4, banks[6])
+        turn(1, 0, 4, banks[7])
+        turn_last(0, banks[7])
         pick(2, 0, 4)
-        turn(2, 0, 4, banks[1])
+        turn(2, 0, 4, banks[0])
         make_slope(0)
         pick(3, 0, 2)
-        turn(3, 0, 2, banks[7])
-        back = [banks[2], banks[3], banks[4], banks[5], banks[0]]
+        turn(3, 0, 2, banks[1])
+        back = [banks[2], banks[3], banks[4], banks[5], banks[6]]
         turn_back(0, back[0])
         turn_back(1, back[1])
         make_slope(1)
         pick(3, 2, 4)
-        turn(3, 2, 4, banks[7])
+        turn(3, 2, 4, banks[1])
         pick(3, 4, BLOCKS)
         pick(2, 4, BLOCKS, tag="picked3_0")
         make_da(0, back[0])
@@ -286,11 +299,11 @@ def tile_moe_sub_relu2_kernel(
         turn_back(2, back[2])
         turn_back(3, back[3])
         turn_back(4, back[4])
-        finish(0, [back[0], banks[7]])
+        finish(0, [back[0], banks[1]])
         make_da(2, back[2])
         make_da(3, back[3])
         quantize(1)
         make_da(4, back[4])
         quantize(2)
-        finish(1, [banks[1], banks[6]])
+        finish(1, [banks[0], banks[7]])
         finish(2, [back[1], back[2]])

@@ -49,7 +49,7 @@ def tile_moe_sub_relu2_kernel(
         gate_cols = keep.tile([P, 2 * BLOCKS], F32, name="gate_cols")
         gate_t = [keep.tile([P, T], F32, name="gate%d" % r) for r in range(2)]
         a_t = keep.tile([P, 4, T], F32, name="a_t")
-        slope = [keep.tile([P, P * (j1 - j0), 4], F32, name="slope%d" % j0) for j0, j1 in TOKEN_GROUPS]
+        slope = {}
         ident = keep.tile([P, P], F32, name="ident")
         y = [keep.tile([P, S], F32, name="y%d" % c)[:] for c in range(CHUNKS)]
         picked = {}
@@ -104,14 +104,14 @@ def tile_moe_sub_relu2_kernel(
                     for c in (c0, c0 + 1):
                         w2_scale[e, c, s] = w2s[g][:, PASSES * (e - e0) + s, P * (c - c0) : P * (c - c0 + 1)]
 
-        nc.sync.dma_start(out=dyw[:], in_=dyw_src)
         nc.sync.dma_start(offs_t[:], offs)
+        nc.sync.dma_start(out=dyw[:], in_=dyw_src)
         for q in range(4):
             queue = nc.sync if q < 2 else nc.scalar
             queue.dma_start(out=dys[32 * q : 32 * q + 4 * PASSES, 0:T].bitcast(I32), in_=dys_src[q].bitcast(I32))
-        nc.scalar.dma_start(out=gate_rows[0 : 2 * BLOCKS, :], in_=gate[:, 0, :].rearrange("r (j u) -> r j u", u=P))
         load_w2_scales(0)
         load_w2_scales(1)
+        nc.sync.dma_start(out=gate_rows[0 : 2 * BLOCKS, :], in_=gate[:, 0, :].rearrange("r (j u) -> r j u", u=P))
         nc.sync.dma_start(pos_t[0][:], pos1)
         nc.sync.dma_start(pos_t[1][:], pos2)
         load_w2(0, 3, 0, CHUNKS)
@@ -171,9 +171,13 @@ def tile_moe_sub_relu2_kernel(
                     )
             nc.scalar.copy(out=y[c][:, C * e0 : C * e1], in_=bank[:, 0 : C * (e1 - e0)])
 
-        def make_slope(g):
-            j0, j1 = TOKEN_GROUPS[g]
-            nc.scalar.activation(out=slope[g][:], in_=a_t[:, :, P * j0 : P * j1].rearrange("p t n -> p n t"), func=RELU, scale=2.0)
+        def slope_room(j0, j1, tag):
+            room = keep.tile([P, P * (j1 - j0), 4], F32, name="slope%d" % j0, tag=tag)
+            for j in range(j0, j1):
+                slope[j] = room[:, P * (j - j0) : P * (j - j0 + 1), :]
+
+        def make_slope(j):
+            nc.scalar.activation(out=slope[j], in_=a_t[:, :, P * j : P * (j + 1)].rearrange("p t n -> p n t"), func=RELU, scale=2.0)
 
         def pick(c, j0, j1, tag=None):
             name = "picked%d_%d" % (c, j0)
@@ -219,7 +223,7 @@ def tile_moe_sub_relu2_kernel(
             nc.vector.tensor_tensor(
                 da[:, P * j : P * (j + 1), :],
                 bank[:].rearrange("p (t n) -> p n t", t=4),
-                slope[j // 2][:, P * (j % 2) : P * (j % 2 + 1), :],
+                slope[j],
                 MULT,
             )
 
@@ -278,32 +282,37 @@ def tile_moe_sub_relu2_kernel(
         turn(0, 0, 4, banks[6])
         turn(1, 0, 4, banks[7])
         turn_last(0, banks[7])
+        slope_room(0, 1, "picked1_0")
+        make_slope(0)
         pick(2, 0, 4)
         turn(2, 0, 4, banks[0])
-        make_slope(0)
         pick(3, 0, 2)
         turn(3, 0, 2, banks[1])
+        pick(3, 2, 4)
+        turn(3, 2, 4, banks[0])
+        slope_room(1, 3, "picked3_2")
+        make_slope(1)
+        make_slope(2)
         back = [banks[2], banks[3], banks[4], banks[5], banks[6]]
         turn_back(0, back[0])
         turn_back(1, back[1])
-        make_slope(1)
-        pick(3, 2, 4)
-        turn(3, 2, 4, banks[1])
         pick(3, 4, BLOCKS)
-        pick(2, 4, BLOCKS, tag="picked3_0")
+        pick(2, 4, BLOCKS, tag="picked2_0")
+        turn_last(2, banks[1])
+        slope_room(3, BLOCKS, "picked3_4")
+        make_slope(3)
+        make_slope(4)
         make_da(0, back[0])
-        turn_last(2, back[0])
-        make_slope(2)
         make_da(1, back[1])
         quantize(0)
         turn_back(2, back[2])
         turn_back(3, back[3])
         turn_back(4, back[4])
-        finish(0, [back[0], banks[1]])
+        finish(0, [banks[1], banks[0]])
         make_da(2, back[2])
         make_da(3, back[3])
         quantize(1)
         make_da(4, back[4])
         quantize(2)
-        finish(1, [banks[0], banks[7]])
+        finish(1, [back[0], banks[7]])
         finish(2, [back[1], back[2]])

@@ -23,9 +23,9 @@ FP4X4 = mybir.dt.float4_e2m1fn_x4
 MULT = mybir.AluOpType.mult
 RELU = mybir.ActivationFunctionType.Relu
 
-BYTE_WINDOW = 1792
+BYTE_PIECES = [[(0, 384)], [(384, 832), (832, 1280)]]
 SHIFT_ROWS = 112
-SCALE_GROUPS = [(0, 5, 0), (5, 10, 0), (0, 5, 2), (5, 10, 2)]
+SCALE_GROUPS = [(0, 5, 0), (5, 10, 0), (0, 4, 2), (4, 7, 2), (7, 10, 2)]
 TOKEN_GROUPS = [(0, 2), (2, 4), (4, 5)]
 
 
@@ -40,8 +40,13 @@ def tile_moe_sub_relu2_kernel(
         offs_t = keep.tile([P, S // 16], U16, name="offs_t")
         pos_t = [keep.tile([P, T // 16], U16, name="pos%d_t" % r) for r in range(2)]
         dyw = keep.tile([P, PASSES, T], I32, name="dyw", align_bytes=64)
-        dys = keep.tile([P, BYTE_WINDOW], U8, name="dys", tag="after_bytes", align_bytes=64)
-        gs = {s: keep.tile([P, S], U8, name="gs%d" % s, align_bytes=64) for s in range(1, PASSES)}
+        dys = keep.tile([P, T], U8, name="dys", tag="after_bytes", align_bytes=64)
+        spans = [(pieces[0][0], pieces[-1][1]) for pieces in BYTE_PIECES]
+        gs = {
+            (s, part): keep.tile([P, j1 - j0], U8, name="gs%d_%d" % (s, part), align_bytes=64)
+            for s in range(PASSES)
+            for part, (j0, j1) in enumerate(spans)
+        }
         w2s = [keep.tile([P, PASSES * (e1 - e0), 2 * P], U8, name="w2s%d_%d" % (e0, c0), align_bytes=64) for e0, e1, c0 in SCALE_GROUPS]
         w1 = keep.tile([P, 2 * K], U8, name="w1", align_bytes=64)
         w1s = keep.tile([P, K], U8, name="w1s", align_bytes=64)
@@ -61,14 +66,14 @@ def tile_moe_sub_relu2_kernel(
 
         banks = [psum.tile([P, 512], F32, name="bank%d" % b) for b in range(8)]
 
-        nc.vector.memset(dys[:, 0:T].bitcast(I32), 0)
+        nc.vector.memset(dys[:].bitcast(I32), 0)
         nc.gpsimd.memset(gate_rows[:], 0.0)
         make_identity(nc, ident[:])
         for room in w2s[0:2]:
             nc.vector.memset(room[:].rearrange("p a b -> p (a b)").bitcast(I32), 0)
-        nc.vector.memset(dys[:, T:BYTE_WINDOW].bitcast(I32), 0)
-        for s in range(1, PASSES):
-            nc.gpsimd.memset(gs[s][:].bitcast(I32), 0)
+        for part in range(len(spans)):
+            for s in range(1, PASSES):
+                nc.gpsimd.memset(gs[s, part][:].bitcast(I32), 0)
         for room in w2s[2:]:
             nc.gpsimd.memset(room[:].rearrange("p a b -> p (a b)").bitcast(I32), 0)
         nc.gpsimd.memset(w1s[:].bitcast(I32), 0)
@@ -108,7 +113,7 @@ def tile_moe_sub_relu2_kernel(
         nc.sync.dma_start(out=dyw[:], in_=dyw_src)
         for q in range(4):
             queue = nc.sync if q < 2 else nc.scalar
-            queue.dma_start(out=dys[32 * q : 32 * q + 4 * PASSES, 0:T].bitcast(I32), in_=dys_src[q].bitcast(I32))
+            queue.dma_start(out=dys[32 * q : 32 * q + 4 * PASSES, :].bitcast(I32), in_=dys_src[q].bitcast(I32))
         load_w2_scales(0)
         load_w2_scales(1)
         nc.sync.dma_start(out=gate_rows[0 : 2 * BLOCKS, :], in_=gate[:, 0, :].rearrange("r (j u) -> r j u", u=P))
@@ -137,15 +142,30 @@ def tile_moe_sub_relu2_kernel(
 
         spread_gate(banks[7], banks[4:6], banks[6])
 
-        gs[0] = keep.tile([P, S], U8, name="gs0", align_bytes=64)
-        nc.vector.tensor_copy(gs[0][:], dys[:].indirect(offs_t[:]))
-        for s in range(1, PASSES):
-            nc.sync.dma_start(out=gs[s][0:SHIFT_ROWS, :].bitcast(I32), in_=gs[0][4 * s : 4 * s + SHIFT_ROWS, :].bitcast(I32))
-        load_w2(3, 6, 0, CHUNKS)
+        for part, pieces in enumerate(BYTE_PIECES):
+            for j0, j1 in pieces:
+                first = spans[part][0]
+                nc.vector.tensor_copy(gs[0, part][:, j0 - first : j1 - first], dys[:].indirect(offs_t[:, j0 // 16 : j1 // 16]))
+
+        def shift_bytes(part):
+            for s in range(1, PASSES):
+                nc.sync.dma_start(
+                    out=gs[s, part][0:SHIFT_ROWS, :].bitcast(I32), in_=gs[0, part][4 * s : 4 * s + SHIFT_ROWS, :].bitcast(I32)
+                )
+
+        def slot_scales(s, e):
+            part = 0 if C * e < spans[0][1] else 1
+            first = C * e - spans[part][0]
+            return gs[s, part][:, first : first + C]
+
+        shift_bytes(0)
+        load_w2(3, 5, 0, CHUNKS)
+        shift_bytes(1)
+        load_w2(5, 6, 0, CHUNKS)
         load_w2(6, 8, 0, 2)
         load_w2(8, 10, 0, 2)
-        load_w2_scales(2)
-        load_w2_scales(3)
+        for g in range(2, len(SCALE_GROUPS)):
+            load_w2_scales(g)
         load_w2(6, 8, 2, 4)
         load_w2(8, 10, 2, 4)
         nc.sync.dma_start(out=a_t[:], in_=a.rearrange("(p t) n -> p t n", t=4))
@@ -158,14 +178,14 @@ def tile_moe_sub_relu2_kernel(
                 gather_words(s, e0, e1, gw_all[:, S * s + C * e0 : S * s + C * e1])
 
         def experts(c, e0, e1, bank):
-            for e in range(e0, e1):
+            for e in reversed(range(e0, e1)) if c == CHUNKS - 1 else range(e0, e1):
                 for s in range(PASSES):
                     nc.tensor.matmul_mx(
                         out=bank[:, C * (e - e0) : C * (e - e0 + 1)],
                         lhsT=w2[e, c, s].bitcast(FP4X4),
                         lhsT_scale=w2_scale[e, c, s],
                         rhs=gw[s, e].bitcast(FP8X4),
-                        rhs_scale=gs[s][:, C * e : C * (e + 1)],
+                        rhs_scale=slot_scales(s, e),
                         start=(s == 0),
                         stop=(s == PASSES - 1),
                     )
@@ -258,7 +278,10 @@ def tile_moe_sub_relu2_kernel(
                     nc.vector.tensor_copy(out=dst, in_=src)
                 else:
                     nc.scalar.copy(out=dst, in_=src)
-                nc.sync.dma_start(out=out_view[:, 2 * half : 2 * half + 2, t0:t1], in_=dst)
+                if g < len(TOKEN_GROUPS) - 1:
+                    nc.sync.dma_start(out=out_view[:, 2 * half : 2 * half + 2, t0:t1], in_=dst)
+            if g == len(TOKEN_GROUPS) - 1:
+                nc.sync.dma_start(out=out_view[:, :, t0:t1], in_=result[:, :, t0:t1])
 
         experts(0, 0, 3, banks[0])
         experts(1, 0, 3, banks[1])
@@ -276,29 +299,28 @@ def tile_moe_sub_relu2_kernel(
         experts(2, 6, 8, banks[3])
         experts(2, 8, 10, banks[7])
         experts(3, 0, 3, banks[2])
-        experts(3, 3, 6, banks[4])
-        experts(3, 6, 8, banks[5])
-        experts(3, 8, 10, banks[6])
+        experts(3, 6, 10, banks[6])
+        experts(3, 3, 6, banks[7])
         turn(0, 0, 4, banks[6])
         turn(1, 0, 4, banks[7])
-        turn_last(0, banks[7])
+        turn_last(0, banks[6])
         slope_room(0, 1, "picked1_0")
         make_slope(0)
         pick(2, 0, 4)
-        turn(2, 0, 4, banks[0])
+        turn(2, 0, 4, banks[7])
         pick(3, 0, 2)
-        turn(3, 0, 2, banks[1])
+        turn(3, 0, 2, banks[6])
         pick(3, 2, 4)
-        turn(3, 2, 4, banks[0])
+        turn(3, 2, 4, banks[7])
         slope_room(1, 3, "picked3_2")
         make_slope(1)
         make_slope(2)
-        back = [banks[2], banks[3], banks[4], banks[5], banks[6]]
+        back = banks[0:BLOCKS]
         turn_back(0, back[0])
         turn_back(1, back[1])
         pick(3, 4, BLOCKS)
         pick(2, 4, BLOCKS, tag="picked2_0")
-        turn_last(2, banks[1])
+        turn_last(2, banks[6])
         slope_room(3, BLOCKS, "picked3_4")
         make_slope(3)
         make_slope(4)
@@ -308,11 +330,11 @@ def tile_moe_sub_relu2_kernel(
         turn_back(2, back[2])
         turn_back(3, back[3])
         turn_back(4, back[4])
-        finish(0, [banks[1], banks[0]])
+        finish(0, banks[6:8])
         make_da(2, back[2])
         make_da(3, back[3])
         quantize(1)
         make_da(4, back[4])
         quantize(2)
-        finish(1, [back[0], banks[7]])
-        finish(2, [back[1], back[2]])
+        finish(1, back[0:2])
+        finish(2, [back[2], banks[5]])

@@ -21,11 +21,13 @@ U8 = mybir.dt.uint8
 FP8X4 = mybir.dt.float8_e4m3fn_x4
 FP4X4 = mybir.dt.float4_e2m1fn_x4
 MULT = mybir.AluOpType.mult
-RELU = mybir.ActivationFunctionType.Relu
+ADD = mybir.AluOpType.add
+MAX = mybir.AluOpType.max
+COPY = mybir.ActivationFunctionType.Copy
 
-BYTE_PIECES = [[(0, 384)], [(384, 832), (832, 1280)]]
+WHOLE = 4
+BYTE_PARTS = [[(0, 384)], [(384, 832), (832, 1280)]]
 SHIFT_ROWS = 112
-SCALE_GROUPS = [(0, 5, 0), (5, 10, 0), (0, 4, 2), (4, 7, 2), (7, 10, 2)]
 TOKEN_GROUPS = [(0, 2), (2, 4), (4, 5)]
 
 
@@ -41,20 +43,23 @@ def tile_moe_sub_relu2_kernel(
         pos_t = [keep.tile([P, T // 16], U16, name="pos%d_t" % r) for r in range(2)]
         dyw = keep.tile([P, PASSES, T], I32, name="dyw", align_bytes=64)
         dys = keep.tile([P, T], U8, name="dys", tag="after_bytes", align_bytes=64)
-        spans = [(pieces[0][0], pieces[-1][1]) for pieces in BYTE_PIECES]
+        spans = [(pieces[0][0], pieces[-1][1]) for pieces in BYTE_PARTS]
         gs = {
             (s, part): keep.tile([P, j1 - j0], U8, name="gs%d_%d" % (s, part), align_bytes=64)
             for s in range(PASSES)
             for part, (j0, j1) in enumerate(spans)
         }
-        w2s = [keep.tile([P, PASSES * (e1 - e0), 2 * P], U8, name="w2s%d_%d" % (e0, c0), align_bytes=64) for e0, e1, c0 in SCALE_GROUPS]
+        scale_sets = [(0, WHOLE, 0, 4), (WHOLE, E, 0, 2), (WHOLE, E, 2, 4)]
+        w2s = [
+            keep.tile([P, PASSES * (e1 - e0), P * (c1 - c0)], U8, name="w2s%d_%d" % (e0, c0), align_bytes=64)
+            for e0, e1, c0, c1 in scale_sets
+        ]
         w1 = keep.tile([P, 2 * K], U8, name="w1", align_bytes=64)
         w1s = keep.tile([P, K], U8, name="w1s", align_bytes=64)
         gate_rows = keep.tile([P, P], F32, name="gate_rows")
         gate_cols = keep.tile([P, 2 * BLOCKS], F32, name="gate_cols")
         gate_t = [keep.tile([P, T], F32, name="gate%d" % r) for r in range(2)]
         a_t = keep.tile([P, 4, T], F32, name="a_t")
-        slope = {}
         ident = keep.tile([P, P], F32, name="ident")
         y = [keep.tile([P, S], F32, name="y%d" % c)[:] for c in range(CHUNKS)]
         picked = {}
@@ -74,8 +79,7 @@ def tile_moe_sub_relu2_kernel(
         for part in range(len(spans)):
             for s in range(1, PASSES):
                 nc.gpsimd.memset(gs[s, part][:].bitcast(I32), 0)
-        for room in w2s[2:]:
-            nc.gpsimd.memset(room[:].rearrange("p a b -> p (a b)").bitcast(I32), 0)
+        nc.gpsimd.memset(w2s[2][:].rearrange("p a b -> p (a b)").bitcast(I32), 0)
         nc.gpsimd.memset(w1s[:].bitcast(I32), 0)
 
         dyw_src = dy_words.rearrange("s p t d -> p s (t d)").bitcast(I32)
@@ -98,15 +102,15 @@ def tile_moe_sub_relu2_kernel(
                         w2[e, c, s] = piece[:, PASSES * (e - e0) + s, 2 * P * (c - c0) : 2 * P * (c - c0 + 1)]
 
         def load_w2_scales(g):
-            e0, e1, c0 = SCALE_GROUPS[g]
+            e0, e1, c0, c1 = scale_sets[g]
             for r in range(4):
                 nc.sync.dma_start(
                     out=w2s[g][r:P:32, :, :].bitcast(I32),
-                    in_=w2s_src[r][:, PASSES * e0 : PASSES * e1, P * c0 : P * (c0 + 2)].bitcast(I32),
+                    in_=w2s_src[r][:, PASSES * e0 : PASSES * e1, P * c0 : P * c1].bitcast(I32),
                 )
             for e in range(e0, e1):
                 for s in range(PASSES):
-                    for c in (c0, c0 + 1):
+                    for c in range(c0, c1):
                         w2_scale[e, c, s] = w2s[g][:, PASSES * (e - e0) + s, P * (c - c0) : P * (c - c0 + 1)]
 
         nc.sync.dma_start(offs_t[:], offs)
@@ -119,30 +123,20 @@ def tile_moe_sub_relu2_kernel(
         nc.sync.dma_start(out=gate_rows[0 : 2 * BLOCKS, :], in_=gate[:, 0, :].rearrange("r (j u) -> r j u", u=P))
         nc.sync.dma_start(pos_t[0][:], pos1)
         nc.sync.dma_start(pos_t[1][:], pos2)
-        load_w2(0, 3, 0, CHUNKS)
+        load_w2(0, 2, 0, CHUNKS)
 
-        gw = {}
+        nc.tensor.transpose(banks[7][:, 0:P], gate_rows[:], ident[:])
+        nc.scalar.activation(out=gate_cols[:], in_=banks[7][:, 0 : 2 * BLOCKS], func=COPY, scale=2.0)
+        for r in range(2):
+            for j in range(BLOCKS):
+                place = banks[4 + r][:, P * j : P * (j + 1)] if j < 4 else banks[6][:, P * r : P * (r + 1)]
+                column = gate_cols[:, BLOCKS * r + j : BLOCKS * r + j + 1]
+                nc.tensor.transpose(place, column.to_broadcast([P, P]), ident[:])
+            nc.scalar.copy(out=gate_t[r][:, 0 : 4 * P], in_=banks[4 + r][:])
+        for r in range(2):
+            nc.scalar.copy(out=gate_t[r][:, 4 * P : T], in_=banks[6][:, P * r : P * (r + 1)])
 
-        def gather_words(s, e0, e1, room):
-            nc.vector.tensor_copy(room.bitcast(U32), dyw[:, s, :].bitcast(U32).indirect(offs_t[:, C * e0 // 16 : C * e1 // 16]))
-            for e in range(e0, e1):
-                gw[s, e] = room[:, C * (e - e0) : C * (e - e0 + 1)]
-
-        def spread_gate(first, wide, rest):
-            nc.tensor.transpose(first[:, 0:P], gate_rows[:], ident[:])
-            nc.scalar.copy(out=gate_cols[:], in_=first[:, 0 : 2 * BLOCKS])
-            for r in range(2):
-                for j in range(BLOCKS):
-                    place = wide[r][:, P * j : P * (j + 1)] if j < 4 else rest[:, P * r : P * (r + 1)]
-                    column = gate_cols[:, BLOCKS * r + j : BLOCKS * r + j + 1]
-                    nc.tensor.transpose(place, column.to_broadcast([P, P]), ident[:])
-                nc.scalar.copy(out=gate_t[r][:, 0 : 4 * P], in_=wide[r][:])
-            for r in range(2):
-                nc.scalar.copy(out=gate_t[r][:, 4 * P : T], in_=rest[:, P * r : P * (r + 1)])
-
-        spread_gate(banks[7], banks[4:6], banks[6])
-
-        for part, pieces in enumerate(BYTE_PIECES):
+        for part, pieces in enumerate(BYTE_PARTS):
             for j0, j1 in pieces:
                 first = spans[part][0]
                 nc.vector.tensor_copy(gs[0, part][:, j0 - first : j1 - first], dys[:].indirect(offs_t[:, j0 // 16 : j1 // 16]))
@@ -159,49 +153,46 @@ def tile_moe_sub_relu2_kernel(
             return gs[s, part][:, first : first + C]
 
         shift_bytes(0)
-        load_w2(3, 5, 0, CHUNKS)
+        load_w2(2, WHOLE, 0, CHUNKS)
         shift_bytes(1)
-        load_w2(5, 6, 0, CHUNKS)
-        load_w2(6, 8, 0, 2)
-        load_w2(8, 10, 0, 2)
-        for g in range(2, len(SCALE_GROUPS)):
-            load_w2_scales(g)
-        load_w2(6, 8, 2, 4)
-        load_w2(8, 10, 2, 4)
-        nc.sync.dma_start(out=a_t[:], in_=a.rearrange("(p t) n -> p t n", t=4))
-        nc.sync.dma_start(out=w1[:].bitcast(I32), in_=w1t_words[0].bitcast(I32))
+        load_w2(4, 7, 0, 2)
+        load_w2(7, 10, 0, 2)
+        load_w2_scales(2)
         for r in range(4):
             nc.sync.dma_start(out=w1s[r:P:32, :].bitcast(I32), in_=w1s_src[r].bitcast(I32))
+        load_w2(4, 7, 2, 4)
+        load_w2(7, 10, 2, 4)
+        nc.sync.dma_start(out=a_t[:], in_=a.rearrange("(p t) n -> p t n", t=4))
+        nc.sync.dma_start(out=w1[:].bitcast(I32), in_=w1t_words[0].bitcast(I32))
+
+        gw = {}
         gw_all = keep.tile([P, PASSES * S], I32, name="gw_all", tag="after_bytes", align_bytes=64)
-        for e0, e1 in ((0, 3), (3, 6), (6, 8), (8, 10)):
+        for e0, e1 in ((0, 2), (2, 4), (4, 7), (7, 10)):
             for s in range(PASSES):
-                gather_words(s, e0, e1, gw_all[:, S * s + C * e0 : S * s + C * e1])
+                room = gw_all[:, S * s + C * e0 : S * s + C * e1]
+                nc.vector.tensor_copy(room.bitcast(U32), dyw[:, s, :].bitcast(U32).indirect(offs_t[:, C * e0 // 16 : C * e1 // 16]))
+                for e in range(e0, e1):
+                    gw[s, e] = room[:, C * (e - e0) : C * (e - e0 + 1)]
+
+        def product(e, c, place):
+            for s in range(PASSES):
+                nc.tensor.matmul_mx(
+                    out=place,
+                    lhsT=w2[e, c, s].bitcast(FP4X4),
+                    lhsT_scale=w2_scale[e, c, s],
+                    rhs=gw[s, e].bitcast(FP8X4),
+                    rhs_scale=slot_scales(s, e),
+                    start=(s == 0),
+                    stop=(s == PASSES - 1),
+                )
 
         def experts(c, e0, e1, bank):
-            for e in reversed(range(e0, e1)) if c == CHUNKS - 1 else range(e0, e1):
-                for s in range(PASSES):
-                    nc.tensor.matmul_mx(
-                        out=bank[:, C * (e - e0) : C * (e - e0 + 1)],
-                        lhsT=w2[e, c, s].bitcast(FP4X4),
-                        lhsT_scale=w2_scale[e, c, s],
-                        rhs=gw[s, e].bitcast(FP8X4),
-                        rhs_scale=slot_scales(s, e),
-                        start=(s == 0),
-                        stop=(s == PASSES - 1),
-                    )
+            for e in range(e0, e1):
+                product(e, c, bank[:, C * (e - e0) : C * (e - e0 + 1)])
             nc.scalar.copy(out=y[c][:, C * e0 : C * e1], in_=bank[:, 0 : C * (e1 - e0)])
 
-        def slope_room(j0, j1, tag):
-            room = keep.tile([P, P * (j1 - j0), 4], F32, name="slope%d" % j0, tag=tag)
-            for j in range(j0, j1):
-                slope[j] = room[:, P * (j - j0) : P * (j - j0 + 1), :]
-
-        def make_slope(j):
-            nc.scalar.activation(out=slope[j], in_=a_t[:, :, P * j : P * (j + 1)].rearrange("p t n -> p n t"), func=RELU, scale=2.0)
-
-        def pick(c, j0, j1, tag=None):
-            name = "picked%d_%d" % (c, j0)
-            room = keep.tile([P, 2, P * (j1 - j0)], F32, name=name, tag=tag or name)
+        def pick_gated(c, j0, j1):
+            room = keep.tile([P, 2, P * (j1 - j0)], F32, name="picked%d_%d" % (c, j0))
             for r in range(2):
                 nc.vector.tensor_tensor(
                     room[:, r, :], y[c].indirect(pos_t[r][:, P * j0 // 16 : P * j1 // 16]), gate_t[r][:, P * j0 : P * j1], MULT
@@ -209,42 +200,68 @@ def tile_moe_sub_relu2_kernel(
                 for j in range(j0, j1):
                     picked[r, c, j] = room[:, r, P * (j - j0) : P * (j - j0 + 1)]
 
-        def add_turned(pieces, bank):
+        def pick_plain(c, j0, j1):
+            room = keep.tile([P, 2, P * (j1 - j0)], F32, name="picked%d_%d" % (c, j0))
             for r in range(2):
-                for n, (c, j) in enumerate(pieces):
+                nc.scalar.activation(out=room[:, r, :], in_=y[c].indirect(pos_t[r][:, P * j0 // 16 : P * j1 // 16]), func=COPY)
+                for j in range(j0, j1):
+                    picked[r, c, j] = room[:, r, P * (j - j0) : P * (j - j0 + 1)]
+
+        def turn_gated(c, j0, j1, place):
+            n = j1 - j0
+            for r in range(2):
+                for j in range(j0, j1):
                     nc.tensor.matmul(
-                        out=bank[:, P * n : P * (n + 1)],
+                        out=place[:, P * (j - j0) : P * (j - j0 + 1)],
                         lhsT=picked[r, c, j],
                         rhs=ident[:],
                         is_transpose=True,
-                        start=(r == 0 and n == 0),
-                        stop=(r == 1 and n == len(pieces) - 1),
+                        start=(r == 0 and j == j0),
+                        stop=(r == 1 and j == j1 - 1),
                     )
 
-        def turn_last(c0, bank):
-            add_turned([(c0, BLOCKS - 1), (c0 + 1, BLOCKS - 1)], bank)
-            nc.scalar.copy(
-                out=dh_t[:, BLOCKS - 1, :, 32 * c0 : 32 * (c0 + 2)],
-                in_=bank[:, 0 : 2 * P].rearrange("p (m t) -> p t m", t=4),
+        def sort_gated(c, j0, j1, place, move=nc.scalar.copy):
+            move(
+                out=dh_t[:, j0:j1, :, 32 * c : 32 * (c + 1)],
+                in_=place[:, 0 : P * (j1 - j0)].rearrange("p (j m t) -> p j t m", m=32, t=4),
             )
 
-        def turn(c, j0, j1, bank):
-            add_turned([(c, j) for j in range(j0, j1)], bank)
-            nc.scalar.copy(
-                out=dh_t[:, j0:j1, :, 32 * c : 32 * (c + 1)],
-                in_=bank[:, 0 : P * (j1 - j0)].rearrange("p (j m t) -> p j t m", m=32, t=4),
-            )
+        def turn_plain(c, j0, j1, r, place):
+            for j in range(j0, j1):
+                nc.tensor.transpose(place[:, P * (j - j0) : P * (j - j0 + 1)], picked[r, c, j], ident[:])
+
+        def gate_and_add(c, j0, j1, first, second):
+            halves = {}
+            for j in range(j0, j1):
+                halves[j] = keep.tile([P, 4, 32], F32, name="second%d_%d" % (c, j))
+                nc.scalar.activation(
+                    out=halves[j][:],
+                    in_=second[:, P * (j - j0) : P * (j - j0 + 1)].rearrange("p (m t) -> p t m", t=4),
+                    func=COPY,
+                    scale=gate_cols[:, BLOCKS + j : BLOCKS + j + 1],
+                )
+            for j in range(j0, j1):
+                nc.vector.scalar_tensor_tensor(
+                    out=dh_t[:, j, :, 32 * c : 32 * (c + 1)],
+                    in0=first[:, P * (j - j0) : P * (j - j0 + 1)].rearrange("p (m t) -> p t m", t=4),
+                    scalar=gate_cols[:, j : j + 1],
+                    in1=halves[j][:],
+                    op0=MULT,
+                    op1=ADD,
+                )
 
         def turn_back(j, bank):
             for t in range(4):
                 nc.tensor.transpose(bank[:, P * t : P * (t + 1)], dh_t[:, j, t, :], ident[:])
 
         def make_da(j, bank):
-            nc.vector.tensor_tensor(
-                da[:, P * j : P * (j + 1), :],
-                bank[:].rearrange("p (t n) -> p n t", t=4),
-                slope[j],
-                MULT,
+            nc.vector.scalar_tensor_tensor(
+                out=da[:, P * j : P * (j + 1), :],
+                in0=a_t[:, :, P * j : P * (j + 1)].rearrange("p t n -> p n t"),
+                scalar=0.0,
+                in1=bank[:].rearrange("p (t n) -> p n t", t=4),
+                op0=MAX,
+                op1=MULT,
             )
 
         def quantize(g):
@@ -255,14 +272,14 @@ def tile_moe_sub_relu2_kernel(
                 in_=da[:, t0:t1, :].rearrange("p n t -> p (n t)"),
             )
 
-        def finish(g, pair):
+        def finish(g, pair, move=nc.scalar.copy):
             t0, t1 = P * TOKEN_GROUPS[g][0], P * TOKEN_GROUPS[g][1]
             n = t1 - t0
             out_view = out.rearrange("(c p) n -> p c n", p=P)
-            for half in range(2):
-                bank = pair[half]
-                for cc in range(2):
-                    c = 2 * half + cc
+            per_bank = CHUNKS // len(pair)
+            for half, bank in enumerate(pair):
+                for cc in range(per_bank):
+                    c = per_bank * half + cc
                     nc.tensor.matmul_mx(
                         out=bank[:, n * cc : n * (cc + 1)],
                         lhsT=w1[:, 256 * c : 256 * (c + 1)].bitcast(FP4X4),
@@ -272,69 +289,52 @@ def tile_moe_sub_relu2_kernel(
                         start=True,
                         stop=True,
                     )
-                dst = result[:, 2 * half : 2 * half + 2, t0:t1]
-                src = bank[:, 0 : 2 * n].rearrange("p (c n) -> p c n", c=2)
-                if g > 0 and half == 1:
-                    nc.vector.tensor_copy(out=dst, in_=src)
-                else:
-                    nc.scalar.copy(out=dst, in_=src)
-                if g < len(TOKEN_GROUPS) - 1:
-                    nc.sync.dma_start(out=out_view[:, 2 * half : 2 * half + 2, t0:t1], in_=dst)
-            if g == len(TOKEN_GROUPS) - 1:
-                nc.sync.dma_start(out=out_view[:, :, t0:t1], in_=result[:, :, t0:t1])
+                rows = slice(per_bank * half, per_bank * (half + 1))
+                move(out=result[:, rows, t0:t1], in_=bank[:, 0 : per_bank * n].rearrange("p (c n) -> p c n", c=per_bank))
+                nc.sync.dma_start(out=out_view[:, rows, t0:t1], in_=result[:, rows, t0:t1])
 
-        experts(0, 0, 3, banks[0])
-        experts(1, 0, 3, banks[1])
-        experts(0, 3, 6, banks[2])
-        experts(1, 3, 6, banks[3])
-        experts(0, 6, 8, banks[4])
-        experts(0, 8, 10, banks[5])
-        experts(1, 6, 8, banks[5])
-        experts(1, 8, 10, banks[6])
+        for e in range(WHOLE):
+            for c in range(CHUNKS):
+                product(e, c, banks[c][:, C * e : C * (e + 1)])
+        for c in range(CHUNKS):
+            nc.scalar.copy(out=y[c][:, 0 : C * WHOLE], in_=banks[c][:, 0 : C * WHOLE])
+        experts(0, 4, 7, banks[4])
+        experts(1, 4, 7, banks[5])
+        experts(0, 7, 10, banks[6])
+        experts(1, 7, 10, banks[7])
 
-        pick(0, 0, BLOCKS)
-        pick(1, 0, BLOCKS)
-        experts(2, 0, 3, banks[0])
-        experts(2, 3, 6, banks[1])
-        experts(2, 6, 8, banks[3])
-        experts(2, 8, 10, banks[7])
-        experts(3, 0, 3, banks[2])
-        experts(3, 6, 10, banks[6])
-        experts(3, 3, 6, banks[7])
-        turn(0, 0, 4, banks[6])
-        turn(1, 0, 4, banks[7])
-        turn_last(0, banks[6])
-        slope_room(0, 1, "picked1_0")
-        make_slope(0)
-        pick(2, 0, 4)
-        turn(2, 0, 4, banks[7])
-        pick(3, 0, 2)
-        turn(3, 0, 2, banks[6])
-        pick(3, 2, 4)
-        turn(3, 2, 4, banks[7])
-        slope_room(1, 3, "picked3_2")
-        make_slope(1)
-        make_slope(2)
-        back = banks[0:BLOCKS]
-        turn_back(0, back[0])
-        turn_back(1, back[1])
-        pick(3, 4, BLOCKS)
-        pick(2, 4, BLOCKS, tag="picked2_0")
-        turn_last(2, banks[6])
-        slope_room(3, BLOCKS, "picked3_4")
-        make_slope(3)
-        make_slope(4)
-        make_da(0, back[0])
-        make_da(1, back[1])
-        quantize(0)
-        turn_back(2, back[2])
-        turn_back(3, back[3])
-        turn_back(4, back[4])
-        finish(0, banks[6:8])
-        make_da(2, back[2])
-        make_da(3, back[3])
-        quantize(1)
-        make_da(4, back[4])
-        quantize(2)
-        finish(1, back[0:2])
-        finish(2, [back[2], banks[5]])
+        pick_plain(1, 0, 3)
+        pick_gated(0, 0, BLOCKS)
+        pick_gated(1, 3, BLOCKS)
+        experts(2, 4, 7, banks[0])
+        experts(3, 4, 7, banks[1])
+        experts(2, 7, 10, banks[2])
+        experts(3, 7, 10, banks[3])
+        turn_plain(1, 0, 3, 0, banks[0])
+        turn_plain(1, 0, 3, 1, banks[1])
+        gate_and_add(1, 0, 3, banks[0], banks[1])
+        turn_gated(0, 0, 4, banks[2])
+        sort_gated(0, 0, 4, banks[2], nc.vector.tensor_copy)
+        turn_gated(0, 4, BLOCKS, banks[3][:, 0:P])
+        turn_gated(1, 3, BLOCKS, banks[3][:, P : 3 * P])
+        sort_gated(0, 4, BLOCKS, banks[3][:, 0:P])
+        sort_gated(1, 3, BLOCKS, banks[3][:, P : 3 * P])
+
+        for (j0, j1), mixed, first in zip(TOKEN_GROUPS, (banks[4], banks[6], banks[4]), (banks[5], banks[7], banks[5])):
+            n = P * (j1 - j0)
+            pick_gated(2, j0, j1)
+            pick_plain(3, j0, j1)
+            turn_gated(2, j0, j1, mixed[:, 0:n])
+            turn_plain(3, j0, j1, 1, mixed[:, n : 2 * n])
+            turn_plain(3, j0, j1, 0, first)
+            sort_gated(2, j0, j1, mixed[:, 0:n])
+            gate_and_add(3, j0, j1, first, mixed[:, n : 2 * n])
+        back = banks[0:4] + [banks[6]]
+        for g, (j0, j1) in enumerate(TOKEN_GROUPS):
+            for j in range(j0, j1):
+                turn_back(j, back[j])
+                make_da(j, back[j])
+            quantize(g)
+        finish(0, banks[0:2])
+        finish(1, banks[2:4])
+        finish(2, banks[7:8], nc.vector.tensor_copy)

@@ -58,6 +58,7 @@ def tile_moe_sub_relu2_kernel(
         w1s = keep.tile([P, K], U8, name="w1s", align_bytes=64)
         gate_rows = keep.tile([P, P], F32, name="gate_rows")
         gate_cols = keep.tile([P, 2 * BLOCKS], F32, name="gate_cols")
+        held_gate = keep.tile([P, 1], F32, name="held_gate", tag="before_last_picks")
         gate_t = [keep.tile([P, T], F32, name="gate%d" % r) for r in range(2)]
         a_t = keep.tile([P, 4, T], F32, name="a_t")
         ident = keep.tile([P, P], F32, name="ident")
@@ -127,6 +128,7 @@ def tile_moe_sub_relu2_kernel(
 
         nc.tensor.transpose(banks[7][:, 0:P], gate_rows[:], ident[:])
         nc.scalar.activation(out=gate_cols[:], in_=banks[7][:, 0 : 2 * BLOCKS], func=COPY, scale=2.0)
+        nc.scalar.activation(out=held_gate[:], in_=banks[7][:, BLOCKS + 3 : BLOCKS + 4], func=COPY, scale=2.0)
         for r in range(2):
             for j in range(BLOCKS):
                 place = banks[4 + r][:, P * j : P * (j + 1)] if j < 4 else banks[6][:, P * r : P * (r + 1)]
@@ -167,7 +169,7 @@ def tile_moe_sub_relu2_kernel(
 
         gw = {}
         gw_all = keep.tile([P, PASSES * S], I32, name="gw_all", tag="after_bytes", align_bytes=64)
-        for e0, e1 in ((0, 2), (2, 4), (4, 7), (7, 10)):
+        for e0, e1 in ((0, 2), (2, 4), (4, 7), (7, 9), (9, 10)):
             for s in range(PASSES):
                 room = gw_all[:, S * s + C * e0 : S * s + C * e1]
                 nc.vector.tensor_copy(room.bitcast(U32), dyw[:, s, :].bitcast(U32).indirect(offs_t[:, C * e0 // 16 : C * e1 // 16]))
@@ -186,10 +188,10 @@ def tile_moe_sub_relu2_kernel(
                     stop=(s == PASSES - 1),
                 )
 
-        def experts(c, e0, e1, bank):
+        def experts(c, e0, e1, bank, move=nc.scalar.copy):
             for e in range(e0, e1):
                 product(e, c, bank[:, C * (e - e0) : C * (e - e0 + 1)])
-            nc.scalar.copy(out=y[c][:, C * e0 : C * e1], in_=bank[:, 0 : C * (e1 - e0)])
+            move(out=y[c][:, C * e0 : C * e1], in_=bank[:, 0 : C * (e1 - e0)])
 
         def pick_gated(c, j0, j1):
             room = keep.tile([P, 2, P * (j1 - j0)], F32, name="picked%d_%d" % (c, j0))
@@ -200,8 +202,9 @@ def tile_moe_sub_relu2_kernel(
                 for j in range(j0, j1):
                     picked[r, c, j] = room[:, r, P * (j - j0) : P * (j - j0 + 1)]
 
-        def pick_plain(c, j0, j1):
-            room = keep.tile([P, 2, P * (j1 - j0)], F32, name="picked%d_%d" % (c, j0))
+        def pick_plain(c, j0, j1, room=None):
+            if room is None:
+                room = keep.tile([P, 2, P * (j1 - j0)], F32, name="picked%d_%d" % (c, j0))
             for r in range(2):
                 nc.scalar.activation(out=room[:, r, :], in_=y[c].indirect(pos_t[r][:, P * j0 // 16 : P * j1 // 16]), func=COPY)
                 for j in range(j0, j1):
@@ -238,7 +241,7 @@ def tile_moe_sub_relu2_kernel(
                     out=halves[j][:],
                     in_=second[:, P * (j - j0) : P * (j - j0 + 1)].rearrange("p (m t) -> p t m", t=4),
                     func=COPY,
-                    scale=gate_cols[:, BLOCKS + j : BLOCKS + j + 1],
+                    scale=held_gate[:] if (c, j) == (3, 3) else gate_cols[:, BLOCKS + j : BLOCKS + j + 1],
                 )
             for j in range(j0, j1):
                 nc.vector.scalar_tensor_tensor(
@@ -272,7 +275,7 @@ def tile_moe_sub_relu2_kernel(
                 in_=da[:, t0:t1, :].rearrange("p n t -> p (n t)"),
             )
 
-        def finish(g, pair, move=nc.scalar.copy):
+        def finish(g, pair, movers):
             t0, t1 = P * TOKEN_GROUPS[g][0], P * TOKEN_GROUPS[g][1]
             n = t1 - t0
             out_view = out.rearrange("(c p) n -> p c n", p=P)
@@ -290,7 +293,7 @@ def tile_moe_sub_relu2_kernel(
                         stop=True,
                     )
                 rows = slice(per_bank * half, per_bank * (half + 1))
-                move(out=result[:, rows, t0:t1], in_=bank[:, 0 : per_bank * n].rearrange("p (c n) -> p c n", c=per_bank))
+                movers[half](out=result[:, rows, t0:t1], in_=bank[:, 0 : per_bank * n].rearrange("p (c n) -> p c n", c=per_bank))
                 nc.sync.dma_start(out=out_view[:, rows, t0:t1], in_=result[:, rows, t0:t1])
 
         for e in range(WHOLE):
@@ -300,27 +303,26 @@ def tile_moe_sub_relu2_kernel(
             nc.scalar.copy(out=y[c][:, 0 : C * WHOLE], in_=banks[c][:, 0 : C * WHOLE])
         experts(0, 4, 7, banks[4])
         experts(1, 4, 7, banks[5])
-        experts(0, 7, 10, banks[6])
-        experts(1, 7, 10, banks[7])
-
+        experts(0, 7, 9, banks[0])
+        experts(1, 7, 9, banks[1])
+        experts(0, 9, 10, banks[2], nc.vector.tensor_copy)
+        experts(1, 9, 10, banks[3])
         pick_plain(1, 0, 3)
         pick_gated(0, 0, BLOCKS)
         pick_gated(1, 3, BLOCKS)
-        experts(2, 4, 7, banks[0])
-        experts(3, 4, 7, banks[1])
-        experts(2, 7, 10, banks[2])
-        experts(3, 7, 10, banks[3])
-        turn_plain(1, 0, 3, 0, banks[0])
-        turn_plain(1, 0, 3, 1, banks[1])
-        gate_and_add(1, 0, 3, banks[0], banks[1])
-        turn_gated(0, 0, 4, banks[2])
-        sort_gated(0, 0, 4, banks[2], nc.vector.tensor_copy)
-        turn_gated(0, 4, BLOCKS, banks[3][:, 0:P])
-        turn_gated(1, 3, BLOCKS, banks[3][:, P : 3 * P])
-        sort_gated(0, 4, BLOCKS, banks[3][:, 0:P])
-        sort_gated(1, 3, BLOCKS, banks[3][:, P : 3 * P])
+        experts(2, 4, 7, banks[6])
+        experts(3, 4, 7, banks[7])
+        experts(2, 7, 10, banks[5])
+        experts(3, 7, 10, banks[4])
+        turn_plain(1, 0, 3, 1, banks[6])
+        turn_plain(1, 0, 3, 0, banks[7])
+        gate_and_add(1, 0, 3, banks[7], banks[6])
+        turn_gated(0, 0, 4, banks[5])
+        sort_gated(0, 0, 4, banks[5], nc.vector.tensor_copy)
+        turn_gated(0, 4, BLOCKS, banks[4][:, 0:P])
+        turn_gated(1, 3, BLOCKS, banks[4][:, P : 3 * P])
 
-        for (j0, j1), mixed, first in zip(TOKEN_GROUPS, (banks[4], banks[6], banks[4]), (banks[5], banks[7], banks[5])):
+        for (j0, j1), mixed, first in zip(TOKEN_GROUPS[:2], (banks[2], banks[0]), (banks[3], banks[1])):
             n = P * (j1 - j0)
             pick_gated(2, j0, j1)
             pick_plain(3, j0, j1)
@@ -329,12 +331,23 @@ def tile_moe_sub_relu2_kernel(
             turn_plain(3, j0, j1, 0, first)
             sort_gated(2, j0, j1, mixed[:, 0:n])
             gate_and_add(3, j0, j1, first, mixed[:, n : 2 * n])
-        back = banks[0:4] + [banks[6]]
+        last = keep.tile([P, 2, 2, P], F32, name="last_picks", tag="before_last_picks")
+        for c in (2, 3):
+            pick_plain(c, 4, BLOCKS, last[:, c - 2])
+        sort_gated(0, 4, BLOCKS, banks[4][:, 0:P])
+        sort_gated(1, 3, BLOCKS, banks[4][:, P : 3 * P])
+        back = [banks[6], banks[5], banks[2], banks[3], banks[4]]
         for g, (j0, j1) in enumerate(TOKEN_GROUPS):
+            if g == 2:
+                for r, bank in ((1, banks[7]), (0, banks[0])):
+                    for c in (2, 3):
+                        turn_plain(c, j0, j1, r, bank[:, P * (c - 2) : P * (c - 1)])
+                for c in (2, 3):
+                    gate_and_add(c, j0, j1, banks[0][:, P * (c - 2) : P * (c - 1)], banks[7][:, P * (c - 2) : P * (c - 1)])
             for j in range(j0, j1):
                 turn_back(j, back[j])
                 make_da(j, back[j])
             quantize(g)
-        finish(0, banks[0:2])
-        finish(1, banks[2:4])
-        finish(2, banks[7:8], nc.vector.tensor_copy)
+        finish(0, back[0:2], [nc.scalar.copy] * 2)
+        finish(1, back[2:4], [nc.scalar.copy] * 2)
+        finish(2, [banks[1], banks[7]], [nc.vector.tensor_copy, nc.scalar.copy])

@@ -26,7 +26,10 @@ MAX = mybir.AluOpType.max
 COPY = mybir.ActivationFunctionType.Copy
 
 WHOLE = 4
-BYTE_PARTS = [[(0, 384)], [(384, 832), (832, 1280)]]
+HALVED_GROUPS = [(4, 7), (7, 9), (9, 10)]
+HALF_LOADS = [(4, 7), (7, 10)]
+BYTE_PARTS = [[(0, 512)], [(512, 1280)]]
+BYTE_WINDOW = 1024
 SHIFT_ROWS = 112
 TOKEN_GROUPS = [(0, 2), (2, 4), (4, 5)]
 
@@ -42,7 +45,7 @@ def tile_moe_sub_relu2_kernel(
         offs_t = keep.tile([P, S // 16], U16, name="offs_t")
         pos_t = [keep.tile([P, T // 16], U16, name="pos%d_t" % r) for r in range(2)]
         dyw = keep.tile([P, PASSES, T], I32, name="dyw", align_bytes=64)
-        dys = keep.tile([P, T], U8, name="dys", tag="after_bytes", align_bytes=64)
+        dys = keep.tile([P, BYTE_WINDOW], U8, name="dys", tag="after_bytes", align_bytes=64)
         spans = [(pieces[0][0], pieces[-1][1]) for pieces in BYTE_PARTS]
         gs = {
             (s, part): keep.tile([P, j1 - j0], U8, name="gs%d_%d" % (s, part), align_bytes=64)
@@ -85,22 +88,21 @@ def tile_moe_sub_relu2_kernel(
 
         dyw_src = dy_words.rearrange("s p t d -> p s (t d)").bitcast(I32)
         dys_src = dy_scales.rearrange("s (q r) t -> q s r t", r=4)
-        w2_src = w2t_words.rearrange("e s p b -> p (e s) b")
+        w2_src = w2t_words.rearrange("e s p b -> p e s b")
         w2s_src = w2t_scales.rearrange("e s (q r) n -> r q (e s) n", r=4)
         w1s_src = w1t_scales[0].rearrange("(q r) n -> r q n", r=4)
         w2 = {}
         w2_scale = {}
 
-        def load_w2(e0, e1, c0, c1):
-            piece = keep.tile([P, (e1 - e0) * PASSES, 2 * P * (c1 - c0)], U8, name="w2_%d_%d" % (e0, c0), align_bytes=64)
-            nc.sync.dma_start(
-                out=piece[:].bitcast(I32),
-                in_=w2_src[:, PASSES * e0 : PASSES * e1, 2 * P * c0 : 2 * P * c1].bitcast(I32),
-            )
+        def load_w2(e0, e1, c0, c1, s0=0, s1=PASSES):
+            name = "w2_%d_%d_%d" % (e0, c0, s0)
+            piece = keep.tile([P, e1 - e0, s1 - s0, 2 * P * (c1 - c0)], U8, name=name, align_bytes=64)
+            rows = w2_src[:, e0:e1, s0:s1, 2 * P * c0 : 2 * P * c1].rearrange("p e s b -> p (e s) b")
+            nc.sync.dma_start(out=piece[:].rearrange("p e s b -> p (e s) b").bitcast(I32), in_=rows.bitcast(I32))
             for e in range(e0, e1):
                 for c in range(c0, c1):
-                    for s in range(PASSES):
-                        w2[e, c, s] = piece[:, PASSES * (e - e0) + s, 2 * P * (c - c0) : 2 * P * (c - c0 + 1)]
+                    for s in range(s0, s1):
+                        w2[e, c, s] = piece[:, e - e0, s - s0, 2 * P * (c - c0) : 2 * P * (c - c0 + 1)]
 
         def load_w2_scales(g):
             e0, e1, c0, c1 = scale_sets[g]
@@ -118,13 +120,13 @@ def tile_moe_sub_relu2_kernel(
         nc.sync.dma_start(out=dyw[:], in_=dyw_src)
         for q in range(4):
             queue = nc.sync if q < 2 else nc.scalar
-            queue.dma_start(out=dys[32 * q : 32 * q + 4 * PASSES, :].bitcast(I32), in_=dys_src[q].bitcast(I32))
+            queue.dma_start(out=dys[32 * q : 32 * q + 4 * PASSES, 0:T].bitcast(I32), in_=dys_src[q].bitcast(I32))
         load_w2_scales(0)
         load_w2_scales(1)
         nc.sync.dma_start(out=gate_rows[0 : 2 * BLOCKS, :], in_=gate[:, 0, :].rearrange("r (j u) -> r j u", u=P))
         nc.sync.dma_start(pos_t[0][:], pos1)
         nc.sync.dma_start(pos_t[1][:], pos2)
-        load_w2(0, 2, 0, CHUNKS)
+        load_w2(0, WHOLE, 0, CHUNKS, 0, 1)
 
         nc.tensor.transpose(banks[7][:, 0:P], gate_rows[:], ident[:])
         nc.scalar.activation(out=gate_cols[:], in_=banks[7][:, 0 : 2 * BLOCKS], func=COPY, scale=2.0)
@@ -155,38 +157,43 @@ def tile_moe_sub_relu2_kernel(
             return gs[s, part][:, first : first + C]
 
         shift_bytes(0)
-        load_w2(2, WHOLE, 0, CHUNKS)
+        load_w2(0, WHOLE, 0, CHUNKS, 1, 2)
+        load_w2(0, WHOLE, 0, CHUNKS, 2, 3)
         shift_bytes(1)
-        load_w2(4, 7, 0, 2)
-        load_w2(7, 10, 0, 2)
+        for e0, e1 in HALF_LOADS:
+            load_w2(e0, e1, 0, 2)
         load_w2_scales(2)
         for r in range(4):
             nc.sync.dma_start(out=w1s[r:P:32, :].bitcast(I32), in_=w1s_src[r].bitcast(I32))
-        load_w2(4, 7, 2, 4)
-        load_w2(7, 10, 2, 4)
+        for e0, e1 in HALVED_GROUPS:
+            load_w2(e0, e1, 2, 4)
         nc.sync.dma_start(out=a_t[:], in_=a.rearrange("(p t) n -> p t n", t=4))
         nc.sync.dma_start(out=w1[:].bitcast(I32), in_=w1t_words[0].bitcast(I32))
 
         gw = {}
+        gw_first = keep.tile([P, C * WHOLE], I32, name="gw_first", align_bytes=64)
         gw_all = keep.tile([P, PASSES * S], I32, name="gw_all", tag="after_bytes", align_bytes=64)
-        for e0, e1 in ((0, 2), (2, 4), (4, 7), (7, 9), (9, 10)):
-            for s in range(PASSES):
-                room = gw_all[:, S * s + C * e0 : S * s + C * e1]
-                nc.vector.tensor_copy(room.bitcast(U32), dyw[:, s, :].bitcast(U32).indirect(offs_t[:, C * e0 // 16 : C * e1 // 16]))
-                for e in range(e0, e1):
-                    gw[s, e] = room[:, C * (e - e0) : C * (e - e0 + 1)]
+        first_pieces = [(e0, e0 + 2, s) for s in range(PASSES) for e0 in (0, 2)]
+        for e0, e1, s in first_pieces + [(e0, e1, s) for e0, e1 in HALVED_GROUPS for s in range(PASSES)]:
+            room = gw_first[:, C * e0 : C * e1] if (s, e0) in ((0, 0), (0, 2)) else gw_all[:, S * s + C * e0 : S * s + C * e1]
+            nc.vector.tensor_copy(room.bitcast(U32), dyw[:, s, :].bitcast(U32).indirect(offs_t[:, C * e0 // 16 : C * e1 // 16]))
+            for e in range(e0, e1):
+                gw[s, e] = room[:, C * (e - e0) : C * (e - e0 + 1)]
+
+        def one_pass(e, c, s, place, start, stop):
+            nc.tensor.matmul_mx(
+                out=place,
+                lhsT=w2[e, c, s].bitcast(FP4X4),
+                lhsT_scale=w2_scale[e, c, s],
+                rhs=gw[s, e].bitcast(FP8X4),
+                rhs_scale=slot_scales(s, e),
+                start=start,
+                stop=stop,
+            )
 
         def product(e, c, place):
             for s in range(PASSES):
-                nc.tensor.matmul_mx(
-                    out=place,
-                    lhsT=w2[e, c, s].bitcast(FP4X4),
-                    lhsT_scale=w2_scale[e, c, s],
-                    rhs=gw[s, e].bitcast(FP8X4),
-                    rhs_scale=slot_scales(s, e),
-                    start=(s == 0),
-                    stop=(s == PASSES - 1),
-                )
+                one_pass(e, c, s, place, s == 0, s == PASSES - 1)
 
         def experts(c, e0, e1, bank, move=nc.scalar.copy):
             for e in range(e0, e1):
@@ -233,25 +240,32 @@ def tile_moe_sub_relu2_kernel(
             for j in range(j0, j1):
                 nc.tensor.transpose(place[:, P * (j - j0) : P * (j - j0 + 1)], picked[r, c, j], ident[:])
 
-        def gate_and_add(c, j0, j1, first, second):
+        def gate_and_add(c, j0, j1, first, second, width=P):
             halves = {}
             for j in range(j0, j1):
-                halves[j] = keep.tile([P, 4, 32], F32, name="second%d_%d" % (c, j))
+                halves[j] = keep.tile([P, 4, width // 4], F32, name="second%d_%d" % (c, j))
                 nc.scalar.activation(
                     out=halves[j][:],
-                    in_=second[:, P * (j - j0) : P * (j - j0 + 1)].rearrange("p (m t) -> p t m", t=4),
+                    in_=second[:, width * (j - j0) : width * (j - j0 + 1)].rearrange("p (m t) -> p t m", t=4),
                     func=COPY,
-                    scale=held_gate[:] if (c, j) == (3, 3) else gate_cols[:, BLOCKS + j : BLOCKS + j + 1],
+                    scale=held_gate[:] if (c, j) == (2, 3) else gate_cols[:, BLOCKS + j : BLOCKS + j + 1],
                 )
             for j in range(j0, j1):
                 nc.vector.scalar_tensor_tensor(
-                    out=dh_t[:, j, :, 32 * c : 32 * (c + 1)],
-                    in0=first[:, P * (j - j0) : P * (j - j0 + 1)].rearrange("p (m t) -> p t m", t=4),
+                    out=dh_t[:, j, :, 32 * c : 32 * c + width // 4],
+                    in0=first[:, width * (j - j0) : width * (j - j0 + 1)].rearrange("p (m t) -> p t m", t=4),
                     scalar=gate_cols[:, j : j + 1],
                     in1=halves[j][:],
                     op0=MULT,
                     op1=ADD,
                 )
+
+        def turn_late(j0, j1, first, second):
+            for r, bank in ((1, second), (0, first)):
+                for j in range(j0, j1):
+                    for c in (2, 3):
+                        at = P * (2 * (j - j0) + c - 2)
+                        nc.tensor.transpose(bank[:, at : at + P], picked[r, c, j], ident[:])
 
         def turn_back(j, bank):
             for t in range(4):
@@ -296,10 +310,11 @@ def tile_moe_sub_relu2_kernel(
                 movers[half](out=result[:, rows, t0:t1], in_=bank[:, 0 : per_bank * n].rearrange("p (c n) -> p c n", c=per_bank))
                 nc.sync.dma_start(out=out_view[:, rows, t0:t1], in_=result[:, rows, t0:t1])
 
-        for e in range(WHOLE):
-            for c in range(CHUNKS):
-                product(e, c, banks[c][:, C * e : C * (e + 1)])
-        for c in range(CHUNKS):
+        for s in range(PASSES):
+            for e in range(WHOLE):
+                for c in range(CHUNKS - 1):
+                    one_pass(e, c, s, banks[c][:, C * e : C * (e + 1)], (s, e) == (0, 0), (s, e) == (PASSES - 1, WHOLE - 1))
+        for c in range(CHUNKS - 1):
             nc.scalar.copy(out=y[c][:, 0 : C * WHOLE], in_=banks[c][:, 0 : C * WHOLE])
         experts(0, 4, 7, banks[4])
         experts(1, 4, 7, banks[5])
@@ -310,10 +325,13 @@ def tile_moe_sub_relu2_kernel(
         pick_plain(1, 0, 3)
         pick_gated(0, 0, BLOCKS)
         pick_gated(1, 3, BLOCKS)
+        experts(3, 0, WHOLE, banks[3])
         experts(2, 4, 7, banks[6])
         experts(3, 4, 7, banks[7])
-        experts(2, 7, 10, banks[5])
-        experts(3, 7, 10, banks[4])
+        experts(2, 7, 9, banks[0])
+        experts(3, 7, 9, banks[1])
+        experts(2, 9, 10, banks[5])
+        experts(3, 9, 10, banks[4])
         turn_plain(1, 0, 3, 1, banks[6])
         turn_plain(1, 0, 3, 0, banks[7])
         gate_and_add(1, 0, 3, banks[7], banks[6])
@@ -322,15 +340,17 @@ def tile_moe_sub_relu2_kernel(
         turn_gated(0, 4, BLOCKS, banks[4][:, 0:P])
         turn_gated(1, 3, BLOCKS, banks[4][:, P : 3 * P])
 
-        for (j0, j1), mixed, first in zip(TOKEN_GROUPS[:2], (banks[2], banks[0]), (banks[3], banks[1])):
-            n = P * (j1 - j0)
-            pick_gated(2, j0, j1)
-            pick_plain(3, j0, j1)
-            turn_gated(2, j0, j1, mixed[:, 0:n])
-            turn_plain(3, j0, j1, 1, mixed[:, n : 2 * n])
-            turn_plain(3, j0, j1, 0, first)
-            sort_gated(2, j0, j1, mixed[:, 0:n])
-            gate_and_add(3, j0, j1, first, mixed[:, n : 2 * n])
+        for c in (2, 3):
+            pick_gated(c, 0, 2)
+            pick_plain(c, 2, 4)
+        for c in (2, 3):
+            turn_gated(c, 0, 2, banks[2][:, 2 * P * (c - 2) : 2 * P * (c - 1)])
+        nc.vector.tensor_copy(
+            out=dh_t[:, 0:2, :, 64:128].rearrange("p j t (c m) -> p c j t m", c=2),
+            in_=banks[2][:].rearrange("p (c j m t) -> p c j t m", c=2, j=2, t=4),
+        )
+        turn_late(2, 4, banks[0], banks[3])
+        gate_and_add(2, 2, 4, banks[0], banks[3], 2 * P)
         last = keep.tile([P, 2, 2, P], F32, name="last_picks", tag="before_last_picks")
         for c in (2, 3):
             pick_plain(c, 4, BLOCKS, last[:, c - 2])
@@ -339,15 +359,12 @@ def tile_moe_sub_relu2_kernel(
         back = [banks[6], banks[5], banks[2], banks[3], banks[4]]
         for g, (j0, j1) in enumerate(TOKEN_GROUPS):
             if g == 2:
-                for r, bank in ((1, banks[7]), (0, banks[0])):
-                    for c in (2, 3):
-                        turn_plain(c, j0, j1, r, bank[:, P * (c - 2) : P * (c - 1)])
-                for c in (2, 3):
-                    gate_and_add(c, j0, j1, banks[0][:, P * (c - 2) : P * (c - 1)], banks[7][:, P * (c - 2) : P * (c - 1)])
+                turn_late(j0, j1, banks[1], banks[7])
+                gate_and_add(2, j0, j1, banks[1], banks[7], 2 * P)
             for j in range(j0, j1):
                 turn_back(j, back[j])
                 make_da(j, back[j])
             quantize(g)
         finish(0, back[0:2], [nc.scalar.copy] * 2)
         finish(1, back[2:4], [nc.scalar.copy] * 2)
-        finish(2, [banks[1], banks[7]], [nc.vector.tensor_copy, nc.scalar.copy])
+        finish(2, [banks[0], banks[7]], [nc.vector.tensor_copy, nc.scalar.copy])

@@ -27,7 +27,6 @@ COPY = mybir.ActivationFunctionType.Copy
 
 WHOLE = 4
 HALVED_GROUPS = [(4, 7), (7, 9), (9, 10)]
-HALF_LOADS = [(4, 7), (7, 10)]
 BYTE_PARTS = [[(0, 512)], [(512, 1280)]]
 BYTE_WINDOW = 1024
 SHIFT_ROWS = 112
@@ -83,8 +82,8 @@ def tile_moe_sub_relu2_kernel(
         for part in range(len(spans)):
             for s in range(1, PASSES):
                 nc.gpsimd.memset(gs[s, part][:].bitcast(I32), 0)
-        nc.gpsimd.memset(w2s[2][:].rearrange("p a b -> p (a b)").bitcast(I32), 0)
-        nc.gpsimd.memset(w1s[:].bitcast(I32), 0)
+        nc.vector.memset(w2s[2][:].rearrange("p a b -> p (a b)").bitcast(I32), 0)
+        nc.vector.memset(w1s[:].bitcast(I32), 0)
 
         dyw_src = dy_words.rearrange("s p t d -> p s (t d)").bitcast(I32)
         dys_src = dy_scales.rearrange("s (q r) t -> q s r t", r=4)
@@ -160,7 +159,7 @@ def tile_moe_sub_relu2_kernel(
         load_w2(0, WHOLE, 0, CHUNKS, 1, 2)
         load_w2(0, WHOLE, 0, CHUNKS, 2, 3)
         shift_bytes(1)
-        for e0, e1 in HALF_LOADS:
+        for e0, e1 in HALVED_GROUPS:
             load_w2(e0, e1, 0, 2)
         load_w2_scales(2)
         for r in range(4):
@@ -201,7 +200,7 @@ def tile_moe_sub_relu2_kernel(
             move(out=y[c][:, C * e0 : C * e1], in_=bank[:, 0 : C * (e1 - e0)])
 
         def pick_gated(c, j0, j1):
-            room = keep.tile([P, 2, P * (j1 - j0)], F32, name="picked%d_%d" % (c, j0))
+            room = keep.tile([P, 2, P * (j1 - j0)], F32, name="picked%d_%d" % (c, j0), tag="gated%d" % c)
             for r in range(2):
                 nc.vector.tensor_tensor(
                     room[:, r, :], y[c].indirect(pos_t[r][:, P * j0 // 16 : P * j1 // 16]), gate_t[r][:, P * j0 : P * j1], MULT
@@ -274,7 +273,7 @@ def tile_moe_sub_relu2_kernel(
         def make_da(j, bank):
             nc.vector.scalar_tensor_tensor(
                 out=da[:, P * j : P * (j + 1), :],
-                in0=a_t[:, :, P * j : P * (j + 1)].rearrange("p t n -> p n t"),
+                in0=a_woven[:, P * j : P * (j + 1), :],
                 scalar=0.0,
                 in1=bank[:].rearrange("p (t n) -> p n t", t=4),
                 op0=MAX,
@@ -349,6 +348,12 @@ def tile_moe_sub_relu2_kernel(
             out=dh_t[:, 0:2, :, 64:128].rearrange("p j t (c m) -> p c j t m", c=2),
             in_=banks[2][:].rearrange("p (c j m t) -> p c j t m", c=2, j=2, t=4),
         )
+        a_woven = keep.tile([P, T, 4], F32, name="a_woven", tag="gated3")
+        for j in range(BLOCKS):
+            tokens = slice(P * j, P * (j + 1))
+            nc.gpsimd.tensor_scalar(
+                out=a_woven[:, tokens, :], in0=a_t[:, :, tokens].rearrange("p t n -> p n t"), scalar1=1.0, scalar2=0.0, op0=MULT, op1=ADD
+            )
         turn_late(2, 4, banks[0], banks[3])
         gate_and_add(2, 2, 4, banks[0], banks[3], 2 * P)
         last = keep.tile([P, 2, 2, P], F32, name="last_picks", tag="before_last_picks")

@@ -74,7 +74,7 @@ def tile_moe_sub_relu2_kernel(
 
         banks = [psum.tile([P, 512], F32, name="bank%d" % b) for b in range(8)]
 
-        nc.vector.memset(dys[:].bitcast(I32), 0)
+        nc.gpsimd.memset(dys[:].bitcast(I32), 0)
         nc.gpsimd.memset(gate_rows[:], 0.0)
         make_identity(nc, ident[:])
         for room in w2s[0:2]:
@@ -116,6 +116,8 @@ def tile_moe_sub_relu2_kernel(
                         w2_scale[e, c, s] = w2s[g][:, PASSES * (e - e0) + s, P * (c - c0) : P * (c - c0 + 1)]
 
         nc.sync.dma_start(offs_t[:], offs)
+        nc.sync.dma_start(pos_t[0][:], pos1)
+        nc.sync.dma_start(pos_t[1][:], pos2)
         nc.sync.dma_start(out=dyw[:], in_=dyw_src)
         for q in range(4):
             queue = nc.sync if q < 2 else nc.scalar
@@ -123,8 +125,6 @@ def tile_moe_sub_relu2_kernel(
         load_w2_scales(0)
         load_w2_scales(1)
         nc.sync.dma_start(out=gate_rows[0 : 2 * BLOCKS, :], in_=gate[:, 0, :].rearrange("r (j u) -> r j u", u=P))
-        nc.sync.dma_start(pos_t[0][:], pos1)
-        nc.sync.dma_start(pos_t[1][:], pos2)
         load_w2(0, WHOLE, 0, CHUNKS, 0, 1)
 
         nc.tensor.transpose(banks[7][:, 0:P], gate_rows[:], ident[:])

@@ -29,6 +29,7 @@ WHOLE = 4
 HALVED_GROUPS = [(4, 7), (7, 9), (9, 10)]
 BYTE_PARTS = [[(0, 512)], [(512, 1280)]]
 BYTE_WINDOW = 1024
+WORD_WINDOW = 704
 SHIFT_ROWS = 112
 TOKEN_GROUPS = [(0, 2), (2, 4), (4, 5)]
 
@@ -43,7 +44,7 @@ def tile_moe_sub_relu2_kernel(
 
         offs_t = keep.tile([P, S // 16], U16, name="offs_t")
         pos_t = [keep.tile([P, T // 16], U16, name="pos%d_t" % r) for r in range(2)]
-        dyw = keep.tile([P, PASSES, T], I32, name="dyw", align_bytes=64)
+        dyw = keep.tile([P, (PASSES - 1) * T + WORD_WINDOW], I32, name="dyw", align_bytes=64)
         dys = keep.tile([P, BYTE_WINDOW], U8, name="dys", tag="after_bytes", align_bytes=64)
         spans = [(pieces[0][0], pieces[-1][1]) for pieces in BYTE_PARTS]
         gs = {
@@ -76,6 +77,7 @@ def tile_moe_sub_relu2_kernel(
 
         nc.gpsimd.memset(dys[:].bitcast(I32), 0)
         nc.gpsimd.memset(gate_rows[:], 0.0)
+        nc.gpsimd.memset(dyw[:, PASSES * T :], 0)
         make_identity(nc, ident[:])
         for room in w2s[0:2]:
             nc.vector.memset(room[:].rearrange("p a b -> p (a b)").bitcast(I32), 0)
@@ -118,14 +120,14 @@ def tile_moe_sub_relu2_kernel(
         nc.sync.dma_start(offs_t[:], offs)
         nc.sync.dma_start(pos_t[0][:], pos1)
         nc.sync.dma_start(pos_t[1][:], pos2)
-        nc.sync.dma_start(out=dyw[:], in_=dyw_src)
+        nc.sync.dma_start(out=dyw[:, 0 : PASSES * T].rearrange("p (s t) -> p s t", t=T), in_=dyw_src)
         for q in range(4):
             queue = nc.sync if q < 2 else nc.scalar
             queue.dma_start(out=dys[32 * q : 32 * q + 4 * PASSES, 0:T].bitcast(I32), in_=dys_src[q].bitcast(I32))
+        load_w2(0, WHOLE, 0, CHUNKS, 0, 1)
         load_w2_scales(0)
         load_w2_scales(1)
         nc.sync.dma_start(out=gate_rows[0 : 2 * BLOCKS, :], in_=gate[:, 0, :].rearrange("r (j u) -> r j u", u=P))
-        load_w2(0, WHOLE, 0, CHUNKS, 0, 1)
 
         nc.tensor.transpose(banks[7][:, 0:P], gate_rows[:], ident[:])
         nc.scalar.activation(out=gate_cols[:], in_=banks[7][:, 0 : 2 * BLOCKS], func=COPY, scale=2.0)
@@ -155,8 +157,8 @@ def tile_moe_sub_relu2_kernel(
             first = C * e - spans[part][0]
             return gs[s, part][:, first : first + C]
 
-        shift_bytes(0)
         load_w2(0, WHOLE, 0, CHUNKS, 1, 2)
+        shift_bytes(0)
         load_w2(0, WHOLE, 0, CHUNKS, 2, 3)
         shift_bytes(1)
         for e0, e1 in HALVED_GROUPS:
@@ -172,12 +174,14 @@ def tile_moe_sub_relu2_kernel(
         gw = {}
         gw_first = keep.tile([P, C * WHOLE], I32, name="gw_first", align_bytes=64)
         gw_all = keep.tile([P, PASSES * S], I32, name="gw_all", tag="after_bytes", align_bytes=64)
-        first_pieces = [(e0, e0 + 2, s) for s in range(PASSES) for e0 in (0, 2)]
-        for e0, e1, s in first_pieces + [(e0, e1, s) for e0, e1 in HALVED_GROUPS for s in range(PASSES)]:
-            room = gw_first[:, C * e0 : C * e1] if (s, e0) in ((0, 0), (0, 2)) else gw_all[:, S * s + C * e0 : S * s + C * e1]
-            nc.vector.tensor_copy(room.bitcast(U32), dyw[:, s, :].bitcast(U32).indirect(offs_t[:, C * e0 // 16 : C * e1 // 16]))
-            for e in range(e0, e1):
-                gw[s, e] = room[:, C * (e - e0) : C * (e - e0 + 1)]
+        for e0, e1 in [(0, WHOLE)] + HALVED_GROUPS:
+            for s in range(PASSES):
+                room = gw_first[:] if (s, e0) == (0, 0) else gw_all[:, S * s + C * e0 : S * s + C * e1]
+                nc.vector.tensor_copy(
+                    room.bitcast(U32), dyw[:, T * s : T * s + WORD_WINDOW].bitcast(U32).indirect(offs_t[:, C * e0 // 16 : C * e1 // 16])
+                )
+                for e in range(e0, e1):
+                    gw[s, e] = room[:, C * (e - e0) : C * (e - e0 + 1)]
 
         def one_pass(e, c, s, place, start, stop):
             nc.tensor.matmul_mx(

@@ -55,11 +55,11 @@ def tile_moe_sub_relu2_kernel(
         scale_sets = [(0, WHOLE, 0, 4), (WHOLE, E, 0, 2), (WHOLE, E, 2, 4)]
         w2s = [
             keep.tile([P, PASSES * (e1 - e0), P * (c1 - c0)], U8, name="w2s%d_%d" % (e0, c0), align_bytes=64)
-            for e0, e1, c0, c1 in scale_sets
+            for e0, e1, c0, c1 in scale_sets[0:2]
         ]
         w1 = keep.tile([P, 2 * K], U8, name="w1", align_bytes=64)
         w1s = keep.tile([P, K], U8, name="w1s", align_bytes=64)
-        gate_rows = keep.tile([P, P], F32, name="gate_rows")
+        gate_rows = keep.tile([P, P], F32, name="gate_rows", tag="after_gate", align_bytes=64)
         gate_cols = keep.tile([P, 2 * BLOCKS], F32, name="gate_cols")
         held_gate = keep.tile([P, 1], F32, name="held_gate", tag="before_last_picks")
         gate_t = [keep.tile([P, T], F32, name="gate%d" % r) for r in range(2)]
@@ -84,8 +84,6 @@ def tile_moe_sub_relu2_kernel(
         for part in range(len(spans)):
             for s in range(1, PASSES):
                 nc.gpsimd.memset(gs[s, part][:].bitcast(I32), 0)
-        nc.vector.memset(w2s[2][:].rearrange("p a b -> p (a b)").bitcast(I32), 0)
-        nc.vector.memset(w1s[:].bitcast(I32), 0)
 
         dyw_src = dy_words.rearrange("s p t d -> p s (t d)").bitcast(I32)
         dys_src = dy_scales.rearrange("s (q r) t -> q s r t", r=4)
@@ -163,6 +161,10 @@ def tile_moe_sub_relu2_kernel(
         shift_bytes(1)
         for e0, e1 in HALVED_GROUPS:
             load_w2(e0, e1, 0, 2)
+        w2s.append(keep.tile([P, PASSES * (E - WHOLE), 2 * P], U8, name="w2s_late", tag="after_gate", align_bytes=64))
+        filled = w2s[1][:].rearrange("p a b -> p (a b)").bitcast(U32)
+        nc.scalar.copy(out=w2s[2][:].rearrange("p a b -> p (a b)").bitcast(U32), in_=filled)
+        nc.scalar.copy(out=w1s[:].bitcast(U32), in_=w2s[2][:, 0:2, :].rearrange("p a b -> p (a b)").bitcast(U32))
         load_w2_scales(2)
         for r in range(4):
             nc.sync.dma_start(out=w1s[r:P:32, :].bitcast(I32), in_=w1s_src[r].bitcast(I32))

from contextlib import ExitStack

import concourse.mybir as mybir
from concourse.masks import make_identity

K, T, E, C, H, N = 512, 640, 10, 128, 512, 1536
S = E * C
P = 128
PASSES = N // 512
CHUNKS = H // P
BLOCKS = T // P

FLOPS = 2 * N * H * S + 2 * H * K * T

F32 = mybir.dt.float32
BF16 = mybir.dt.bfloat16
I32 = mybir.dt.int32
U32 = mybir.dt.uint32
U16 = mybir.dt.uint16
U8 = mybir.dt.uint8
FP8X4 = mybir.dt.float8_e4m3fn_x4
FP4X4 = mybir.dt.float4_e2m1fn_x4
MULT = mybir.AluOpType.mult
ADD = mybir.AluOpType.add
MAX = mybir.AluOpType.max
COPY = mybir.ActivationFunctionType.Copy

WHOLE = 4
HALVED_GROUPS = [(4, 7), (7, 9), (9, 10)]
BYTE_PARTS = [[(0, 512)], [(512, 1280)]]
BYTE_WINDOW = 1024
WORD_WINDOW = 704
SHIFT_ROWS = 112
TOKEN_GROUPS = [(0, 2), (2, 4), (4, 5)]


def tile_moe_sub_relu2_kernel(
    tc, dy_words, dy_scales, w2t_words, w2t_scales, w1t_words, w1t_scales, a, gate, offs, pos1, pos2, out
):
    nc = tc.nc
    with ExitStack() as ctx:
        keep = ctx.enter_context(tc.tile_pool(name="keep", bufs=1))
        psum = ctx.enter_context(tc.psum_pool(name="psum", bufs=1))

        offs_t = keep.tile([P, S // 16], U16, name="offs_t")
        pos_t = [keep.tile([P, T // 16], U16, name="pos%d_t" % r) for r in range(2)]
        dyw = keep.tile([P, (PASSES - 1) * T + WORD_WINDOW], I32, name="dyw", align_bytes=64)
        dys = keep.tile([P, BYTE_WINDOW], U8, name="dys", tag="after_bytes", align_bytes=64)
        spans = [(pieces[0][0], pieces[-1][1]) for pieces in BYTE_PARTS]
        gs = {
            (s, part): keep.tile([P, j1 - j0], U8, name="gs%d_%d" % (s, part), align_bytes=64)
            for s in range(PASSES)
            for part, (j0, j1) in enumerate(spans)
        }
        scale_sets = [(0, WHOLE, 0, 4), (WHOLE, E, 0, 2), (WHOLE, E, 2, 4)]
        w2s = [
            keep.tile([P, PASSES * (e1 - e0), P * (c1 - c0)], U8, name="w2s%d_%d" % (e0, c0), align_bytes=64)
            for e0, e1, c0, c1 in scale_sets[0:2]
        ]
        w1 = keep.tile([P, 2 * K], U8, name="w1", align_bytes=64)
        w1s = keep.tile([P, K], U8, name="w1s", align_bytes=64)
        gate_rows = keep.tile([P, P], F32, name="gate_rows", tag="after_gate", align_bytes=64)
        gate_cols = keep.tile([P, 2 * BLOCKS], F32, name="gate_cols")
        held_gate = keep.tile([P, 1], F32, name="held_gate", tag="before_last_picks")
        gate_t = [keep.tile([P, T], F32, name="gate%d" % r) for r in range(2)]
        a_t = keep.tile([P, 4, T], F32, name="a_t")
        ident = keep.tile([P, P], F32, name="ident")
        y = [keep.tile([P, S], F32, name="y%d" % c)[:] for c in range(CHUNKS)]
        picked = {}
        dh_t = keep.tile([P, BLOCKS, 4, P], F32, name="dh_t")
        da = keep.tile([P, T, 4], BF16, name="da", align_bytes=64)
        da_codes = keep.tile([P, T], U32, name="da_codes", align_bytes=64)
        da_scales = keep.tile([P, T], U8, name="da_scales", align_bytes=64)
        result = keep.tile([P, CHUNKS, T], F32, name="result")

        banks = [psum.tile([P, 512], F32, name="bank%d" % b) for b in range(8)]

        nc.gpsimd.memset(dys[:].bitcast(I32), 0)
        nc.gpsimd.memset(gate_rows[:], 0.0)
        nc.gpsimd.memset(dyw[:, PASSES * T :], 0)
        make_identity(nc, ident[:])
        for room in w2s[0:2]:
            nc.vector.memset(room[:].rearrange("p a b -> p (a b)").bitcast(I32), 0)
        for part in range(len(spans)):
            for s in range(1, PASSES):
                nc.gpsimd.memset(gs[s, part][:].bitcast(I32), 0)

        dyw_src = dy_words.rearrange("s p t d -> p s (t d)").bitcast(I32)
        dys_src = dy_scales.rearrange("s (q r) t -> q s r t", r=4)
        w2_src = w2t_words.rearrange("e s p b -> p e s b")
        w2s_src = w2t_scales.rearrange("e s (q r) n -> r q (e s) n", r=4)
        w1s_src = w1t_scales[0].rearrange("(q r) n -> r q n", r=4)
        w2 = {}
        w2_scale = {}

        def load_w2(e0, e1, c0, c1, s0=0, s1=PASSES):
            name = "w2_%d_%d_%d" % (e0, c0, s0)
            piece = keep.tile([P, e1 - e0, s1 - s0, 2 * P * (c1 - c0)], U8, name=name, align_bytes=64)
            rows = w2_src[:, e0:e1, s0:s1, 2 * P * c0 : 2 * P * c1].rearrange("p e s b -> p (e s) b")
            nc.sync.dma_start(out=piece[:].rearrange("p e s b -> p (e s) b").bitcast(I32), in_=rows.bitcast(I32))
            for e in range(e0, e1):
                for c in range(c0, c1):
                    for s in range(s0, s1):
                        w2[e, c, s] = piece[:, e - e0, s - s0, 2 * P * (c - c0) : 2 * P * (c - c0 + 1)]

        def load_w2_scales(g):
            e0, e1, c0, c1 = scale_sets[g]
            for r in range(4):
                nc.sync.dma_start(
                    out=w2s[g][r:P:32, :, :].bitcast(I32),
                    in_=w2s_src[r][:, PASSES * e0 : PASSES * e1, P * c0 : P * c1].bitcast(I32),
                )
            for e in range(e0, e1):
                for s in range(PASSES):
                    for c in range(c0, c1):
                        w2_scale[e, c, s] = w2s[g][:, PASSES * (e - e0) + s, P * (c - c0) : P * (c - c0 + 1)]

        nc.sync.dma_start(offs_t[:], offs)
        nc.sync.dma_start(pos_t[0][:], pos1)
        nc.sync.dma_start(pos_t[1][:], pos2)
        nc.sync.dma_start(out=dyw[:, 0 : PASSES * T].rearrange("p (s t) -> p s t", t=T), in_=dyw_src)
        for q in range(4):
            queue = nc.sync if q < 2 else nc.scalar
            queue.dma_start(out=dys[32 * q : 32 * q + 4 * PASSES, 0:T].bitcast(I32), in_=dys_src[q].bitcast(I32))
        load_w2(0, WHOLE, 0, CHUNKS, 0, 1)
        load_w2_scales(0)
        load_w2_scales(1)
        nc.sync.dma_start(out=gate_rows[0 : 2 * BLOCKS, :], in_=gate[:, 0, :].rearrange("r (j u) -> r j u", u=P))

        nc.tensor.transpose(banks[7][:, 0:P], gate_rows[:], ident[:])
        nc.scalar.activation(out=gate_cols[:], in_=banks[7][:, 0 : 2 * BLOCKS], func=COPY, scale=2.0)
        nc.scalar.activation(out=held_gate[:], in_=banks[7][:, BLOCKS + 3 : BLOCKS + 4], func=COPY, scale=2.0)
        for r in range(2):
            for j in range(BLOCKS):
                place = banks[4 + r][:, P * j : P * (j + 1)] if j < 4 else banks[6][:, P * r : P * (r + 1)]
                column = gate_cols[:, BLOCKS * r + j : BLOCKS * r + j + 1]
                nc.tensor.transpose(place, column.to_broadcast([P, P]), ident[:])
            nc.scalar.copy(out=gate_t[r][:, 0 : 4 * P], in_=banks[4 + r][:])
        for r in range(2):
            nc.scalar.copy(out=gate_t[r][:, 4 * P : T], in_=banks[6][:, P * r : P * (r + 1)])

        for part, pieces in enumerate(BYTE_PARTS):
            for j0, j1 in pieces:
                first = spans[part][0]
                nc.vector.tensor_copy(gs[0, part][:, j0 - first : j1 - first], dys[:].indirect(offs_t[:, j0 // 16 : j1 // 16]))

        def shift_bytes(part):
            for s in range(1, PASSES):
                nc.sync.dma_start(
                    out=gs[s, part][0:SHIFT_ROWS, :].bitcast(I32), in_=gs[0, part][4 * s : 4 * s + SHIFT_ROWS, :].bitcast(I32)
                )

        def slot_scales(s, e):
            part = 0 if C * e < spans[0][1] else 1
            first = C * e - spans[part][0]
            return gs[s, part][:, first : first + C]

        load_w2(0, WHOLE, 0, CHUNKS, 1, 2)
        shift_bytes(0)
        load_w2(0, WHOLE, 0, CHUNKS, 2, 3)
        shift_bytes(1)
        for e0, e1 in HALVED_GROUPS:
            load_w2(e0, e1, 0, 2)
        w2s.append(keep.tile([P, PASSES * (E - WHOLE), 2 * P], U8, name="w2s_late", tag="after_gate", align_bytes=64))
        filled = w2s[1][:].rearrange("p a b -> p (a b)").bitcast(U32)
        nc.scalar.copy(out=w2s[2][:].rearrange("p a b -> p (a b)").bitcast(U32), in_=filled)
        nc.scalar.copy(out=w1s[:].bitcast(U32), in_=w2s[2][:, 0:2, :].rearrange("p a b -> p (a b)").bitcast(U32))
        load_w2_scales(2)
        for r in range(4):
            nc.sync.dma_start(out=w1s[r:P:32, :].bitcast(I32), in_=w1s_src[r].bitcast(I32))
        for e0, e1 in HALVED_GROUPS:
            load_w2(e0, e1, 2, 4)
        nc.sync.dma_start(out=a_t[:], in_=a.rearrange("(p t) n -> p t n", t=4))
        nc.sync.dma_start(out=w1[:].bitcast(I32), in_=w1t_words[0].bitcast(I32))

        gw = {}
        gw_first = keep.tile([P, C * WHOLE], I32, name="gw_first", align_bytes=64)
        gw_all = keep.tile([P, PASSES * S], I32, name="gw_all", tag="after_bytes", align_bytes=64)
        for e0, e1 in [(0, WHOLE)] + HALVED_GROUPS:
            for s in range(PASSES):
                room = gw_first[:] if (s, e0) == (0, 0) else gw_all[:, S * s + C * e0 : S * s + C * e1]
                nc.vector.tensor_copy(
                    room.bitcast(U32), dyw[:, T * s : T * s + WORD_WINDOW].bitcast(U32).indirect(offs_t[:, C * e0 // 16 : C * e1 // 16])
                )
                for e in range(e0, e1):
                    gw[s, e] = room[:, C * (e - e0) : C * (e - e0 + 1)]

        def one_pass(e, c, s, place, start, stop):
            nc.tensor.matmul_mx(
                out=place,
                lhsT=w2[e, c, s].bitcast(FP4X4),
                lhsT_scale=w2_scale[e, c, s],
                rhs=gw[s, e].bitcast(FP8X4),
                rhs_scale=slot_scales(s, e),
                start=start,
                stop=stop,
            )

        def product(e, c, place):
            for s in range(PASSES):
                one_pass(e, c, s, place, s == 0, s == PASSES - 1)

        def experts(c, e0, e1, bank, move=nc.scalar.copy):
            for e in range(e0, e1):
                product(e, c, bank[:, C * (e - e0) : C * (e - e0 + 1)])
            move(out=y[c][:, C * e0 : C * e1], in_=bank[:, 0 : C * (e1 - e0)])

        def pick_gated(c, j0, j1):
            room = keep.tile([P, 2, P * (j1 - j0)], F32, name="picked%d_%d" % (c, j0), tag="gated%d" % c)
            for r in range(2):
                nc.vector.tensor_tensor(
                    room[:, r, :], y[c].indirect(pos_t[r][:, P * j0 // 16 : P * j1 // 16]), gate_t[r][:, P * j0 : P * j1], MULT
                )
                for j in range(j0, j1):
                    picked[r, c, j] = room[:, r, P * (j - j0) : P * (j - j0 + 1)]

        def pick_plain(c, j0, j1, room=None):
            if room is None:
                room = keep.tile([P, 2, P * (j1 - j0)], F32, name="picked%d_%d" % (c, j0))
            for r in range(2):
                nc.scalar.activation(out=room[:, r, :], in_=y[c].indirect(pos_t[r][:, P * j0 // 16 : P * j1 // 16]), func=COPY)
                for j in range(j0, j1):
                    picked[r, c, j] = room[:, r, P * (j - j0) : P * (j - j0 + 1)]

        def turn_gated(c, j0, j1, place):
            n = j1 - j0
            for r in range(2):
                for j in range(j0, j1):
                    nc.tensor.matmul(
                        out=place[:, P * (j - j0) : P * (j - j0 + 1)],
                        lhsT=picked[r, c, j],
                        rhs=ident[:],
                        is_transpose=True,
                        start=(r == 0 and j == j0),
                        stop=(r == 1 and j == j1 - 1),
                    )

        def sort_gated(c, j0, j1, place, move=nc.scalar.copy):
            move(
                out=dh_t[:, j0:j1, :, 32 * c : 32 * (c + 1)],
                in_=place[:, 0 : P * (j1 - j0)].rearrange("p (j m t) -> p j t m", m=32, t=4),
            )

        def turn_plain(c, j0, j1, r, place):
            for j in range(j0, j1):
                nc.tensor.transpose(place[:, P * (j - j0) : P * (j - j0 + 1)], picked[r, c, j], ident[:])

        def gate_and_add(c, j0, j1, first, second, width=P):
            halves = {}
            for j in range(j0, j1):
                halves[j] = keep.tile([P, 4, width // 4], F32, name="second%d_%d" % (c, j))
                nc.scalar.activation(
                    out=halves[j][:],
                    in_=second[:, width * (j - j0) : width * (j - j0 + 1)].rearrange("p (m t) -> p t m", t=4),
                    func=COPY,
                    scale=held_gate[:] if (c, j) == (2, 3) else gate_cols[:, BLOCKS + j : BLOCKS + j + 1],
                )
            for j in range(j0, j1):
                nc.vector.scalar_tensor_tensor(
                    out=dh_t[:, j, :, 32 * c : 32 * c + width // 4],
                    in0=first[:, width * (j - j0) : width * (j - j0 + 1)].rearrange("p (m t) -> p t m", t=4),
                    scalar=gate_cols[:, j : j + 1],
                    in1=halves[j][:],
                    op0=MULT,
                    op1=ADD,
                )

        def turn_late(j0, j1, first, second):
            for r, bank in ((1, second), (0, first)):
                for j in range(j0, j1):
                    for c in (2, 3):
                        at = P * (2 * (j - j0) + c - 2)
                        nc.tensor.transpose(bank[:, at : at + P], picked[r, c, j], ident[:])

        def turn_back(j, bank):
            for t in range(4):
                nc.tensor.transpose(bank[:, P * t : P * (t + 1)], dh_t[:, j, t, :], ident[:])

        def make_da(j, bank):
            nc.vector.scalar_tensor_tensor(
                out=da[:, P * j : P * (j + 1), :],
                in0=a_woven[:, P * j : P * (j + 1), :],
                scalar=0.0,
                in1=bank[:].rearrange("p (t n) -> p n t", t=4),
                op0=MAX,
                op1=MULT,
            )

        def quantize(g):
            t0, t1 = P * TOKEN_GROUPS[g][0], P * TOKEN_GROUPS[g][1]
            nc.vector.quantize_mx(
                out=da_codes[:, t0:t1].bitcast(FP8X4),
                scales=da_scales[:, t0:t1],
                in_=da[:, t0:t1, :].rearrange("p n t -> p (n t)"),
            )

        def finish(g, pair, movers):
            t0, t1 = P * TOKEN_GROUPS[g][0], P * TOKEN_GROUPS[g][1]
            n = t1 - t0
            out_view = out.rearrange("(c p) n -> p c n", p=P)
            per_bank = CHUNKS // len(pair)
            for half, bank in enumerate(pair):
                for cc in range(per_bank):
                    c = per_bank * half + cc
                    nc.tensor.matmul_mx(
                        out=bank[:, n * cc : n * (cc + 1)],
                        lhsT=w1[:, 256 * c : 256 * (c + 1)].bitcast(FP4X4),
                        lhsT_scale=w1s[:, P * c : P * (c + 1)],
                        rhs=da_codes[:, t0:t1].bitcast(FP8X4),
                        rhs_scale=da_scales[:, t0:t1],
                        start=True,
                        stop=True,
                    )
                rows = slice(per_bank * half, per_bank * (half + 1))
                movers[half](out=result[:, rows, t0:t1], in_=bank[:, 0 : per_bank * n].rearrange("p (c n) -> p c n", c=per_bank))
                nc.sync.dma_start(out=out_view[:, rows, t0:t1], in_=result[:, rows, t0:t1])

        for s in range(PASSES):
            for e in range(WHOLE):
                for c in range(CHUNKS - 1):
                    one_pass(e, c, s, banks[c][:, C * e : C * (e + 1)], (s, e) == (0, 0), (s, e) == (PASSES - 1, WHOLE - 1))
        for c in range(CHUNKS - 1):
            nc.scalar.copy(out=y[c][:, 0 : C * WHOLE], in_=banks[c][:, 0 : C * WHOLE])
        experts(0, 4, 7, banks[4])
        experts(1, 4, 7, banks[5])
        experts(0, 7, 9, banks[0])
        experts(1, 7, 9, banks[1])
        experts(0, 9, 10, banks[2], nc.vector.tensor_copy)
        experts(1, 9, 10, banks[3])
        pick_plain(1, 0, 3)
        pick_gated(0, 0, BLOCKS)
        pick_gated(1, 3, BLOCKS)
        experts(3, 0, WHOLE, banks[3])
        experts(2, 4, 7, banks[6])
        experts(3, 4, 7, banks[7])
        experts(2, 7, 9, banks[0])
        experts(3, 7, 9, banks[1])
        experts(2, 9, 10, banks[5])
        experts(3, 9, 10, banks[4])
        turn_plain(1, 0, 3, 1, banks[6])
        turn_plain(1, 0, 3, 0, banks[7])
        gate_and_add(1, 0, 3, banks[7], banks[6])
        turn_gated(0, 0, 4, banks[5])
        sort_gated(0, 0, 4, banks[5], nc.vector.tensor_copy)
        turn_gated(0, 4, BLOCKS, banks[4][:, 0:P])
        turn_gated(1, 3, BLOCKS, banks[4][:, P : 3 * P])

        for c in (2, 3):
            pick_gated(c, 0, 2)
            pick_plain(c, 2, 4)
        for c in (2, 3):
            turn_gated(c, 0, 2, banks[2][:, 2 * P * (c - 2) : 2 * P * (c - 1)])
        nc.vector.tensor_copy(
            out=dh_t[:, 0:2, :, 64:128].rearrange("p j t (c m) -> p c j t m", c=2),
            in_=banks[2][:].rearrange("p (c j m t) -> p c j t m", c=2, j=2, t=4),
        )
        a_woven = keep.tile([P, T, 4], F32, name="a_woven", tag="gated3")
        for j in range(BLOCKS):
            tokens = slice(P * j, P * (j + 1))
            nc.gpsimd.tensor_scalar(
                out=a_woven[:, tokens, :], in0=a_t[:, :, tokens].rearrange("p t n -> p n t"), scalar1=1.0, scalar2=0.0, op0=MULT, op1=ADD
            )
        turn_late(2, 4, banks[0], banks[3])
        gate_and_add(2, 2, 4, banks[0], banks[3], 2 * P)
        last = keep.tile([P, 2, 2, P], F32, name="last_picks", tag="before_last_picks")
        for c in (2, 3):
            pick_plain(c, 4, BLOCKS, last[:, c - 2])
        sort_gated(0, 4, BLOCKS, banks[4][:, 0:P])
        sort_gated(1, 3, BLOCKS, banks[4][:, P : 3 * P])
        back = [banks[6], banks[5], banks[2], banks[3], banks[4]]
        for g, (j0, j1) in enumerate(TOKEN_GROUPS):
            if g == 2:
                turn_late(j0, j1, banks[1], banks[7])
                gate_and_add(2, j0, j1, banks[1], banks[7], 2 * P)
            for j in range(j0, j1):
                turn_back(j, back[j])
                make_da(j, back[j])
            quantize(g)
        finish(0, back[0:2], [nc.scalar.copy] * 2)
        finish(1, back[2:4], [nc.scalar.copy] * 2)
        finish(2, [banks[0], banks[7]], [nc.vector.tensor_copy, nc.scalar.copy])
